import numpy as np
import ml_dtypes


def mxq(x, axis, fmt="e4m3"):
    dtype, down = {"e4m3": (ml_dtypes.float8_e4m3fn, 7), "e5m2": (ml_dtypes.float8_e5m2, 14)}[fmt]
    v = np.moveaxis(np.asarray(x, np.float32).astype(ml_dtypes.bfloat16).astype(np.float64), axis, -1)
    blocks = v.reshape(v.shape[:-1] + (-1, 32))
    amax = np.abs(blocks).max(-1, keepdims=True)
    byte = np.maximum(np.where(amax > 0, np.frexp(amax)[1] - 1 + 127, 0) - down, 1)
    scale = np.exp2(byte - 127.0)
    codes = (blocks / scale).astype(np.float32).astype(dtype).astype(np.float64)
    return np.moveaxis((codes * scale).reshape(v.shape), -1, axis)


WIDE = False


def mx_kscale(k):
    if not WIDE:
        return np.ones(k)
    levels = np.array([10, -10, 5, -5, 0])
    if k % 512:
        return np.exp2(np.random.permutation(np.resize(levels, k // 32))).repeat(32)
    a = np.empty((k // 512, 16))
    for p in range(k // 512):
        a[p, :8] = np.random.permutation(np.resize(levels, 8))
        for g in range(8):
            far = levels[np.abs(levels - a[p, g]) >= 10]
            a[p, g + 8] = far[np.random.randint(len(far))]
    return np.exp2(a.ravel()).repeat(32)


def f64(x):
    return np.asarray(x).astype(np.float64)


def striped(idx):
    return np.tile(idx.reshape(-1, 16).T, (8, 1)).astype(np.uint16)


def unstriped(offs):
    return offs[:16].T.reshape(-1).astype(np.int64)


E2M1 = np.array([0.0, 0.5, 1.0, 1.5, 2.0, 3.0, 4.0, 6.0, -0.0, -0.5, -1.0, -1.5, -2.0, -3.0, -4.0, -6.0])


def pack_weight(w, fmt):
    k, n = w.shape
    w = f64(np.asarray(w, np.float32).astype(ml_dtypes.bfloat16)).reshape(k // 32, 32, n)
    amax = np.abs(w).max(1)
    if fmt == "e4m3":
        byte = np.frexp(amax)[1] - 1 + 127 - 7
    else:
        mant, ex = np.frexp(amax / 6.0)
        byte = np.where(mant > 0.5, ex, ex - 1) + 127
    byte = np.clip(np.where(amax > 0, byte, 1), 1, 254)
    scaled = (w * np.exp2(127.0 - byte)[:, None, :]).reshape(k, n).astype(np.float32)
    by_word = np.ascontiguousarray(scaled.reshape(k // 512, 128, 4, n).transpose(0, 1, 3, 2))
    if fmt == "e4m3":
        words = by_word.astype(ml_dtypes.float8_e4m3fn).view(np.uint8)
    else:
        c = by_word.astype(ml_dtypes.float4_e2m1fn).view(np.uint8) & 0xF
        words = (c[..., 0::2] | (c[..., 1::2] << 4)).reshape(k // 512, 128, 2 * n)
    return np.ascontiguousarray(words), np.ascontiguousarray(byte.astype(np.uint8).reshape(k // 512, 16, n))


def unpack_weight(words, scales, fmt):
    g, _, n = scales.shape
    words = np.ascontiguousarray(words).reshape(g, 128, n, -1)
    if fmt == "e4m3":
        vals = words.view(ml_dtypes.float8_e4m3fn).astype(np.float64)
    else:
        nib = np.empty((g, 128, n, 4), np.uint8)
        nib[..., 0::2] = words & 0xF
        nib[..., 1::2] = words >> 4
        vals = E2M1[nib]
    vals = vals * np.repeat(np.exp2(scales.astype(np.float64) - 127.0), 8, axis=1)[..., None]
    return vals.transpose(0, 1, 3, 2).reshape(g * 512, n)


def gelu(v):
    return 0.5 * v * (1.0 + np.tanh(np.sqrt(2.0 / np.pi) * (v + 0.044715 * v**3)))


K, H, N, T, S, T2, P = 1024, 1024, 512, 2048, 1024, 2048, 128

def setup_inputs():
    n = np.random.standard_normal
    s = mx_kscale(K)[:, None]
    u = mx_kscale(H)[:, None]
    tab_words, tab_scales = pack_weight(n((K, T)) * s, "e4m3")
    w1 = n((K, H)) / np.sqrt(K) / s * u.T
    w2_words, w2_scales = pack_weight(2.0 * n((H, N)) / np.sqrt(H) / u, "e2m1")
    return {
        "tab_words": tab_words, "tab_scales": tab_scales,
        "offs": striped(np.random.permutation(T)[:S]),
        "w1": w1.astype(np.float32),
        "wgs": np.exp(0.3 * n((P, S))).astype(np.float32),
        "offs2": striped(np.random.permutation(T2)[:S]),
        "old": (n((H, T2)) * u).astype(np.float32),
        "w2_words": w2_words, "w2_scales": w2_scales,
    }

def reference(tab_words, tab_scales, offs, w1, wgs, offs2, old, w2_words, w2_scales):
    v = unpack_weight(tab_words, tab_scales, "e4m3")[:, unstriped(offs)]
    w1q = mxq(f64(w1), 0, "e4m3")
    h = np.maximum(w1q.T @ v, 0.0)
    page = np.zeros((H, T2))
    page[:, unstriped(offs2)] = np.tile(f64(wgs), (H // P, 1)) * h
    z = 0.5 * (page + f64(old))
    zq = mxq(z, 0, "e4m3")
    w2 = unpack_weight(w2_words, w2_scales, "e2m1")
    y = w2.T @ zq
    return np.log(1.0 + np.abs(y))

@@ -1,0 +1,322 @@
+from contextlib import ExitStack
+
+import concourse.mybir as mybir
+from concourse.masks import make_identity
+
+K, H, N, T, S, T2, P = 1024, 1024, 512, 2048, 1024, 2048, 128
+FLOPS = 2 * K * H * S + 2 * H * N * T2
+
+F32 = mybir.dt.float32
+BF16 = mybir.dt.bfloat16
+I32 = mybir.dt.int32
+U32 = mybir.dt.uint32
+U16 = mybir.dt.uint16
+U8 = mybir.dt.uint8
+FP8X4 = mybir.dt.float8_e4m3fn_x4
+FP4X4 = mybir.dt.float4_e2m1fn_x4
+ACT = mybir.ActivationFunctionType
+ALU = mybir.AluOpType
+
+BANK = 512
+PASSES = 2
+SLICES = H // P
+CHUNKS = T2 // BANK
+N_TILES = N // P
+PAGES = 3
+H_BUFS = 6
+STREAM_BUFS = 5
+VECTOR_ABS = 7
+
+
+def tile_list_early_exit_refill_kernel(
+    tc, tab_words, tab_scales, offs, w1, wgs, offs2, old, w2_words, w2_scales, out
+):
+    nc = tc.nc
+    with ExitStack() as ctx:
+        keep = ctx.enter_context(tc.tile_pool(name="keep", bufs=1))
+        ring = ctx.enter_context(tc.tile_pool(name="ring", bufs=4))
+        stream = ctx.enter_context(tc.tile_pool(name="stream", bufs=STREAM_BUFS))
+        hpool = ctx.enter_context(tc.tile_pool(name="hpool", bufs=H_BUFS))
+        psum = ctx.enter_context(tc.psum_pool(name="psum", bufs=1))
+
+        banks = [psum.tile([P, BANK], F32, name="bank%d" % b)[:] for b in range(8)]
+
+        tab_planes = keep.tile([P, T], U8, name="tab_planes", align_bytes=64)
+        nc.gpsimd.memset(tab_planes[:].bitcast(I32), 0)
+        one = keep.tile([P, 1], F32, name="one")
+        nc.gpsimd.memset(one[:], 1.0)
+        zero = keep.tile([P, 1], F32, name="zero")
+        nc.scalar.activation(out=zero[:], in_=one[:], func=ACT.Ln)
+        w2_planes = keep.tile([P, PASSES, N], U8, name="w2_planes", align_bytes=64)
+        nc.gpsimd.memset(w2_planes[:].rearrange("p a n -> p (a n)").bitcast(I32), 0)
+        pages = [keep.tile([P, T2], F32, name="page%d" % i) for i in range(PAGES)]
+        for page in pages[:2]:
+            nc.vector.memset(page[:].bitcast(I32), 0)
+        nc.gpsimd.memset(pages[2][:], 0.0)
+        ident = keep.tile([P, P], F32, name="ident")
+        make_identity(nc, ident[:])
+
+        offsets = keep.tile([P, S // 16], U16, name="offsets")
+        nc.sync.dma_start(offsets[:], offs)
+        tabs = [keep.tile([P, T], I32, name="tab%d" % a, align_bytes=64) for a in range(PASSES)]
+
+        def load_tab(a):
+            nc.sync.dma_start(out=tabs[a][:], in_=tab_words[a].rearrange("p t i -> p (t i)").bitcast(I32))
+
+        def load_w1(pool, name, a, c0, c1):
+            raw = pool.tile([P, 4, c1 - c0], F32, name=name, tag=name, align_bytes=64)
+            rows = w1[512 * a : 512 * (a + 1), c0:c1]
+            nc.sync.dma_start(out=raw[:], in_=rows.rearrange("(p j) c -> p j c", j=4))
+            return raw
+
+        load_tab(0)
+        for q in range(4):
+            nc.sync.dma_start(
+                out=tab_planes[32 * q : 32 * q + 8, :].bitcast(I32),
+                in_=tab_scales[:, 4 * q : 4 * q + 4, :].bitcast(I32),
+            )
+        w1_raw = {}
+        for a in range(PASSES):
+            w1_raw[0, a] = load_w1(keep, "w1_s0_%d" % a, a, 0, 128)[:]
+        load_tab(1)
+        for a in range(PASSES):
+            w1_raw[1, a] = load_w1(keep, "w1_s1_%d" % a, a, 128, 256)[:]
+        wgs_rows = keep.tile([P, S], F32, name="wgs_rows")
+        nc.sync.dma_start(out=wgs_rows[:, 0:BANK], in_=wgs[:, 0:BANK])
+        offsets2 = keep.tile([P, S // 16], U16, name="offsets2")
+        nc.sync.dma_start(offsets2[:], offs2)
+        for a in range(PASSES):
+            raw = load_w1(ring, "wide", a, 256, 512)
+            w1_raw[2, a] = raw[:, :, 0:128]
+            w1_raw[3, a] = raw[:, :, 128:256]
+        w1_upper = [load_w1(stream, "stream", 0, 512, 1024)]
+        nc.sync.dma_start(out=wgs_rows[:, BANK:S], in_=wgs[:, BANK:S])
+        w1_upper.append(load_w1(stream, "stream", 1, 512, 1024))
+
+        olds = {}
+
+        def load_old(s):
+            tile = stream.tile([P, T2], F32, name="stream", tag="stream", align_bytes=64)
+            if s < 4:
+                rows = old[P * s : P * (s + 1), :]
+            else:
+                rows = old[512:1024, :].rearrange("(p i) t -> p i t", i=4)[:, s - 4, :]
+            nc.sync.dma_start(out=tile[:], in_=rows)
+            olds[s] = tile
+
+        load_old(0)
+        load_old(1)
+        wgs_dealt = keep.tile([P, 4, S], F32, name="wgs_dealt")
+        for g in (0, 2, 1, 3):
+            nc.sync.dma_start(
+                out=wgs_dealt[32 * g : 32 * (g + 1), :, :], in_=wgs.rearrange("(q i) j -> q i j", i=4)
+            )
+        load_old(2)
+        w2_codes = keep.tile([P, PASSES, 2 * N], U8, name="w2_codes", align_bytes=64)
+        nc.sync.dma_start(out=w2_codes[:].bitcast(I32), in_=w2_words.rearrange("a p c -> p a c").bitcast(I32))
+        for q in range(4):
+            nc.sync.dma_start(
+                out=w2_planes[32 * q : 32 * q + 4, :, :].bitcast(I32),
+                in_=w2_scales[:, 4 * q : 4 * q + 4, :].rearrange("a r n -> r a n").bitcast(I32),
+            )
+
+        v_planes = keep.tile([P, S], U8, name="v_planes", align_bytes=64)
+        v_words = [keep.tile([P, S], U32, name="v_words%d" % a, align_bytes=64) for a in range(PASSES)]
+        halves = [(slice(BANK * f, BANK * (f + 1)), slice(32 * f, 32 * (f + 1))) for f in range(2)]
+        for a in range(PASSES):
+            for cols, ocols in halves:
+                if a == 1:
+                    nc.vector.tensor_copy(v_planes[:, cols], tab_planes[:].indirect(offsets[:, ocols]))
+                nc.vector.tensor_copy(v_words[a][:, cols], tabs[a][:].bitcast(U32).indirect(offsets[:, ocols]))
+
+        w1_codes = {}
+        w1_planes = {}
+        for s in range(4):
+            grouped = ring.tile([P, PASSES, P, 4], BF16, name="w1_grouped", align_bytes=64, bufs=2)
+            for a in range(PASSES):
+                nc.scalar.copy(
+                    out=grouped[:, a, :, :].rearrange("p (c i) j -> p c j i", i=4),
+                    in_=w1_raw[s, a].rearrange("p j (c i) -> p c j i", i=4),
+                )
+            codes = keep.tile([P, PASSES, P], U32, name="w1_codes%d" % s, align_bytes=64)
+            planes = keep.tile([P, PASSES, P], U8, name="w1_planes%d" % s, align_bytes=64)
+            nc.vector.quantize_mx(
+                out=codes[:].rearrange("p a c -> p (a c)").bitcast(FP8X4),
+                scales=planes[:].rearrange("p a c -> p (a c)"),
+                in_=grouped[:].rearrange("p a c j -> p (a c j)"),
+            )
+            for a in range(PASSES):
+                w1_codes[s, a] = codes[:, a, :]
+                w1_planes[s, a] = planes[:, a, :]
+        for a in range(PASSES):
+            grouped = ring.tile([P, 4, P, 4], BF16, name="wide", tag="wide", align_bytes=64)
+            nc.scalar.copy(
+                out=grouped[:].rearrange("p i m j -> p m i j"),
+                in_=w1_upper[a][:].rearrange("p j (m i) -> p m i j", i=4),
+            )
+            codes = keep.tile([P, 4, P], U32, name="w1_codes_upper%d" % a, align_bytes=64)
+            planes = keep.tile([P, 4, P], U8, name="w1_planes_upper%d" % a, align_bytes=64)
+            nc.vector.quantize_mx(
+                out=codes[:].rearrange("p i m -> p (i m)").bitcast(FP8X4),
+                scales=planes[:].rearrange("p i m -> p (i m)"),
+                in_=grouped[:].rearrange("p i m j -> p (i m j)"),
+            )
+            for i in range(4):
+                w1_codes[4 + i, a] = codes[:, i, :]
+                w1_planes[4 + i, a] = planes[:, i, :]
+
+        hs = {}
+
+        def first_product(s, first_bank, h=None):
+            if h is None:
+                h = hpool.tile([P, S], F32, name="h", tag="h")[:]
+            for f, (cols, ocols) in enumerate(halves):
+                acc = banks[first_bank + f]
+                for a in range(PASSES):
+                    nc.tensor.matmul_mx(
+                        out=acc[:],
+                        lhsT=w1_codes[s, a].bitcast(FP8X4),
+                        lhsT_scale=w1_planes[s, a],
+                        rhs=v_words[a][:, cols].bitcast(FP8X4),
+                        rhs_scale=v_planes[4 * a : P, cols],
+                        start=(a == 0),
+                        stop=(a == PASSES - 1),
+                    )
+                nc.scalar.activation(
+                    out=h[:, cols], in_=acc[:], func=ACT.Relu, bias=zero[:],
+                    scale=0.5 if s == SLICES - 1 else 1.0,
+                )
+            hs[s] = h
+
+        def scatter(s):
+            page = pages[s % PAGES]
+            weights = wgs_rows[:] if s < 4 else wgs_dealt[:, s - 4, :]
+            if s == 0:
+                for cols, ocols in halves:
+                    nc.vector.tensor_tensor(page[:].indirect(offsets2[:, ocols]), hs[s][:, cols], weights[:, cols], ALU.mult)
+            else:
+                nc.vector.tensor_tensor(page[:].indirect(offsets2[:]), hs[s][:], weights, ALU.mult)
+
+        z_turned = [keep.tile([P, 4, 2, P, 2], BF16, name="z_turned%d" % c) for c in range(CHUNKS)]
+
+        def average_turned(s):
+            page = pages[s % PAGES]
+            sums = [banks[2 + c].rearrange("t (b r) -> t b r", b=4) for c in range(CHUNKS)]
+            for src in (olds[s], page):
+                for c in range(CHUNKS):
+                    for b in range(4):
+                        t0 = BANK * c + P * b
+                        nc.tensor.matmul(
+                            out=sums[c][:, b, :], lhsT=src[:, t0 : t0 + P], rhs=ident[:], is_transpose=True,
+                            start=(src is olds[s] and b == 0), stop=(src is page and b == 3),
+                        )
+            for c in range(CHUNKS):
+                if s < 4:
+                    for u in range(2):
+                        nc.scalar.activation(
+                            out=z_turned[c][:, :, u, 32 * s : 32 * (s + 1), :],
+                            in_=sums[c][:].rearrange("t b (q u e) -> t b q u e", u=2, e=2)[:, :, :, u, :],
+                            func=ACT.Copy, scale=0.5,
+                        )
+                else:
+                    u, e = divmod(s - 4, 2)
+                    nc.scalar.activation(out=z_turned[c][:, :, u, :, e], in_=sums[c][:], func=ACT.Copy, scale=0.5)
+
+        def turn_back(c, grouped):
+            src = z_turned[c][:].rearrange("t b u p e -> t (b u p e)").bitcast(F32)
+            dst = grouped[:].rearrange("p t i -> p (t i)").bitcast(F32)
+            for hb in range(2):
+                pairs = banks[6 + hb if c % 2 == 0 else hb].rearrange("p (b u t) -> p b u t", b=2, u=2)
+                for b in range(2):
+                    for u in range(2):
+                        w0 = P * (2 * (2 * hb + b) + u)
+                        nc.tensor.transpose(pairs[:, b, u, :], src[:, w0 : w0 + P], ident[:])
+                nc.scalar.copy(
+                    out=dst[:, BANK * hb : BANK * (hb + 1)].rearrange("p (b t u) -> p b t u", b=2, u=2),
+                    in_=pairs[:].rearrange("p b u t -> p b t u"),
+                )
+
+        z_codes = {}
+        z_planes = {}
+
+        def quantize_z(a, c, grouped):
+            z_codes[a, c] = keep.tile([P, BANK], U32, name="z_codes%d_%d" % (a, c), align_bytes=64)
+            z_planes[a, c] = keep.tile([P, BANK], U8, name="z_planes%d_%d" % (a, c), align_bytes=64)
+            nc.vector.quantize_mx(
+                out=z_codes[a, c][:].bitcast(FP8X4),
+                scales=z_planes[a, c][:],
+                in_=grouped[:].rearrange("p t i -> p (t i)"),
+            )
+
+        def second_product(acc, a, c, n):
+            nc.tensor.matmul_mx(
+                out=acc[:],
+                lhsT=w2_codes[:, a, 2 * P * n : 2 * P * (n + 1)].bitcast(FP4X4),
+                lhsT_scale=w2_planes[:, a, P * n : P * (n + 1)],
+                rhs=z_codes[a, c][:].bitcast(FP8X4),
+                rhs_scale=z_planes[a, c][:],
+                start=(a == 0),
+                stop=(a == PASSES - 1),
+            )
+
+        for s in range(4):
+            first_product(s, 0)
+        z_lower = []
+        for s in range(SLICES):
+            scatter(s)
+            if s + 3 < SLICES:
+                load_old(s + 3)
+            if s < SLICES - 1:
+                average_turned(s)
+            if s == 3:
+                for c in range(CHUNKS):
+                    grouped = ring.tile([P, BANK, 4], BF16, name="wide", tag="wide", align_bytes=64)
+                    turn_back(c, grouped)
+                    quantize_z(0, c, grouped)
+                    z_lower.append(grouped)
+            if s == 0:
+                first_product(4, 2)
+                first_product(5, 4)
+            if s == 4:
+                for late in range(2):
+                    first_product(6 + late, 0, z_lower[late][:].rearrange("p t i -> p (t i)").bitcast(F32))
+            if s == SLICES - 2:
+                z_upper = [keep.tile([P, BANK, 4], BF16, name="z_upper%d" % c, align_bytes=64) for c in range(CHUNKS)]
+                for c in range(CHUNKS):
+                    turn_back(c, z_upper[c])
+
+        last = SLICES - 1
+        accs = {}
+        for idx in range(8):
+            c, n = divmod(idx, N_TILES)
+            accs[c, n] = banks[(idx + 2) % 8]
+            second_product(accs[c, n], 0, c, n)
+        for c in range(CHUNKS):
+            for hb in range(2):
+                t0 = BANK * c + 256 * hb
+                nc.vector.scalar_tensor_tensor(
+                    out=z_upper[c][:, 256 * hb : 256 * (hb + 1), 3],
+                    in0=olds[last][:, t0 : t0 + 256], scalar=0.5, in1=pages[last % PAGES][:, t0 : t0 + 256],
+                    op0=ALU.mult, op1=ALU.add,
+                )
+            quantize_z(1, c, z_upper[c])
+        out_rows = out.rearrange("(n p) t -> p n t", p=P)
+        for c in range(CHUNKS):
+            result = stream.tile([P, N_TILES, BANK], F32, name="stream", tag="stream", align_bytes=64)
+            for n in range(N_TILES):
+                idx = N_TILES * c + n
+                if (c, n) not in accs:
+                    accs[c, n] = banks[(idx + 2) % 8]
+                    second_product(accs[c, n], 0, c, n)
+                second_product(accs[c, n], 1, c, n)
+                magnitude = hpool.tile([P, BANK], F32, name="h", tag="h")
+                if 8 <= idx < 8 + VECTOR_ABS:
+                    signed = hpool.tile([P, BANK], F32, name="h", tag="h")
+                    nc.vector.tensor_copy(out=signed[:], in_=accs[c, n][:])
+                    nc.vector.scalar_tensor_tensor(
+                        out=magnitude[:], in0=signed[:], scalar=-1.0, in1=signed[:], op0=ALU.mult, op1=ALU.max
+                    )
+                else:
+                    nc.scalar.activation(out=magnitude[:], in_=accs[c, n][:], func=ACT.Abs)
+                nc.scalar.activation(out=result[:, n, :], in_=magnitude[:], func=ACT.Ln, bias=one[:])
+                nc.sync.dma_start(out=out_rows[:, n, BANK * c : BANK * (c + 1)], in_=result[:, n, :])

@@ -23,9 +23,11 @@ SLICES = H // P
 CHUNKS = T2 // BANK
 N_TILES = N // P
 PAGES = 3
-H_BUFS = 6
+H_BUFS = 8
 STREAM_BUFS = 5
-VECTOR_ABS = 7
+SCALAR_ABS = 10
+LAG = 1
+EARLY = 2
 
 
 def tile_list_early_exit_refill_kernel(
@@ -50,11 +52,12 @@ def tile_list_early_exit_refill_kernel(
         w2_planes = keep.tile([P, PASSES, N], U8, name="w2_planes", align_bytes=64)
         nc.gpsimd.memset(w2_planes[:].rearrange("p a n -> p (a n)").bitcast(I32), 0)
         pages = [keep.tile([P, T2], F32, name="page%d" % i) for i in range(PAGES)]
-        for page in pages[:2]:
+        for page in pages:
             nc.vector.memset(page[:].bitcast(I32), 0)
-        nc.gpsimd.memset(pages[2][:], 0.0)
         ident = keep.tile([P, P], F32, name="ident")
         make_identity(nc, ident[:])
+        ident_bf16 = keep.tile([P, P], BF16, name="ident_bf16")
+        make_identity(nc, ident_bf16[:])
 
         offsets = keep.tile([P, S // 16], U16, name="offsets")
         nc.sync.dma_start(offsets[:], offs)
@@ -69,29 +72,28 @@ def tile_list_early_exit_refill_kernel(
             nc.sync.dma_start(out=raw[:], in_=rows.rearrange("(p j) c -> p j c", j=4))
             return raw
 
+        offsets2 = keep.tile([P, S // 16], U16, name="offsets2")
+        nc.sync.dma_start(offsets2[:], offs2)
         load_tab(0)
+        w1_raw = {}
+        for a in range(PASSES):
+            w1_raw[0, a] = load_w1(hpool, "h", a, 0, 128)[:]
+        wgs_rows = keep.tile([P, S], F32, name="wgs_rows")
+        nc.sync.dma_start(out=wgs_rows[:, 0:BANK], in_=wgs[:, 0:BANK])
         for q in range(4):
             nc.sync.dma_start(
                 out=tab_planes[32 * q : 32 * q + 8, :].bitcast(I32),
                 in_=tab_scales[:, 4 * q : 4 * q + 4, :].bitcast(I32),
             )
-        w1_raw = {}
-        for a in range(PASSES):
-            w1_raw[0, a] = load_w1(keep, "w1_s0_%d" % a, a, 0, 128)[:]
         load_tab(1)
         for a in range(PASSES):
-            w1_raw[1, a] = load_w1(keep, "w1_s1_%d" % a, a, 128, 256)[:]
-        wgs_rows = keep.tile([P, S], F32, name="wgs_rows")
-        nc.sync.dma_start(out=wgs_rows[:, 0:BANK], in_=wgs[:, 0:BANK])
-        offsets2 = keep.tile([P, S // 16], U16, name="offsets2")
-        nc.sync.dma_start(offsets2[:], offs2)
+            w1_raw[1, a] = load_w1(hpool, "h", a, 128, 256)[:]
         for a in range(PASSES):
             raw = load_w1(ring, "wide", a, 256, 512)
             w1_raw[2, a] = raw[:, :, 0:128]
             w1_raw[3, a] = raw[:, :, 128:256]
-        w1_upper = [load_w1(stream, "stream", 0, 512, 1024)]
         nc.sync.dma_start(out=wgs_rows[:, BANK:S], in_=wgs[:, BANK:S])
-        w1_upper.append(load_w1(stream, "stream", 1, 512, 1024))
+        w1_upper = [load_w1(stream, "stream", a, 512, 1024) for a in range(PASSES)]
 
         olds = {}
 
@@ -123,10 +125,9 @@ def tile_list_early_exit_refill_kernel(
         v_planes = keep.tile([P, S], U8, name="v_planes", align_bytes=64)
         v_words = [keep.tile([P, S], U32, name="v_words%d" % a, align_bytes=64) for a in range(PASSES)]
         halves = [(slice(BANK * f, BANK * (f + 1)), slice(32 * f, 32 * (f + 1))) for f in range(2)]
-        for a in range(PASSES):
-            for cols, ocols in halves:
-                if a == 1:
-                    nc.vector.tensor_copy(v_planes[:, cols], tab_planes[:].indirect(offsets[:, ocols]))
+        for cols, ocols in halves:
+            nc.vector.tensor_copy(v_planes[:, cols], tab_planes[:].indirect(offsets[:, ocols]))
+            for a in range(PASSES):
                 nc.vector.tensor_copy(v_words[a][:, cols], tabs[a][:].bitcast(U32).indirect(offsets[:, ocols]))
 
         w1_codes = {}
@@ -148,28 +149,10 @@ def tile_list_early_exit_refill_kernel(
             for a in range(PASSES):
                 w1_codes[s, a] = codes[:, a, :]
                 w1_planes[s, a] = planes[:, a, :]
-        for a in range(PASSES):
-            grouped = ring.tile([P, 4, P, 4], BF16, name="wide", tag="wide", align_bytes=64)
-            nc.scalar.copy(
-                out=grouped[:].rearrange("p i m j -> p m i j"),
-                in_=w1_upper[a][:].rearrange("p j (m i) -> p m i j", i=4),
-            )
-            codes = keep.tile([P, 4, P], U32, name="w1_codes_upper%d" % a, align_bytes=64)
-            planes = keep.tile([P, 4, P], U8, name="w1_planes_upper%d" % a, align_bytes=64)
-            nc.vector.quantize_mx(
-                out=codes[:].rearrange("p i m -> p (i m)").bitcast(FP8X4),
-                scales=planes[:].rearrange("p i m -> p (i m)"),
-                in_=grouped[:].rearrange("p i m j -> p (i m j)"),
-            )
-            for i in range(4):
-                w1_codes[4 + i, a] = codes[:, i, :]
-                w1_planes[4 + i, a] = planes[:, i, :]
-
         hs = {}
 
-        def first_product(s, first_bank, h=None):
-            if h is None:
-                h = hpool.tile([P, S], F32, name="h", tag="h")[:]
+        def first_product(s, first_bank):
+            h = hpool.tile([P, S], F32, name="h", tag="h", align_bytes=64)[:]
             for f, (cols, ocols) in enumerate(halves):
                 acc = banks[first_bank + f]
                 for a in range(PASSES):
@@ -199,6 +182,9 @@ def tile_list_early_exit_refill_kernel(
 
         z_turned = [keep.tile([P, 4, 2, P, 2], BF16, name="z_turned%d" % c) for c in range(CHUNKS)]
 
+        def single(c):
+            return z_turned[c][:, :, 1, :, :].rearrange("t b p e -> t b (p e)")[:, :, 0:P]
+
         def average_turned(s):
             page = pages[s % PAGES]
             sums = [banks[2 + c].rearrange("t (b r) -> t b r", b=4) for c in range(CHUNKS)]
@@ -218,9 +204,10 @@ def tile_list_early_exit_refill_kernel(
                             in_=sums[c][:].rearrange("t b (q u e) -> t b q u e", u=2, e=2)[:, :, :, u, :],
                             func=ACT.Copy, scale=0.5,
                         )
+                elif s < 6:
+                    nc.scalar.activation(out=z_turned[c][:, :, 0, :, s - 4], in_=sums[c][:], func=ACT.Copy, scale=0.5)
                 else:
-                    u, e = divmod(s - 4, 2)
-                    nc.scalar.activation(out=z_turned[c][:, :, u, :, e], in_=sums[c][:], func=ACT.Copy, scale=0.5)
+                    nc.scalar.activation(out=single(c), in_=sums[c][:], func=ACT.Copy, scale=0.5)
 
         def turn_back(c, grouped):
             src = z_turned[c][:].rearrange("t b u p e -> t (b u p e)").bitcast(F32)
@@ -259,31 +246,76 @@ def tile_list_early_exit_refill_kernel(
                 stop=(a == PASSES - 1),
             )
 
+        upper = keep.tile([P, 5 * CHUNKS + LAG, BANK], BF16, name="upper", align_bytes=64)
+        first_z = CHUNKS + LAG
+        z_upper = [
+            upper[:, first_z + 4 * c : first_z + 4 * (c + 1), :].rearrange("p r t -> p (r t)").rearrange("p (t i) -> p t i", i=4)
+            for c in range(CHUNKS)
+        ]
+        last_row = [CHUNKS + c if c < LAG else first_z + 4 * (c - LAG) for c in range(CHUNKS)]
+
+        def turn_back_pair(c):
+            src = z_turned[c][:].rearrange("t b u p e -> t (b u p e)").bitcast(F32)
+            dst = z_upper[c].rearrange("p t i -> p (t i)").bitcast(F32).rearrange("p (t u) -> p t u", u=2)
+            pairs = banks[(6 + c) % 8]
+            for b in range(4):
+                nc.tensor.transpose(pairs[:, P * b : P * (b + 1)], src[:, 2 * P * b : 2 * P * b + P], ident[:])
+            nc.scalar.copy(out=dst[:, :, 0], in_=pairs)
+
+        def turn_back_single(c):
+            back = banks[(6 + c) % 8].bitcast(BF16)[:, 0:BANK]
+            for b in range(4):
+                nc.tensor.transpose(back[:, P * b : P * (b + 1)], single(c)[:, b, :], ident_bf16[:])
+            nc.scalar.copy(out=upper[:, c, :], in_=back)
+
+        def average_direct(s, c):
+            cols = slice(BANK * c, BANK * (c + 1))
+            nc.vector.scalar_tensor_tensor(
+                out=upper[:, last_row[c] if s == SLICES - 1 else c, :], in0=olds[s][:, cols], scalar=0.5, in1=pages[s % PAGES][:, cols],
+                op0=ALU.mult, op1=ALU.add,
+            )
+
         for s in range(4):
             first_product(s, 0)
-        z_lower = []
+        for a in range(PASSES):
+            grouped = ring.tile([P, 4, P, 4], BF16, name="wide", tag="wide", align_bytes=64)
+            nc.scalar.copy(
+                out=grouped[:].rearrange("p i m j -> p m i j"),
+                in_=w1_upper[a][:].rearrange("p j (m i) -> p m i j", i=4),
+            )
+            codes = keep.tile([P, 4, P], U32, name="w1_codes_upper%d" % a, align_bytes=64)
+            planes = keep.tile([P, 4, P], U8, name="w1_planes_upper%d" % a, align_bytes=64)
+            nc.vector.quantize_mx(
+                out=codes[:].rearrange("p i m -> p (i m)").bitcast(FP8X4),
+                scales=planes[:].rearrange("p i m -> p (i m)"),
+                in_=grouped[:].rearrange("p i m j -> p (i m j)"),
+            )
+            for i in range(4):
+                w1_codes[4 + i, a] = codes[:, i, :]
+                w1_planes[4 + i, a] = planes[:, i, :]
+
         for s in range(SLICES):
             scatter(s)
             if s + 3 < SLICES:
                 load_old(s + 3)
             if s < SLICES - 1:
                 average_turned(s)
+            if s < 2:
+                first_product(2 * s + 4, 2)
+                first_product(2 * s + 5, 4)
             if s == 3:
                 for c in range(CHUNKS):
                     grouped = ring.tile([P, BANK, 4], BF16, name="wide", tag="wide", align_bytes=64)
                     turn_back(c, grouped)
                     quantize_z(0, c, grouped)
-                    z_lower.append(grouped)
-            if s == 0:
-                first_product(4, 2)
-                first_product(5, 4)
-            if s == 4:
-                for late in range(2):
-                    first_product(6 + late, 0, z_lower[late][:].rearrange("p t i -> p (t i)").bitcast(F32))
+            if s == SLICES - 3:
+                for c in range(EARLY):
+                    turn_back_pair(c)
             if s == SLICES - 2:
-                z_upper = [keep.tile([P, BANK, 4], BF16, name="z_upper%d" % c, align_bytes=64) for c in range(CHUNKS)]
                 for c in range(CHUNKS):
-                    turn_back(c, z_upper[c])
+                    if c >= EARLY:
+                        turn_back_pair(c)
+                    turn_back_single(c)
 
         last = SLICES - 1
         accs = {}
@@ -292,13 +324,9 @@ def tile_list_early_exit_refill_kernel(
             accs[c, n] = banks[(idx + 2) % 8]
             second_product(accs[c, n], 0, c, n)
         for c in range(CHUNKS):
-            for hb in range(2):
-                t0 = BANK * c + 256 * hb
-                nc.vector.scalar_tensor_tensor(
-                    out=z_upper[c][:, 256 * hb : 256 * (hb + 1), 3],
-                    in0=olds[last][:, t0 : t0 + 256], scalar=0.5, in1=pages[last % PAGES][:, t0 : t0 + 256],
-                    op0=ALU.mult, op1=ALU.add,
-                )
+            average_direct(last, c)
+            both = upper[:, c : last_row[c] + 1 : last_row[c] - c, :]
+            nc.vector.tensor_copy(out=z_upper[c][:, :, 2:4], in_=both.rearrange("p e t -> p t e"))
             quantize_z(1, c, z_upper[c])
         out_rows = out.rearrange("(n p) t -> p n t", p=P)
         for c in range(CHUNKS):
@@ -309,9 +337,9 @@ def tile_list_early_exit_refill_kernel(
                     accs[c, n] = banks[(idx + 2) % 8]
                     second_product(accs[c, n], 0, c, n)
                 second_product(accs[c, n], 1, c, n)
-                magnitude = hpool.tile([P, BANK], F32, name="h", tag="h")
-                if 8 <= idx < 8 + VECTOR_ABS:
-                    signed = hpool.tile([P, BANK], F32, name="h", tag="h")
+                magnitude = hpool.tile([P, BANK], F32, name="h", tag="h", align_bytes=64)
+                if idx >= SCALAR_ABS:
+                    signed = hpool.tile([P, BANK], F32, name="h", tag="h", align_bytes=64)
                     nc.vector.tensor_copy(out=signed[:], in_=accs[c, n][:])
                     nc.vector.scalar_tensor_tensor(
                         out=magnitude[:], in0=signed[:], scalar=-1.0, in1=signed[:], op0=ALU.mult, op1=ALU.max

@@ -23,11 +23,9 @@ SLICES = H // P
 CHUNKS = T2 // BANK
 N_TILES = N // P
 PAGES = 3
-H_BUFS = 8
 STREAM_BUFS = 5
-SCALAR_ABS = 10
-LAG = 1
-EARLY = 2
+VECTOR_ABS = (9, 11, 13, 14, 15)
+EARLY_CHUNKS = 1
 
 
 def tile_list_early_exit_refill_kernel(
@@ -36,12 +34,22 @@ def tile_list_early_exit_refill_kernel(
     nc = tc.nc
     with ExitStack() as ctx:
         keep = ctx.enter_context(tc.tile_pool(name="keep", bufs=1))
-        ring = ctx.enter_context(tc.tile_pool(name="ring", bufs=4))
+        ring = ctx.enter_context(tc.tile_pool(name="ring", bufs=2))
         stream = ctx.enter_context(tc.tile_pool(name="stream", bufs=STREAM_BUFS))
-        hpool = ctx.enter_context(tc.tile_pool(name="hpool", bufs=H_BUFS))
         psum = ctx.enter_context(tc.psum_pool(name="psum", bufs=1))
 
         banks = [psum.tile([P, BANK], F32, name="bank%d" % b)[:] for b in range(8)]
+        taken = []
+
+        def next_bank():
+            taken.append(banks[len(taken) % len(banks)])
+            return taken[-1]
+
+        def slot(index, shape, dtype):
+            return keep.tile(shape, dtype, name="slot%d" % index, tag="slot%d" % index, align_bytes=64)
+
+        def big(index, shape, dtype):
+            return keep.tile(shape, dtype, name="big%d" % index, tag="big%d" % index, align_bytes=64)
 
         tab_planes = keep.tile([P, T], U8, name="tab_planes", align_bytes=64)
         nc.gpsimd.memset(tab_planes[:].bitcast(I32), 0)
@@ -49,71 +57,89 @@ def tile_list_early_exit_refill_kernel(
         nc.gpsimd.memset(one[:], 1.0)
         zero = keep.tile([P, 1], F32, name="zero")
         nc.scalar.activation(out=zero[:], in_=one[:], func=ACT.Ln)
-        w2_planes = keep.tile([P, PASSES, N], U8, name="w2_planes", align_bytes=64)
-        nc.gpsimd.memset(w2_planes[:].rearrange("p a n -> p (a n)").bitcast(I32), 0)
-        pages = [keep.tile([P, T2], F32, name="page%d" % i) for i in range(PAGES)]
-        for page in pages:
-            nc.vector.memset(page[:].bitcast(I32), 0)
         ident = keep.tile([P, P], F32, name="ident")
         make_identity(nc, ident[:])
         ident_bf16 = keep.tile([P, P], BF16, name="ident_bf16")
-        make_identity(nc, ident_bf16[:])
+        nc.scalar.copy(out=ident_bf16[:], in_=ident[:])
+        w2_planes = keep.tile([P, PASSES, N], U8, name="w2_planes", align_bytes=64)
+        pages = [keep.tile([P, T2], F32, name="page0")]
+        nc.vector.memset(pages[0][:].bitcast(I32), 0)
 
         offsets = keep.tile([P, S // 16], U16, name="offsets")
         nc.sync.dma_start(offsets[:], offs)
-        tabs = [keep.tile([P, T], I32, name="tab%d" % a, align_bytes=64) for a in range(PASSES)]
+        tabs = [big(a, [P, T], I32) for a in range(PASSES)]
 
         def load_tab(a):
             nc.sync.dma_start(out=tabs[a][:], in_=tab_words[a].rearrange("p t i -> p (t i)").bitcast(I32))
 
-        def load_w1(pool, name, a, c0, c1):
-            raw = pool.tile([P, 4, c1 - c0], F32, name=name, tag=name, align_bytes=64)
-            rows = w1[512 * a : 512 * (a + 1), c0:c1]
-            nc.sync.dma_start(out=raw[:], in_=rows.rearrange("(p j) c -> p j c", j=4))
-            return raw
-
-        offsets2 = keep.tile([P, S // 16], U16, name="offsets2")
-        nc.sync.dma_start(offsets2[:], offs2)
-        load_tab(0)
         w1_raw = {}
-        for a in range(PASSES):
-            w1_raw[0, a] = load_w1(hpool, "h", a, 0, 128)[:]
-        wgs_rows = keep.tile([P, S], F32, name="wgs_rows")
-        nc.sync.dma_start(out=wgs_rows[:, 0:BANK], in_=wgs[:, 0:BANK])
-        for q in range(4):
-            nc.sync.dma_start(
-                out=tab_planes[32 * q : 32 * q + 8, :].bitcast(I32),
-                in_=tab_scales[:, 4 * q : 4 * q + 4, :].bitcast(I32),
-            )
-        load_tab(1)
-        for a in range(PASSES):
-            w1_raw[1, a] = load_w1(hpool, "h", a, 128, 256)[:]
-        for a in range(PASSES):
-            raw = load_w1(ring, "wide", a, 256, 512)
-            w1_raw[2, a] = raw[:, :, 0:128]
-            w1_raw[3, a] = raw[:, :, 128:256]
-        nc.sync.dma_start(out=wgs_rows[:, BANK:S], in_=wgs[:, BANK:S])
-        w1_upper = [load_w1(stream, "stream", a, 512, 1024) for a in range(PASSES)]
+
+        def load_w1_lower(s, index):
+            raw = slot(index, [P, PASSES, 4, P], F32)
+            for a in range(PASSES):
+                rows = w1[512 * a : 512 * (a + 1), P * s : P * (s + 1)]
+                nc.sync.dma_start(out=raw[:, a, :, :], in_=rows.rearrange("(p j) c -> p j c", j=4))
+            w1_raw[s] = raw
+
+        def load_w1_upper(half, indices):
+            for a in range(PASSES):
+                raw = slot(indices[a], [P, 4, 2 * P], F32)
+                rows = w1[512 * a : 512 * (a + 1), 512 + 2 * P * half : 512 + 2 * P * (half + 1)]
+                nc.sync.dma_start(out=raw[:], in_=rows.rearrange("(p j) c -> p j c", j=4))
+                w1_raw[4 + half, a] = raw
 
         olds = {}
 
         def load_old(s):
             tile = stream.tile([P, T2], F32, name="stream", tag="stream", align_bytes=64)
+            lanes = old[512:1024, :].rearrange("(p i) t -> p i t", i=4)
             if s < 4:
-                rows = old[P * s : P * (s + 1), :]
+                nc.sync.dma_start(out=tile[:], in_=old[P * s : P * (s + 1), :])
+            elif s < 6:
+                for e in range(2):
+                    nc.sync.dma_start(out=tile[e:P:2, :], in_=lanes[64 * (s - 4) : 64 * (s - 3), e, :])
             else:
-                rows = old[512:1024, :].rearrange("(p i) t -> p i t", i=4)[:, s - 4, :]
-            nc.sync.dma_start(out=tile[:], in_=rows)
+                nc.sync.dma_start(out=tile[:], in_=lanes[:, s - 4, :])
             olds[s] = tile
 
+        old_last = []
+
+        def load_old_last():
+            lane = old[512:1024, :].rearrange("(p i) t -> p i t", i=4)[:, 3, :]
+            for c in range(CHUNKS):
+                old_last.append(keep.tile([P, BANK], F32, name="old_last", tag="old_last%d" % c, align_bytes=64))
+                nc.sync.dma_start(out=old_last[c][:], in_=lane[:, BANK * c : BANK * (c + 1)])
+
+        scale_rows = keep.tile([P, T // 4], I32, name="scale_rows")
+        for q in range(4):
+            queue = nc.sync if q < 2 else nc.scalar
+            queue.dma_start(out=scale_rows[32 * q : 32 * q + 8, :], in_=tab_scales[:, 4 * q : 4 * q + 4, :].bitcast(I32))
+        for q in range(4):
+            nc.vector.tensor_copy(tab_planes[32 * q : 32 * q + 8, :].bitcast(I32), scale_rows[32 * q : 32 * q + 8, :])
+        nc.vector.memset(w2_planes[:].rearrange("p a n -> p (a n)").bitcast(I32), 0)
+        load_tab(0)
+        load_w1_lower(0, 6)
+        load_tab(1)
+        offsets2 = keep.tile([P, S // 16], U16, name="offsets2")
+        nc.sync.dma_start(offsets2[:], offs2)
+        wgs_rows = keep.tile([P, S], F32, name="wgs_rows")
+        nc.sync.dma_start(out=wgs_rows[:], in_=wgs)
+        load_w1_lower(1, 0)
+        load_w1_lower(2, 1)
         load_old(0)
+        load_w1_lower(3, 2)
+        load_w1_upper(0, (7, 6))
         load_old(1)
-        wgs_dealt = keep.tile([P, 4, S], F32, name="wgs_dealt")
-        for g in (0, 2, 1, 3):
-            nc.sync.dma_start(
-                out=wgs_dealt[32 * g : 32 * (g + 1), :, :], in_=wgs.rearrange("(q i) j -> q i j", i=4)
-            )
+        load_w1_upper(1, (5, 3))
         load_old(2)
+        wgs_by_lane = wgs.rearrange("(q i) j -> q i j", i=4)
+        wgs_pair = keep.tile([P, S], F32, name="wgs_pair")
+        for e in range(2):
+            for g in range(2):
+                nc.sync.dma_start(out=wgs_pair[64 * g + e : 64 * (g + 1) : 2, :], in_=wgs_by_lane[:, e, :])
+        wgs_lanes = keep.tile([P, 2, S], F32, name="wgs_lanes")
+        for g in (0, 2, 1, 3):
+            nc.sync.dma_start(out=wgs_lanes[32 * g : 32 * (g + 1), :, :], in_=wgs_by_lane[:, 2:4, :])
         w2_codes = keep.tile([P, PASSES, 2 * N], U8, name="w2_codes", align_bytes=64)
         nc.sync.dma_start(out=w2_codes[:].bitcast(I32), in_=w2_words.rearrange("a p c -> p a c").bitcast(I32))
         for q in range(4):
@@ -124,96 +150,136 @@ def tile_list_early_exit_refill_kernel(
 
         v_planes = keep.tile([P, S], U8, name="v_planes", align_bytes=64)
         v_words = [keep.tile([P, S], U32, name="v_words%d" % a, align_bytes=64) for a in range(PASSES)]
-        halves = [(slice(BANK * f, BANK * (f + 1)), slice(32 * f, 32 * (f + 1))) for f in range(2)]
-        for cols, ocols in halves:
-            nc.vector.tensor_copy(v_planes[:, cols], tab_planes[:].indirect(offsets[:, ocols]))
-            for a in range(PASSES):
-                nc.vector.tensor_copy(v_words[a][:, cols], tabs[a][:].bitcast(U32).indirect(offsets[:, ocols]))
+        halves = [(0, BANK), (BANK, S)]
+        first_pieces = [(0, BANK // 2), (BANK // 2, BANK), (BANK, S)]
+        nc.vector.tensor_copy(v_planes[:], tab_planes[:].indirect(offsets[:]))
+        nc.vector.tensor_copy(v_words[0][:], tabs[0][:].bitcast(U32).indirect(offsets[:]))
 
         w1_codes = {}
         w1_planes = {}
-        for s in range(4):
-            grouped = ring.tile([P, PASSES, P, 4], BF16, name="w1_grouped", align_bytes=64, bufs=2)
+
+        def quantize_w1(first, grouped):
+            count = grouped.shape[1]
+            codes = keep.tile([P, count, PASSES, P], U32, name="w1_codes%d" % first, align_bytes=64)
+            planes = keep.tile([P, count, PASSES, P], U8, name="w1_planes%d" % first, align_bytes=64)
+            nc.vector.quantize_mx(
+                out=codes[:].rearrange("p i a c -> p (i a c)").bitcast(FP8X4),
+                scales=planes[:].rearrange("p i a c -> p (i a c)"),
+                in_=grouped.rearrange("p i a c j -> p (i a c j)"),
+            )
+            for i in range(count):
+                for a in range(PASSES):
+                    w1_codes[first + i, a] = codes[:, i, a, :]
+                    w1_planes[first + i, a] = planes[:, i, a, :]
+
+        def prepare_w1_lower(s):
+            if s == 2:
+                grouped = big(3, [P, 1, PASSES, P, 4], BF16)
+            else:
+                grouped = ring.tile([P, 1, PASSES, P, 4], BF16, name="w1_grouped", tag="w1_grouped", align_bytes=64)
             for a in range(PASSES):
                 nc.scalar.copy(
-                    out=grouped[:, a, :, :].rearrange("p (c i) j -> p c j i", i=4),
-                    in_=w1_raw[s, a].rearrange("p j (c i) -> p c j i", i=4),
+                    out=grouped[:, 0, a, :, :].rearrange("p (c i) j -> p c j i", i=4),
+                    in_=w1_raw[s][:, a, :, :].rearrange("p j (c i) -> p c j i", i=4),
                 )
-            codes = keep.tile([P, PASSES, P], U32, name="w1_codes%d" % s, align_bytes=64)
-            planes = keep.tile([P, PASSES, P], U8, name="w1_planes%d" % s, align_bytes=64)
-            nc.vector.quantize_mx(
-                out=codes[:].rearrange("p a c -> p (a c)").bitcast(FP8X4),
-                scales=planes[:].rearrange("p a c -> p (a c)"),
-                in_=grouped[:].rearrange("p a c j -> p (a c j)"),
-            )
-            for a in range(PASSES):
-                w1_codes[s, a] = codes[:, a, :]
-                w1_planes[s, a] = planes[:, a, :]
-        hs = {}
+            quantize_w1(s, grouped[:])
 
-        def first_product(s, first_bank):
-            h = hpool.tile([P, S], F32, name="h", tag="h", align_bytes=64)[:]
-            for f, (cols, ocols) in enumerate(halves):
-                acc = banks[first_bank + f]
-                for a in range(PASSES):
-                    nc.tensor.matmul_mx(
-                        out=acc[:],
-                        lhsT=w1_codes[s, a].bitcast(FP8X4),
-                        lhsT_scale=w1_planes[s, a],
-                        rhs=v_words[a][:, cols].bitcast(FP8X4),
-                        rhs_scale=v_planes[4 * a : P, cols],
-                        start=(a == 0),
-                        stop=(a == PASSES - 1),
-                    )
-                nc.scalar.activation(
-                    out=h[:, cols], in_=acc[:], func=ACT.Relu, bias=zero[:],
-                    scale=0.5 if s == SLICES - 1 else 1.0,
+        lanes_grouped = keep.tile([P, 2, PASSES, P, 4], BF16, name="lanes_grouped", align_bytes=64)
+
+        def prepare_w1_upper(half):
+            grouped = ring.tile([P, 1, PASSES, P, 4], BF16, name="w1_grouped", tag="w1_grouped", align_bytes=64)
+            for a in range(PASSES):
+                raw = w1_raw[4 + half, a][:].rearrange("p j (m i) -> p m j i", i=4)
+                nc.scalar.copy(out=grouped[:, 0, a, :, :].rearrange("p (m e) j -> p m j e", e=2), in_=raw[:, :, :, 0:2])
+                nc.scalar.copy(
+                    out=lanes_grouped[:, :, a, 64 * half : 64 * (half + 1), :].rearrange("p i m j -> p m j i"),
+                    in_=raw[:, :, :, 2:4],
                 )
-            hs[s] = h
+            quantize_w1(4 + half, grouped[:])
+
+        hs = {}
+        h_first = keep.tile([P, BANK], F32, name="h_first")
+
+        def first_product(s, piece):
+            cols = slice(*piece)
+            if s == 0 and piece[0] < BANK:
+                h = h_first[:, cols]
+            else:
+                if s not in hs:
+                    hs[s] = slot(s, [P, S], F32)[:]
+                h = hs[s][:, cols]
+            hs[s, piece] = h
+            acc = next_bank()[:, 0 : piece[1] - piece[0]]
+            for a in range(PASSES):
+                nc.tensor.matmul_mx(
+                    out=acc,
+                    lhsT=w1_codes[s, a].bitcast(FP8X4),
+                    lhsT_scale=w1_planes[s, a],
+                    rhs=v_words[a][:, cols].bitcast(FP8X4),
+                    rhs_scale=v_planes[4 * a : P, cols],
+                    start=(a == 0),
+                    stop=(a == PASSES - 1),
+                )
+            nc.scalar.activation(out=h, in_=acc, func=ACT.Relu, bias=zero[:])
 
         def scatter(s):
             page = pages[s % PAGES]
-            weights = wgs_rows[:] if s < 4 else wgs_dealt[:, s - 4, :]
+            weights = wgs_rows[:] if s < 4 else wgs_pair[:] if s < 6 else wgs_lanes[:, s - 6, :]
             if s == 0:
-                for cols, ocols in halves:
-                    nc.vector.tensor_tensor(page[:].indirect(offsets2[:, ocols]), hs[s][:, cols], weights[:, cols], ALU.mult)
+                for j0, j1 in first_pieces:
+                    places = page[:].indirect(offsets2[:, j0 // 16 : j1 // 16])
+                    nc.vector.tensor_tensor(places, hs[s, (j0, j1)], weights[:, j0:j1], ALU.mult)
             else:
                 nc.vector.tensor_tensor(page[:].indirect(offsets2[:]), hs[s][:], weights, ALU.mult)
 
-        z_turned = [keep.tile([P, 4, 2, P, 2], BF16, name="z_turned%d" % c) for c in range(CHUNKS)]
+        z_turned = [
+            keep.tile([P, 4, 2, P, 2], BF16, name="z_turned%d" % c, align_bytes=64)
+            for c in range(CHUNKS)
+        ]
+
+        rows = keep.tile([P, 2 * CHUNKS * BANK], BF16, name="rows", align_bytes=64)[:].rearrange("p (r b t) -> p r b t", b=4, t=P)
+        lane2_row = [CHUNKS - 1 - c for c in range(CHUNKS)]
+        turned_row = [CHUNKS + c for c in range(CHUNKS)]
+        lane3_row = [turned_row[-1], turned_row[-1], lane2_row[0], lane2_row[1]]
 
         def single(c):
-            return z_turned[c][:, :, 1, :, :].rearrange("t b p e -> t b (p e)")[:, :, 0:P]
+            return rows[:, turned_row[c]]
 
-        def average_turned(s):
-            page = pages[s % PAGES]
-            sums = [banks[2 + c].rearrange("t (b r) -> t b r", b=4) for c in range(CHUNKS)]
-            for src in (olds[s], page):
-                for c in range(CHUNKS):
-                    for b in range(4):
-                        t0 = BANK * c + P * b
-                        nc.tensor.matmul(
-                            out=sums[c][:, b, :], lhsT=src[:, t0 : t0 + P], rhs=ident[:], is_transpose=True,
-                            start=(src is olds[s] and b == 0), stop=(src is page and b == 3),
-                        )
+        sum_banks = {}
+
+        def add_turned(s, src, first):
+            if first:
+                sum_banks[s] = [next_bank() for c in range(CHUNKS)]
+            for c in range(CHUNKS):
+                for b in range(4):
+                    t0 = BANK * c + P * b
+                    nc.tensor.matmul(
+                        out=sum_banks[s][c][:, P * b : P * (b + 1)], lhsT=src[:, t0 : t0 + P], rhs=ident[:],
+                        is_transpose=True, start=(first and b == 0), stop=(not first and b == 3),
+                    )
+
+        def sum_turned(s):
+            add_turned(s, pages[s % PAGES], False)
+            sums = [bank.rearrange("t (b r) -> t b r", b=4) for bank in sum_banks[s]]
             for c in range(CHUNKS):
                 if s < 4:
-                    for u in range(2):
-                        nc.scalar.activation(
-                            out=z_turned[c][:, :, u, 32 * s : 32 * (s + 1), :],
-                            in_=sums[c][:].rearrange("t b (q u e) -> t b q u e", u=2, e=2)[:, :, :, u, :],
-                            func=ACT.Copy, scale=0.5,
-                        )
+                    nc.scalar.copy(
+                        out=z_turned[c][:, :, :, 32 * s : 32 * (s + 1), :],
+                        in_=sums[c].rearrange("t b (q u e) -> t b u q e", u=2, e=2),
+                    )
                 elif s < 6:
-                    nc.scalar.activation(out=z_turned[c][:, :, 0, :, s - 4], in_=sums[c][:], func=ACT.Copy, scale=0.5)
+                    nc.scalar.copy(
+                        out=z_turned[c][:, :, 0, 64 * (s - 4) : 64 * (s - 3), :].rearrange("t b m e -> t b (m e)"),
+                        in_=sums[c],
+                    )
                 else:
-                    nc.scalar.activation(out=single(c), in_=sums[c][:], func=ACT.Copy, scale=0.5)
+                    nc.scalar.copy(out=single(c), in_=sums[c])
 
         def turn_back(c, grouped):
             src = z_turned[c][:].rearrange("t b u p e -> t (b u p e)").bitcast(F32)
-            dst = grouped[:].rearrange("p t i -> p (t i)").bitcast(F32)
+            dst = grouped.rearrange("p t i -> p (t i)").bitcast(F32)
             for hb in range(2):
-                pairs = banks[6 + hb if c % 2 == 0 else hb].rearrange("p (b u t) -> p b u t", b=2, u=2)
+                pairs = next_bank().rearrange("p (b u t) -> p b u t", b=2, u=2)
                 for b in range(2):
                     for u in range(2):
                         w0 = P * (2 * (2 * hb + b) + u)
@@ -226,125 +292,154 @@ def tile_list_early_exit_refill_kernel(
         z_codes = {}
         z_planes = {}
 
-        def quantize_z(a, c, grouped):
-            z_codes[a, c] = keep.tile([P, BANK], U32, name="z_codes%d_%d" % (a, c), align_bytes=64)
-            z_planes[a, c] = keep.tile([P, BANK], U8, name="z_planes%d_%d" % (a, c), align_bytes=64)
+        def quantize_z(a, c, grouped, cols):
             nc.vector.quantize_mx(
-                out=z_codes[a, c][:].bitcast(FP8X4),
-                scales=z_planes[a, c][:],
-                in_=grouped[:].rearrange("p t i -> p (t i)"),
+                out=z_codes[a, c][:, cols].bitcast(FP8X4),
+                scales=z_planes[a, c][:, cols],
+                in_=grouped[:, cols, :].rearrange("p t i -> p (t i)"),
             )
 
-        def second_product(acc, a, c, n):
-            nc.tensor.matmul_mx(
-                out=acc[:],
-                lhsT=w2_codes[:, a, 2 * P * n : 2 * P * (n + 1)].bitcast(FP4X4),
-                lhsT_scale=w2_planes[:, a, P * n : P * (n + 1)],
-                rhs=z_codes[a, c][:].bitcast(FP8X4),
-                rhs_scale=z_planes[a, c][:],
-                start=(a == 0),
-                stop=(a == PASSES - 1),
-            )
+        def z_tiles(a, c, tag):
+            z_codes[a, c] = keep.tile([P, BANK], U32, name="z_codes", tag=tag, align_bytes=64)
+            z_planes[a, c] = keep.tile([P, BANK], U8, name="z_planes%d_%d" % (a, c), align_bytes=64)
 
-        upper = keep.tile([P, 5 * CHUNKS + LAG, BANK], BF16, name="upper", align_bytes=64)
-        first_z = CHUNKS + LAG
-        z_upper = [
-            upper[:, first_z + 4 * c : first_z + 4 * (c + 1), :].rearrange("p r t -> p (r t)").rearrange("p (t i) -> p t i", i=4)
-            for c in range(CHUNKS)
-        ]
-        last_row = [CHUNKS + c if c < LAG else first_z + 4 * (c - LAG) for c in range(CHUNKS)]
+        def second_product(acc, a, c, parts):
+            for i, (n, t0, width) in enumerate(parts):
+                nc.tensor.matmul_mx(
+                    out=acc[:, width * i : width * (i + 1)],
+                    lhsT=w2_codes[:, a, 2 * P * n : 2 * P * (n + 1)].bitcast(FP4X4),
+                    lhsT_scale=w2_planes[:, a, P * n : P * (n + 1)],
+                    rhs=z_codes[a, c][:, t0 : t0 + width].bitcast(FP8X4),
+                    rhs_scale=z_planes[a, c][:, t0 : t0 + width],
+                    start=(a == 0 and i == 0),
+                    stop=(a == PASSES - 1 and i == len(parts) - 1),
+                )
+
+        z_upper = [keep.tile([P, BANK, 4], BF16, name="z_upper%d" % c, align_bytes=64)[:] for c in range(CHUNKS)]
 
         def turn_back_pair(c):
             src = z_turned[c][:].rearrange("t b u p e -> t (b u p e)").bitcast(F32)
             dst = z_upper[c].rearrange("p t i -> p (t i)").bitcast(F32).rearrange("p (t u) -> p t u", u=2)
-            pairs = banks[(6 + c) % 8]
+            pairs = next_bank()
             for b in range(4):
                 nc.tensor.transpose(pairs[:, P * b : P * (b + 1)], src[:, 2 * P * b : 2 * P * b + P], ident[:])
-            nc.scalar.copy(out=dst[:, :, 0], in_=pairs)
+            nc.scalar.copy(out=dst, in_=pairs.unsqueeze(2).to_broadcast([P, BANK, 2]))
 
         def turn_back_single(c):
-            back = banks[(6 + c) % 8].bitcast(BF16)[:, 0:BANK]
+            back = next_bank().bitcast(BF16)[:, 0:BANK]
             for b in range(4):
                 nc.tensor.transpose(back[:, P * b : P * (b + 1)], single(c)[:, b, :], ident_bf16[:])
-            nc.scalar.copy(out=upper[:, c, :], in_=back)
+            nc.scalar.copy(out=rows[:, lane2_row[c]], in_=back.rearrange("p (b t) -> p b t", b=4))
 
-        def average_direct(s, c):
-            cols = slice(BANK * c, BANK * (c + 1))
-            nc.vector.scalar_tensor_tensor(
-                out=upper[:, last_row[c] if s == SLICES - 1 else c, :], in0=olds[s][:, cols], scalar=0.5, in1=pages[s % PAGES][:, cols],
-                op0=ALU.mult, op1=ALU.add,
-            )
+        prepare_w1_lower(0)
+        for j0, j1 in first_pieces:
+            nc.vector.tensor_copy(v_words[1][:, j0:j1], tabs[1][:].bitcast(U32).indirect(offsets[:, j0 // 16 : j1 // 16]))
+        pages.append(big(1, [P, T2], F32))
+        nc.gpsimd.memset(pages[-1][:].bitcast(I32), 0)
+        prepare_w1_lower(1)
+        for piece in first_pieces:
+            first_product(0, piece)
+        prepare_w1_lower(2)
+        pages.append(big(3, [P, T2], F32))
+        nc.gpsimd.memset(pages[-1][:].bitcast(I32), 0)
+        for piece in halves:
+            first_product(1, piece)
+        add_turned(0, olds[0], True)
 
-        for s in range(4):
-            first_product(s, 0)
-        for a in range(PASSES):
-            grouped = ring.tile([P, 4, P, 4], BF16, name="wide", tag="wide", align_bytes=64)
-            nc.scalar.copy(
-                out=grouped[:].rearrange("p i m j -> p m i j"),
-                in_=w1_upper[a][:].rearrange("p j (m i) -> p m i j", i=4),
-            )
-            codes = keep.tile([P, 4, P], U32, name="w1_codes_upper%d" % a, align_bytes=64)
-            planes = keep.tile([P, 4, P], U8, name="w1_planes_upper%d" % a, align_bytes=64)
-            nc.vector.quantize_mx(
-                out=codes[:].rearrange("p i m -> p (i m)").bitcast(FP8X4),
-                scales=planes[:].rearrange("p i m -> p (i m)"),
-                in_=grouped[:].rearrange("p i m j -> p (i m j)"),
-            )
-            for i in range(4):
-                w1_codes[4 + i, a] = codes[:, i, :]
-                w1_planes[4 + i, a] = planes[:, i, :]
-
+        z_lower = {}
+        products = {0: [(2, 0), (2, 1)], 1: [(3, 0), (3, 1)], 2: [(4, 0), (4, 1), (5, 0), (7, 0)], 3: [(5, 1), (6, 0)], 4: [(6, 1)], 5: [(7, 1)]}
         for s in range(SLICES):
             scatter(s)
-            if s + 3 < SLICES:
+            if s + 3 < SLICES - 1:
                 load_old(s + 3)
+            if s + 3 == SLICES - 1:
+                load_old_last()
+            if s == 0:
+                prepare_w1_lower(3)
+            if s == 1:
+                prepare_w1_upper(1)
+                quantize_w1(6, lanes_grouped[:])
+            for later, f in products.get(s, ()):
+                first_product(later, halves[f])
+            if s == 0:
+                prepare_w1_upper(0)
             if s < SLICES - 1:
-                average_turned(s)
-            if s < 2:
-                first_product(2 * s + 4, 2)
-                first_product(2 * s + 5, 4)
+                sum_turned(s)
             if s == 3:
                 for c in range(CHUNKS):
-                    grouped = ring.tile([P, BANK, 4], BF16, name="wide", tag="wide", align_bytes=64)
-                    turn_back(c, grouped)
-                    quantize_z(0, c, grouped)
+                    if c % 2 == 0:
+                        both = big(c, [P, 2, BANK, 4], BF16)
+                    z_lower[c] = both[:, c % 2, :, :]
+                    turn_back(c, z_lower[c])
+                    if c < EARLY_CHUNKS:
+                        z_tiles(0, c, "codes0_%d" % c)
+                        quantize_z(0, c, z_lower[c], slice(0, BANK))
             if s == SLICES - 3:
-                for c in range(EARLY):
+                for c in range(CHUNKS):
                     turn_back_pair(c)
             if s == SLICES - 2:
+                acc_banks = [next_bank() for c in range(CHUNKS)]
                 for c in range(CHUNKS):
-                    if c >= EARLY:
-                        turn_back_pair(c)
                     turn_back_single(c)
+            if s + 1 < SLICES - 1:
+                add_turned(s + 1, olds[s + 1], True)
 
         last = SLICES - 1
-        accs = {}
-        for idx in range(8):
-            c, n = divmod(idx, N_TILES)
-            accs[c, n] = banks[(idx + 2) % 8]
-            second_product(accs[c, n], 0, c, n)
-        for c in range(CHUNKS):
-            average_direct(last, c)
-            both = upper[:, c : last_row[c] + 1 : last_row[c] - c, :]
-            nc.vector.tensor_copy(out=z_upper[c][:, :, 2:4], in_=both.rearrange("p e t -> p t e"))
-            quantize_z(1, c, z_upper[c])
+        acc_banks = acc_banks + taken[-CHUNKS:]
         out_rows = out.rearrange("(n p) t -> p n t", p=P)
+        groups = []
         for c in range(CHUNKS):
-            result = stream.tile([P, N_TILES, BANK], F32, name="stream", tag="stream", align_bytes=64)
-            for n in range(N_TILES):
-                idx = N_TILES * c + n
-                if (c, n) not in accs:
-                    accs[c, n] = banks[(idx + 2) % 8]
-                    second_product(accs[c, n], 0, c, n)
-                second_product(accs[c, n], 1, c, n)
-                magnitude = hpool.tile([P, BANK], F32, name="h", tag="h", align_bytes=64)
-                if idx >= SCALAR_ABS:
-                    signed = hpool.tile([P, BANK], F32, name="h", tag="h", align_bytes=64)
-                    nc.vector.tensor_copy(out=signed[:], in_=accs[c, n][:])
-                    nc.vector.scalar_tensor_tensor(
-                        out=magnitude[:], in0=signed[:], scalar=-1.0, in1=signed[:], op0=ALU.mult, op1=ALU.max
-                    )
+            for g in range(N_TILES):
+                if c == 0 and g < 2:
+                    b = 3 - g
+                    groups.append((c, [(n, P * b, P) for n in range(N_TILES)], out_rows[:, :, P * b : P * (b + 1)]))
+                elif c == 0:
+                    pair = (2 * g - 4, 2 * g - 3)
+                    groups.append((c, [(n, P * b, P) for n in pair for b in (0, 1)], out_rows[:, pair[0] : pair[1] + 1, 0 : 2 * P]))
                 else:
-                    nc.scalar.activation(out=magnitude[:], in_=accs[c, n][:], func=ACT.Abs)
-                nc.scalar.activation(out=result[:, n, :], in_=magnitude[:], func=ACT.Ln, bias=one[:])
-                nc.sync.dma_start(out=out_rows[:, n, BANK * c : BANK * (c + 1)], in_=result[:, n, :])
+                    groups.append((c, [(g, 0, BANK)], out_rows[:, g : g + 1, BANK * c : BANK * (c + 1)]))
+        for idx in range(N_TILES * EARLY_CHUNKS):
+            second_product(acc_banks[idx], 0, *groups[idx][:2])
+        for c in range(CHUNKS):
+            z_tiles(1, c, "codes1_%d" % c)
+            for b0, b1 in ((3, 4), (2, 3), (0, 2)) if c == 0 else ((0, 4),):
+                cols = slice(BANK * c + P * b0, BANK * c + P * b1)
+                if (c, b0) == (0, 0):
+                    both = rows[:, lane2_row[c]].rearrange("p (e b) t -> p e b t", e=2)
+                else:
+                    both = rows[:, lane2_row[c] : lane3_row[c] + 1 : lane3_row[c] - lane2_row[c], b0:b1, :]
+                nc.vector.tensor_tensor(
+                    both[:, 1],
+                    old_last[c][:, P * b0 : P * b1].rearrange("p (b t) -> p b t", t=P),
+                    pages[last % PAGES][:, cols].rearrange("p (b t) -> p b t", t=P),
+                    ALU.add,
+                )
+                nc.vector.tensor_copy(
+                    out=z_upper[c][:, P * b0 : P * b1, 2:4].rearrange("p (b t) e -> p b t e", t=P),
+                    in_=both.rearrange("p e b t -> p b t e"),
+                )
+                quantize_z(1, c, z_upper[c], slice(P * b0, P * b1))
+            late = c + EARLY_CHUNKS
+            if late < CHUNKS:
+                z_tiles(0, late, "old_last%d" % c)
+                quantize_z(0, late, z_lower[late], slice(0, BANK))
+        for idx, (c, parts, dst) in enumerate(groups):
+            acc = acc_banks[idx % 8]
+            if idx % N_TILES == 0:
+                result = stream.tile([P, N_TILES, BANK], F32, name="stream", tag="stream", align_bytes=64)
+            if idx >= N_TILES * EARLY_CHUNKS:
+                second_product(acc, 0, c, parts)
+            second_product(acc, 1, c, parts)
+            staged = slot(idx % 7, [P, 2, BANK], F32)
+            magnitude = staged[:, 0, :]
+            if idx in VECTOR_ABS:
+                signed = staged[:, 1, :]
+                nc.vector.tensor_copy(out=signed, in_=acc)
+                nc.vector.scalar_tensor_tensor(
+                    out=magnitude, in0=signed, scalar=-1.0, in1=signed, op0=ALU.mult, op1=ALU.max
+                )
+            else:
+                nc.scalar.activation(out=magnitude, in_=acc, func=ACT.Abs)
+            logs = result[:, idx % N_TILES, :]
+            nc.scalar.activation(out=logs, in_=magnitude, func=ACT.Ln, bias=one[:], scale=0.5)
+            nc.sync.dma_start(out=dst, in_=logs.rearrange("p (n t) -> p n t", n=dst.shape[1]))

@@ -323,7 +323,7 @@ def tile_list_early_exit_refill_kernel(
             pairs = next_bank()
             for b in range(4):
                 nc.tensor.transpose(pairs[:, P * b : P * (b + 1)], src[:, 2 * P * b : 2 * P * b + P], ident[:])
-            nc.scalar.copy(out=dst, in_=pairs.unsqueeze(2).to_broadcast([P, BANK, 2]))
+            nc.scalar.copy(out=dst[:, :, 0], in_=pairs)
 
         def turn_back_single(c):
             back = next_bank().bitcast(BF16)[:, 0:BANK]

@@ -18,14 +18,20 @@ ACT = mybir.ActivationFunctionType
 ALU = mybir.AluOpType
 
 BANK = 512
+PASS_ROWS = 512
 PASSES = 2
 SLICES = H // P
 CHUNKS = T2 // BANK
 N_TILES = N // P
+AS_THEY_LIE = 4
+FIRST_LANE_SLICE = 6
 PAGES = 3
 STREAM_BUFS = 5
-VECTOR_ABS = (9, 11, 13, 14, 15)
+OLD_AHEAD = 3
+EARLY_HALVES = {2: (5, 7), 3: (6,)}
 EARLY_CHUNKS = 1
+VECTOR_ABS = (9, 11, 13, 14, 15)
+STAGING_SLOTS = 7
 
 
 def tile_list_early_exit_refill_kernel(
@@ -62,11 +68,8 @@ def tile_list_early_exit_refill_kernel(
         ident_bf16 = keep.tile([P, P], BF16, name="ident_bf16")
         nc.scalar.copy(out=ident_bf16[:], in_=ident[:])
         w2_planes = keep.tile([P, PASSES, N], U8, name="w2_planes", align_bytes=64)
-        pages = [keep.tile([P, T2], F32, name="page0")]
-        nc.vector.memset(pages[0][:].bitcast(I32), 0)
+        nc.vector.memset(w2_planes[:].rearrange("p a n -> p (a n)").bitcast(I32), 0)
 
-        offsets = keep.tile([P, S // 16], U16, name="offsets")
-        nc.sync.dma_start(offsets[:], offs)
         tabs = [big(a, [P, T], I32) for a in range(PASSES)]
 
         def load_tab(a):
@@ -77,46 +80,50 @@ def tile_list_early_exit_refill_kernel(
         def load_w1_lower(s, index):
             raw = slot(index, [P, PASSES, 4, P], F32)
             for a in range(PASSES):
-                rows = w1[512 * a : 512 * (a + 1), P * s : P * (s + 1)]
-                nc.sync.dma_start(out=raw[:, a, :, :], in_=rows.rearrange("(p j) c -> p j c", j=4))
+                part = w1[PASS_ROWS * a : PASS_ROWS * (a + 1), P * s : P * (s + 1)]
+                nc.sync.dma_start(out=raw[:, a, :, :], in_=part.rearrange("(p j) c -> p j c", j=4))
             w1_raw[s] = raw
 
         def load_w1_upper(half, indices):
+            c0 = PASS_ROWS + 2 * P * half
             for a in range(PASSES):
                 raw = slot(indices[a], [P, 4, 2 * P], F32)
-                rows = w1[512 * a : 512 * (a + 1), 512 + 2 * P * half : 512 + 2 * P * (half + 1)]
-                nc.sync.dma_start(out=raw[:], in_=rows.rearrange("(p j) c -> p j c", j=4))
-                w1_raw[4 + half, a] = raw
+                part = w1[PASS_ROWS * a : PASS_ROWS * (a + 1), c0 : c0 + 2 * P]
+                nc.sync.dma_start(out=raw[:], in_=part.rearrange("(p j) c -> p j c", j=4))
+                w1_raw[AS_THEY_LIE + half, a] = raw
 
         olds = {}
+        old_lanes = old[PASS_ROWS:H, :].rearrange("(p i) t -> p i t", i=4)
 
         def load_old(s):
             tile = stream.tile([P, T2], F32, name="stream", tag="stream", align_bytes=64)
-            lanes = old[512:1024, :].rearrange("(p i) t -> p i t", i=4)
-            if s < 4:
+            if s < AS_THEY_LIE:
                 nc.sync.dma_start(out=tile[:], in_=old[P * s : P * (s + 1), :])
-            elif s < 6:
+            elif s < FIRST_LANE_SLICE:
+                m0 = 64 * (s - AS_THEY_LIE)
                 for e in range(2):
-                    nc.sync.dma_start(out=tile[e:P:2, :], in_=lanes[64 * (s - 4) : 64 * (s - 3), e, :])
+                    nc.sync.dma_start(out=tile[e:P:2, :], in_=old_lanes[m0 : m0 + 64, e, :])
             else:
-                nc.sync.dma_start(out=tile[:], in_=lanes[:, s - 4, :])
+                nc.sync.dma_start(out=tile[:], in_=old_lanes[:, s - AS_THEY_LIE, :])
             olds[s] = tile
 
         old_last = []
 
         def load_old_last():
-            lane = old[512:1024, :].rearrange("(p i) t -> p i t", i=4)[:, 3, :]
             for c in range(CHUNKS):
                 old_last.append(keep.tile([P, BANK], F32, name="old_last", tag="old_last%d" % c, align_bytes=64))
-                nc.sync.dma_start(out=old_last[c][:], in_=lane[:, BANK * c : BANK * (c + 1)])
+                nc.sync.dma_start(out=old_last[c][:], in_=old_lanes[:, 3, BANK * c : BANK * (c + 1)])
 
-        scale_rows = keep.tile([P, T // 4], I32, name="scale_rows")
+        scale_rows = big(4, [P, T // 4], I32)
         for q in range(4):
             queue = nc.sync if q < 2 else nc.scalar
             queue.dma_start(out=scale_rows[32 * q : 32 * q + 8, :], in_=tab_scales[:, 4 * q : 4 * q + 4, :].bitcast(I32))
-        for q in range(4):
+        for q in (0, 2, 1, 3):
             nc.vector.tensor_copy(tab_planes[32 * q : 32 * q + 8, :].bitcast(I32), scale_rows[32 * q : 32 * q + 8, :])
-        nc.vector.memset(w2_planes[:].rearrange("p a n -> p (a n)").bitcast(I32), 0)
+        pages = [big(4, [P, T2], F32)]
+        nc.gpsimd.memset(pages[0][:].bitcast(I32), 0)
+        offsets = keep.tile([P, S // 16], U16, name="offsets")
+        nc.sync.dma_start(offsets[:], offs)
         load_tab(0)
         load_w1_lower(0, 6)
         load_tab(1)
@@ -173,7 +180,7 @@ def tile_list_early_exit_refill_kernel(
                     w1_planes[first + i, a] = planes[:, i, a, :]
 
         def prepare_w1_lower(s):
-            if s == 2:
+            if s == PAGES - 1:
                 grouped = big(3, [P, 1, PASSES, P, 4], BF16)
             else:
                 grouped = ring.tile([P, 1, PASSES, P, 4], BF16, name="w1_grouped", tag="w1_grouped", align_bytes=64)
@@ -189,15 +196,16 @@ def tile_list_early_exit_refill_kernel(
         def prepare_w1_upper(half):
             grouped = ring.tile([P, 1, PASSES, P, 4], BF16, name="w1_grouped", tag="w1_grouped", align_bytes=64)
             for a in range(PASSES):
-                raw = w1_raw[4 + half, a][:].rearrange("p j (m i) -> p m j i", i=4)
+                raw = w1_raw[AS_THEY_LIE + half, a][:].rearrange("p j (m i) -> p m j i", i=4)
                 nc.scalar.copy(out=grouped[:, 0, a, :, :].rearrange("p (m e) j -> p m j e", e=2), in_=raw[:, :, :, 0:2])
                 nc.scalar.copy(
                     out=lanes_grouped[:, :, a, 64 * half : 64 * (half + 1), :].rearrange("p i m j -> p m j i"),
                     in_=raw[:, :, :, 2:4],
                 )
-            quantize_w1(4 + half, grouped[:])
+            quantize_w1(AS_THEY_LIE + half, grouped[:])
 
-        hs = {}
+        h_tiles = {}
+        h_pieces = {}
         h_first = keep.tile([P, BANK], F32, name="h_first")
 
         def first_product(s, piece):
@@ -205,10 +213,10 @@ def tile_list_early_exit_refill_kernel(
             if s == 0 and piece[0] < BANK:
                 h = h_first[:, cols]
             else:
-                if s not in hs:
-                    hs[s] = slot(s, [P, S], F32)[:]
-                h = hs[s][:, cols]
-            hs[s, piece] = h
+                if s not in h_tiles:
+                    h_tiles[s] = slot(s, [P, S], F32)[:]
+                h = h_tiles[s][:, cols]
+            h_pieces[s, piece] = h
             acc = next_bank()[:, 0 : piece[1] - piece[0]]
             for a in range(PASSES):
                 nc.tensor.matmul_mx(
@@ -224,26 +232,26 @@ def tile_list_early_exit_refill_kernel(
 
         def scatter(s):
             page = pages[s % PAGES]
-            weights = wgs_rows[:] if s < 4 else wgs_pair[:] if s < 6 else wgs_lanes[:, s - 6, :]
+            if s < AS_THEY_LIE:
+                weights = wgs_rows[:]
+            elif s < FIRST_LANE_SLICE:
+                weights = wgs_pair[:]
+            else:
+                weights = wgs_lanes[:, s - FIRST_LANE_SLICE, :]
             if s == 0:
                 for j0, j1 in first_pieces:
                     places = page[:].indirect(offsets2[:, j0 // 16 : j1 // 16])
-                    nc.vector.tensor_tensor(places, hs[s, (j0, j1)], weights[:, j0:j1], ALU.mult)
+                    nc.vector.tensor_tensor(places, h_pieces[s, (j0, j1)], weights[:, j0:j1], ALU.mult)
             else:
-                nc.vector.tensor_tensor(page[:].indirect(offsets2[:]), hs[s][:], weights, ALU.mult)
+                nc.vector.tensor_tensor(page[:].indirect(offsets2[:]), h_tiles[s], weights, ALU.mult)
 
-        z_turned = [
-            keep.tile([P, 4, 2, P, 2], BF16, name="z_turned%d" % c, align_bytes=64)
-            for c in range(CHUNKS)
-        ]
+        z_turned = [keep.tile([P, 4, 2, P, 2], BF16, name="z_turned%d" % c, align_bytes=64) for c in range(CHUNKS)]
 
-        rows = keep.tile([P, 2 * CHUNKS * BANK], BF16, name="rows", align_bytes=64)[:].rearrange("p (r b t) -> p r b t", b=4, t=P)
+        lane_tile = keep.tile([P, 2 * CHUNKS * BANK], BF16, name="rows", align_bytes=64)
+        rows = lane_tile[:].rearrange("p (r b t) -> p r b t", b=4, t=P)
         lane2_row = [CHUNKS - 1 - c for c in range(CHUNKS)]
         turned_row = [CHUNKS + c for c in range(CHUNKS)]
         lane3_row = [turned_row[-1], turned_row[-1], lane2_row[0], lane2_row[1]]
-
-        def single(c):
-            return rows[:, turned_row[c]]
 
         sum_banks = {}
 
@@ -262,18 +270,18 @@ def tile_list_early_exit_refill_kernel(
             add_turned(s, pages[s % PAGES], False)
             sums = [bank.rearrange("t (b r) -> t b r", b=4) for bank in sum_banks[s]]
             for c in range(CHUNKS):
-                if s < 4:
+                if s < AS_THEY_LIE:
                     nc.scalar.copy(
                         out=z_turned[c][:, :, :, 32 * s : 32 * (s + 1), :],
                         in_=sums[c].rearrange("t b (q u e) -> t b u q e", u=2, e=2),
                     )
-                elif s < 6:
+                elif s < FIRST_LANE_SLICE:
+                    m0 = 64 * (s - AS_THEY_LIE)
                     nc.scalar.copy(
-                        out=z_turned[c][:, :, 0, 64 * (s - 4) : 64 * (s - 3), :].rearrange("t b m e -> t b (m e)"),
-                        in_=sums[c],
+                        out=z_turned[c][:, :, 0, m0 : m0 + 64, :].rearrange("t b m e -> t b (m e)"), in_=sums[c]
                     )
                 else:
-                    nc.scalar.copy(out=single(c), in_=sums[c])
+                    nc.scalar.copy(out=rows[:, turned_row[c]], in_=sums[c])
 
         def turn_back(c, grouped):
             src = z_turned[c][:].rearrange("t b u p e -> t (b u p e)").bitcast(F32)
@@ -325,10 +333,10 @@ def tile_list_early_exit_refill_kernel(
                 nc.tensor.transpose(pairs[:, P * b : P * (b + 1)], src[:, 2 * P * b : 2 * P * b + P], ident[:])
             nc.scalar.copy(out=dst[:, :, 0], in_=pairs)
 
-        def turn_back_single(c):
+        def turn_back_lane2(c):
             back = next_bank().bitcast(BF16)[:, 0:BANK]
             for b in range(4):
-                nc.tensor.transpose(back[:, P * b : P * (b + 1)], single(c)[:, b, :], ident_bf16[:])
+                nc.tensor.transpose(back[:, P * b : P * (b + 1)], rows[:, turned_row[c], b, :], ident_bf16[:])
             nc.scalar.copy(out=rows[:, lane2_row[c]], in_=back.rearrange("p (b t) -> p b t", b=4))
 
         prepare_w1_lower(0)
@@ -347,44 +355,47 @@ def tile_list_early_exit_refill_kernel(
         add_turned(0, olds[0], True)
 
         z_lower = {}
-        products = {0: [(2, 0), (2, 1)], 1: [(3, 0), (3, 1)], 2: [(4, 0), (4, 1), (5, 0), (7, 0)], 3: [(5, 1), (6, 0)], 4: [(6, 1)], 5: [(7, 1)]}
+        last = SLICES - 1
         for s in range(SLICES):
             scatter(s)
-            if s + 3 < SLICES - 1:
-                load_old(s + 3)
-            if s + 3 == SLICES - 1:
+            if s + OLD_AHEAD < last:
+                load_old(s + OLD_AHEAD)
+            if s + OLD_AHEAD == last:
                 load_old_last()
             if s == 0:
-                prepare_w1_lower(3)
+                prepare_w1_lower(AS_THEY_LIE - 1)
             if s == 1:
                 prepare_w1_upper(1)
-                quantize_w1(6, lanes_grouped[:])
-            for later, f in products.get(s, ()):
-                first_product(later, halves[f])
+                quantize_w1(FIRST_LANE_SLICE, lanes_grouped[:])
+            if s + 2 < SLICES:
+                for piece in halves:
+                    if (s + 2, piece) not in h_pieces:
+                        first_product(s + 2, piece)
+            for early in EARLY_HALVES.get(s, ()):
+                first_product(early, halves[0])
             if s == 0:
                 prepare_w1_upper(0)
-            if s < SLICES - 1:
+            if s < last:
                 sum_turned(s)
-            if s == 3:
+            if s == AS_THEY_LIE - 1:
                 for c in range(CHUNKS):
                     if c % 2 == 0:
-                        both = big(c, [P, 2, BANK, 4], BF16)
-                    z_lower[c] = both[:, c % 2, :, :]
+                        two_chunks = big(c, [P, 2, BANK, 4], BF16)
+                    z_lower[c] = two_chunks[:, c % 2, :, :]
                     turn_back(c, z_lower[c])
                     if c < EARLY_CHUNKS:
                         z_tiles(0, c, "codes0_%d" % c)
                         quantize_z(0, c, z_lower[c], slice(0, BANK))
-            if s == SLICES - 3:
+            if s == FIRST_LANE_SLICE - 1:
                 for c in range(CHUNKS):
                     turn_back_pair(c)
-            if s == SLICES - 2:
+            if s == FIRST_LANE_SLICE:
                 acc_banks = [next_bank() for c in range(CHUNKS)]
                 for c in range(CHUNKS):
-                    turn_back_single(c)
-            if s + 1 < SLICES - 1:
+                    turn_back_lane2(c)
+            if s + 1 < last:
                 add_turned(s + 1, olds[s + 1], True)
 
-        last = SLICES - 1
         acc_banks = acc_banks + taken[-CHUNKS:]
         out_rows = out.rearrange("(n p) t -> p n t", p=P)
         groups = []
@@ -395,7 +406,8 @@ def tile_list_early_exit_refill_kernel(
                     groups.append((c, [(n, P * b, P) for n in range(N_TILES)], out_rows[:, :, P * b : P * (b + 1)]))
                 elif c == 0:
                     pair = (2 * g - 4, 2 * g - 3)
-                    groups.append((c, [(n, P * b, P) for n in pair for b in (0, 1)], out_rows[:, pair[0] : pair[1] + 1, 0 : 2 * P]))
+                    parts = [(n, P * b, P) for n in pair for b in (0, 1)]
+                    groups.append((c, parts, out_rows[:, pair[0] : pair[1] + 1, 0 : 2 * P]))
                 else:
                     groups.append((c, [(g, 0, BANK)], out_rows[:, g : g + 1, BANK * c : BANK * (c + 1)]))
         for idx in range(N_TILES * EARLY_CHUNKS):
@@ -424,13 +436,13 @@ def tile_list_early_exit_refill_kernel(
                 z_tiles(0, late, "old_last%d" % c)
                 quantize_z(0, late, z_lower[late], slice(0, BANK))
         for idx, (c, parts, dst) in enumerate(groups):
-            acc = acc_banks[idx % 8]
+            acc = acc_banks[idx % len(acc_banks)]
             if idx % N_TILES == 0:
                 result = stream.tile([P, N_TILES, BANK], F32, name="stream", tag="stream", align_bytes=64)
             if idx >= N_TILES * EARLY_CHUNKS:
                 second_product(acc, 0, c, parts)
             second_product(acc, 1, c, parts)
-            staged = slot(idx % 7, [P, 2, BANK], F32)
+            staged = slot(idx % STAGING_SLOTS, [P, 2, BANK], F32)
             magnitude = staged[:, 0, :]
             if idx in VECTOR_ABS:
                 signed = staged[:, 1, :]

@@ -79,9 +79,10 @@ def tile_list_early_exit_refill_kernel(
 
         def load_w1_lower(s, index):
             raw = slot(index, [P, PASSES, 4, P], F32)
+            queue = nc.scalar if s == 0 else nc.sync
             for a in range(PASSES):
                 part = w1[PASS_ROWS * a : PASS_ROWS * (a + 1), P * s : P * (s + 1)]
-                nc.sync.dma_start(out=raw[:, a, :, :], in_=part.rearrange("(p j) c -> p j c", j=4))
+                queue.dma_start(out=raw[:, a, :, :], in_=part.rearrange("(p j) c -> p j c", j=4))
             w1_raw[s] = raw
 
         def load_w1_upper(half, indices):

@@ -58,7 +58,7 @@ def tile_list_early_exit_refill_kernel(
             return keep.tile(shape, dtype, name="big%d" % index, tag="big%d" % index, align_bytes=64)
 
         tab_planes = keep.tile([P, T], U8, name="tab_planes", align_bytes=64)
-        nc.gpsimd.memset(tab_planes[:].bitcast(I32), 0)
+        nc.vector.memset(tab_planes[:].bitcast(I32), 0)
         one = keep.tile([P, 1], F32, name="one")
         nc.gpsimd.memset(one[:], 1.0)
         zero = keep.tile([P, 1], F32, name="zero")
@@ -79,10 +79,9 @@ def tile_list_early_exit_refill_kernel(
 
         def load_w1_lower(s, index):
             raw = slot(index, [P, PASSES, 4, P], F32)
-            queue = nc.scalar if s == 0 else nc.sync
             for a in range(PASSES):
                 part = w1[PASS_ROWS * a : PASS_ROWS * (a + 1), P * s : P * (s + 1)]
-                queue.dma_start(out=raw[:, a, :, :], in_=part.rearrange("(p j) c -> p j c", j=4))
+                nc.sync.dma_start(out=raw[:, a, :, :], in_=part.rearrange("(p j) c -> p j c", j=4))
             w1_raw[s] = raw
 
         def load_w1_upper(half, indices):
@@ -115,17 +114,16 @@ def tile_list_early_exit_refill_kernel(
                 old_last.append(keep.tile([P, BANK], F32, name="old_last", tag="old_last%d" % c, align_bytes=64))
                 nc.sync.dma_start(out=old_last[c][:], in_=old_lanes[:, 3, BANK * c : BANK * (c + 1)])
 
-        scale_rows = big(4, [P, T // 4], I32)
-        for q in range(4):
-            queue = nc.sync if q < 2 else nc.scalar
-            queue.dma_start(out=scale_rows[32 * q : 32 * q + 8, :], in_=tab_scales[:, 4 * q : 4 * q + 4, :].bitcast(I32))
-        for q in (0, 2, 1, 3):
-            nc.vector.tensor_copy(tab_planes[32 * q : 32 * q + 8, :].bitcast(I32), scale_rows[32 * q : 32 * q + 8, :])
-        pages = [big(4, [P, T2], F32)]
-        nc.gpsimd.memset(pages[0][:].bitcast(I32), 0)
+        pages = [big(4, [P, T2], F32), big(3, [P, T2], F32)]
+        for page in pages:
+            nc.vector.memset(page[:].bitcast(I32), 0)
         offsets = keep.tile([P, S // 16], U16, name="offsets")
         nc.sync.dma_start(offsets[:], offs)
         load_tab(0)
+        for q in range(4):
+            nc.sync.dma_start(
+                out=tab_planes[32 * q : 32 * q + 8, :].bitcast(I32), in_=tab_scales[:, 4 * q : 4 * q + 4, :].bitcast(I32)
+            )
         load_w1_lower(0, 6)
         load_tab(1)
         offsets2 = keep.tile([P, S // 16], U16, name="offsets2")
@@ -160,8 +158,8 @@ def tile_list_early_exit_refill_kernel(
         v_words = [keep.tile([P, S], U32, name="v_words%d" % a, align_bytes=64) for a in range(PASSES)]
         halves = [(0, BANK), (BANK, S)]
         first_pieces = [(0, BANK // 2), (BANK // 2, BANK), (BANK, S)]
-        nc.vector.tensor_copy(v_planes[:], tab_planes[:].indirect(offsets[:]))
         nc.vector.tensor_copy(v_words[0][:], tabs[0][:].bitcast(U32).indirect(offsets[:]))
+        nc.vector.tensor_copy(v_planes[:], tab_planes[:].indirect(offsets[:]))
 
         w1_codes = {}
         w1_planes = {}
@@ -181,10 +179,7 @@ def tile_list_early_exit_refill_kernel(
                     w1_planes[first + i, a] = planes[:, i, a, :]
 
         def prepare_w1_lower(s):
-            if s == PAGES - 1:
-                grouped = big(3, [P, 1, PASSES, P, 4], BF16)
-            else:
-                grouped = ring.tile([P, 1, PASSES, P, 4], BF16, name="w1_grouped", tag="w1_grouped", align_bytes=64)
+            grouped = ring.tile([P, 1, PASSES, P, 4], BF16, name="w1_grouped", tag="w1_grouped", align_bytes=64)
             for a in range(PASSES):
                 nc.scalar.copy(
                     out=grouped[:, 0, a, :, :].rearrange("p (c i) j -> p c j i", i=4),
@@ -349,8 +344,6 @@ def tile_list_early_exit_refill_kernel(
         for piece in first_pieces:
             first_product(0, piece)
         prepare_w1_lower(2)
-        pages.append(big(3, [P, T2], F32))
-        nc.gpsimd.memset(pages[-1][:].bitcast(I32), 0)
         for piece in halves:
             first_product(1, piece)
         add_turned(0, olds[0], True)

@@ -29,7 +29,7 @@ PAGES = 3
 STREAM_BUFS = 5
 OLD_AHEAD = 3
 EARLY_HALVES = {2: (5, 7), 3: (6,)}
-EARLY_CHUNKS = 1
+PAGE_BUFFERS = (4, 3, 1)
 VECTOR_ABS = (9, 11, 13, 14, 15)
 STAGING_SLOTS = 7
 
@@ -235,9 +235,9 @@ def tile_list_early_exit_refill_kernel(
             else:
                 weights = wgs_lanes[:, s - FIRST_LANE_SLICE, :]
             if s == 0:
-                for j0, j1 in first_pieces:
+                for (j0, j1), h in zip(halves, (h_first[:], h_tiles[0][:, BANK:S])):
                     places = page[:].indirect(offsets2[:, j0 // 16 : j1 // 16])
-                    nc.vector.tensor_tensor(places, h_pieces[s, (j0, j1)], weights[:, j0:j1], ALU.mult)
+                    nc.vector.tensor_tensor(places, h, weights[:, j0:j1], ALU.mult)
             else:
                 nc.vector.tensor_tensor(page[:].indirect(offsets2[:]), h_tiles[s], weights, ALU.mult)
 
@@ -377,9 +377,6 @@ def tile_list_early_exit_refill_kernel(
                         two_chunks = big(c, [P, 2, BANK, 4], BF16)
                     z_lower[c] = two_chunks[:, c % 2, :, :]
                     turn_back(c, z_lower[c])
-                    if c < EARLY_CHUNKS:
-                        z_tiles(0, c, "codes0_%d" % c)
-                        quantize_z(0, c, z_lower[c], slice(0, BANK))
             if s == FIRST_LANE_SLICE - 1:
                 for c in range(CHUNKS):
                     turn_back_pair(c)
@@ -404,8 +401,8 @@ def tile_list_early_exit_refill_kernel(
                     groups.append((c, parts, out_rows[:, pair[0] : pair[1] + 1, 0 : 2 * P]))
                 else:
                     groups.append((c, [(g, 0, BANK)], out_rows[:, g : g + 1, BANK * c : BANK * (c + 1)]))
-        for idx in range(N_TILES * EARLY_CHUNKS):
-            second_product(acc_banks[idx], 0, *groups[idx][:2])
+        z_tiles(0, 0, "big%d" % PAGE_BUFFERS[(last - 1) % PAGES])
+        quantize_z(0, 0, z_lower[0], slice(0, BANK))
         for c in range(CHUNKS):
             z_tiles(1, c, "codes1_%d" % c)
             for b0, b1 in ((3, 4), (2, 3), (0, 2)) if c == 0 else ((0, 4),):
@@ -425,7 +422,7 @@ def tile_list_early_exit_refill_kernel(
                     in_=both.rearrange("p e b t -> p b t e"),
                 )
                 quantize_z(1, c, z_upper[c], slice(P * b0, P * b1))
-            late = c + EARLY_CHUNKS
+            late = c + 1
             if late < CHUNKS:
                 z_tiles(0, late, "old_last%d" % c)
                 quantize_z(0, late, z_lower[late], slice(0, BANK))
@@ -433,8 +430,7 @@ def tile_list_early_exit_refill_kernel(
             acc = acc_banks[idx % len(acc_banks)]
             if idx % N_TILES == 0:
                 result = stream.tile([P, N_TILES, BANK], F32, name="stream", tag="stream", align_bytes=64)
-            if idx >= N_TILES * EARLY_CHUNKS:
-                second_product(acc, 0, c, parts)
+            second_product(acc, 0, c, parts)
             second_product(acc, 1, c, parts)
             staged = slot(idx % STAGING_SLOTS, [P, 2, BANK], F32)
             magnitude = staged[:, 0, :]

@@ -29,6 +29,7 @@ PAGES = 3
 STREAM_BUFS = 5
 OLD_AHEAD = 3
 EARLY_HALVES = {2: (5, 7), 3: (6,)}
+EARLY_TILES = 2
 PAGE_BUFFERS = (4, 3, 1)
 VECTOR_ABS = (9, 11, 13, 14, 15)
 STAGING_SLOTS = 7
@@ -235,9 +236,9 @@ def tile_list_early_exit_refill_kernel(
             else:
                 weights = wgs_lanes[:, s - FIRST_LANE_SLICE, :]
             if s == 0:
-                for (j0, j1), h in zip(halves, (h_first[:], h_tiles[0][:, BANK:S])):
+                for j0, j1 in first_pieces:
                     places = page[:].indirect(offsets2[:, j0 // 16 : j1 // 16])
-                    nc.vector.tensor_tensor(places, h, weights[:, j0:j1], ALU.mult)
+                    nc.vector.tensor_tensor(places, h_pieces[s, (j0, j1)], weights[:, j0:j1], ALU.mult)
             else:
                 nc.vector.tensor_tensor(page[:].indirect(offsets2[:]), h_tiles[s], weights, ALU.mult)
 
@@ -377,6 +378,9 @@ def tile_list_early_exit_refill_kernel(
                         two_chunks = big(c, [P, 2, BANK, 4], BF16)
                     z_lower[c] = two_chunks[:, c % 2, :, :]
                     turn_back(c, z_lower[c])
+                    if c == 0:
+                        z_tiles(0, 0, "codes0_0")
+                        quantize_z(0, 0, z_lower[0], slice(BANK // 2, BANK))
             if s == FIRST_LANE_SLICE - 1:
                 for c in range(CHUNKS):
                     turn_back_pair(c)
@@ -401,8 +405,10 @@ def tile_list_early_exit_refill_kernel(
                     groups.append((c, parts, out_rows[:, pair[0] : pair[1] + 1, 0 : 2 * P]))
                 else:
                     groups.append((c, [(g, 0, BANK)], out_rows[:, g : g + 1, BANK * c : BANK * (c + 1)]))
-        z_tiles(0, 0, "big%d" % PAGE_BUFFERS[(last - 1) % PAGES])
-        quantize_z(0, 0, z_lower[0], slice(0, BANK))
+        for idx in range(EARLY_TILES):
+            second_product(acc_banks[idx], 0, *groups[idx][:2])
+        z_codes[0, 0] = big(PAGE_BUFFERS[(last - 1) % PAGES], [P, BANK // 2], U32)
+        quantize_z(0, 0, z_lower[0], slice(0, BANK // 2))
         for c in range(CHUNKS):
             z_tiles(1, c, "codes1_%d" % c)
             for b0, b1 in ((3, 4), (2, 3), (0, 2)) if c == 0 else ((0, 4),):
@@ -430,7 +436,8 @@ def tile_list_early_exit_refill_kernel(
             acc = acc_banks[idx % len(acc_banks)]
             if idx % N_TILES == 0:
                 result = stream.tile([P, N_TILES, BANK], F32, name="stream", tag="stream", align_bytes=64)
-            second_product(acc, 0, c, parts)
+            if idx >= EARLY_TILES:
+                second_product(acc, 0, c, parts)
             second_product(acc, 1, c, parts)
             staged = slot(idx % STAGING_SLOTS, [P, 2, BANK], F32)
             magnitude = staged[:, 0, :]
@@ -443,5 +450,10 @@ def tile_list_early_exit_refill_kernel(
             else:
                 nc.scalar.activation(out=magnitude, in_=acc, func=ACT.Abs)
             logs = result[:, idx % N_TILES, :]
-            nc.scalar.activation(out=logs, in_=magnitude, func=ACT.Ln, bias=one[:], scale=0.5)
-            nc.sync.dma_start(out=dst, in_=logs.rearrange("p (n t) -> p n t", n=dst.shape[1]))
+            if idx < len(groups) - 1:
+                nc.scalar.activation(out=logs, in_=magnitude, func=ACT.Ln, bias=one[:], scale=0.5)
+                nc.sync.dma_start(out=dst, in_=logs.rearrange("p (n t) -> p n t", n=dst.shape[1]))
+            else:
+                for cols, queue in ((slice(0, 3 * P), nc.sync), (slice(3 * P, BANK), nc.scalar)):
+                    nc.scalar.activation(out=logs[:, cols], in_=magnitude[:, cols], func=ACT.Ln, bias=one[:], scale=0.5)
+                    queue.dma_start(out=dst[:, 0, cols], in_=logs[:, cols])

@@ -31,6 +31,7 @@ OLD_AHEAD = 3
 EARLY_HALVES = {2: (5, 7), 3: (6,)}
 EARLY_TILES = 2
 PAGE_BUFFERS = (4, 3, 1)
+LAST_PIECE = P
 VECTOR_ABS = (9, 11, 13, 14, 15)
 STAGING_SLOTS = 7
 
@@ -115,16 +116,18 @@ def tile_list_early_exit_refill_kernel(
                 old_last.append(keep.tile([P, BANK], F32, name="old_last", tag="old_last%d" % c, align_bytes=64))
                 nc.sync.dma_start(out=old_last[c][:], in_=old_lanes[:, 3, BANK * c : BANK * (c + 1)])
 
-        pages = [big(4, [P, T2], F32), big(3, [P, T2], F32)]
+        pages = [big(index, [P, T2], F32) for index in PAGE_BUFFERS[:2]]
         for page in pages:
             nc.vector.memset(page[:].bitcast(I32), 0)
+        load_tab(0)
         offsets = keep.tile([P, S // 16], U16, name="offsets")
         nc.sync.dma_start(offsets[:], offs)
-        load_tab(0)
         for q in range(4):
-            nc.sync.dma_start(
-                out=tab_planes[32 * q : 32 * q + 8, :].bitcast(I32), in_=tab_scales[:, 4 * q : 4 * q + 4, :].bitcast(I32)
-            )
+            for passes in ([slice(0, 2)] if q % 2 == 0 else [slice(0, 1), slice(1, 2)]):
+                rows_of = slice(32 * q + 4 * passes.start, 32 * q + 4 * passes.stop)
+                nc.sync.dma_start(
+                    out=tab_planes[rows_of, :].bitcast(I32), in_=tab_scales[passes, 4 * q : 4 * q + 4, :].bitcast(I32)
+                )
         load_w1_lower(0, 6)
         load_tab(1)
         offsets2 = keep.tile([P, S // 16], U16, name="offsets2")
@@ -339,7 +342,7 @@ def tile_list_early_exit_refill_kernel(
         prepare_w1_lower(0)
         for j0, j1 in first_pieces:
             nc.vector.tensor_copy(v_words[1][:, j0:j1], tabs[1][:].bitcast(U32).indirect(offsets[:, j0 // 16 : j1 // 16]))
-        pages.append(big(1, [P, T2], F32))
+        pages.append(big(PAGE_BUFFERS[2], [P, T2], F32))
         nc.gpsimd.memset(pages[-1][:].bitcast(I32), 0)
         prepare_w1_lower(1)
         for piece in first_pieces:
@@ -454,6 +457,7 @@ def tile_list_early_exit_refill_kernel(
                 nc.scalar.activation(out=logs, in_=magnitude, func=ACT.Ln, bias=one[:], scale=0.5)
                 nc.sync.dma_start(out=dst, in_=logs.rearrange("p (n t) -> p n t", n=dst.shape[1]))
             else:
-                for cols, queue in ((slice(0, 3 * P), nc.sync), (slice(3 * P, BANK), nc.scalar)):
+                cut = BANK - LAST_PIECE
+                for cols, queue in ((slice(0, cut), nc.sync), (slice(cut, BANK), nc.scalar)):
                     nc.scalar.activation(out=logs[:, cols], in_=magnitude[:, cols], func=ACT.Ln, bias=one[:], scale=0.5)
                     queue.dma_start(out=dst[:, 0, cols], in_=logs[:, cols])

@@ -230,8 +230,11 @@ def tile_list_early_exit_refill_kernel(
                 )
             nc.scalar.activation(out=h, in_=acc, func=ACT.Relu, bias=zero[:])
 
+        def page_of(s):
+            return pages[2 * s % PAGES]
+
         def scatter(s):
-            page = pages[s % PAGES]
+            page = page_of(s)
             if s < AS_THEY_LIE:
                 weights = wgs_rows[:]
             elif s < FIRST_LANE_SLICE:
@@ -239,8 +242,8 @@ def tile_list_early_exit_refill_kernel(
             else:
                 weights = wgs_lanes[:, s - FIRST_LANE_SLICE, :]
             if s == 0:
-                for j0, j1 in first_pieces:
-                    places = page[:].indirect(offsets2[:, j0 // 16 : j1 // 16])
+                for (j0, j1), target in zip(first_pieces, (page, pages[1], page)):
+                    places = target[:].indirect(offsets2[:, j0 // 16 : j1 // 16])
                     nc.vector.tensor_tensor(places, h_pieces[s, (j0, j1)], weights[:, j0:j1], ALU.mult)
             else:
                 nc.vector.tensor_tensor(page[:].indirect(offsets2[:]), h_tiles[s], weights, ALU.mult)
@@ -255,7 +258,7 @@ def tile_list_early_exit_refill_kernel(
 
         sum_banks = {}
 
-        def add_turned(s, src, first):
+        def add_turned(s, src, first, closes):
             if first:
                 sum_banks[s] = [next_bank() for c in range(CHUNKS)]
             for c in range(CHUNKS):
@@ -263,11 +266,13 @@ def tile_list_early_exit_refill_kernel(
                     t0 = BANK * c + P * b
                     nc.tensor.matmul(
                         out=sum_banks[s][c][:, P * b : P * (b + 1)], lhsT=src[:, t0 : t0 + P], rhs=ident[:],
-                        is_transpose=True, start=(first and b == 0), stop=(not first and b == 3),
+                        is_transpose=True, start=(first and b == 0), stop=(closes and b == 3),
                     )
 
         def sum_turned(s):
-            add_turned(s, pages[s % PAGES], False)
+            if s == 0:
+                add_turned(s, pages[1], False, False)
+            add_turned(s, page_of(s), False, True)
             sums = [bank.rearrange("t (b r) -> t b r", b=4) for bank in sum_banks[s]]
             for c in range(CHUNKS):
                 if s < AS_THEY_LIE:
@@ -350,7 +355,7 @@ def tile_list_early_exit_refill_kernel(
         prepare_w1_lower(2)
         for piece in halves:
             first_product(1, piece)
-        add_turned(0, olds[0], True)
+        add_turned(0, olds[0], True, False)
 
         z_lower = {}
         last = SLICES - 1
@@ -392,7 +397,7 @@ def tile_list_early_exit_refill_kernel(
                 for c in range(CHUNKS):
                     turn_back_lane2(c)
             if s + 1 < last:
-                add_turned(s + 1, olds[s + 1], True)
+                add_turned(s + 1, olds[s + 1], True, False)
 
         acc_banks = acc_banks + taken[-CHUNKS:]
         out_rows = out.rearrange("(n p) t -> p n t", p=P)
@@ -410,7 +415,7 @@ def tile_list_early_exit_refill_kernel(
                     groups.append((c, [(g, 0, BANK)], out_rows[:, g : g + 1, BANK * c : BANK * (c + 1)]))
         for idx in range(EARLY_TILES):
             second_product(acc_banks[idx], 0, *groups[idx][:2])
-        z_codes[0, 0] = big(PAGE_BUFFERS[(last - 1) % PAGES], [P, BANK // 2], U32)
+        z_codes[0, 0] = big(PAGE_BUFFERS[2 * (last - 1) % PAGES], [P, BANK // 2], U32)
         quantize_z(0, 0, z_lower[0], slice(0, BANK // 2))
         for c in range(CHUNKS):
             z_tiles(1, c, "codes1_%d" % c)
@@ -423,7 +428,7 @@ def tile_list_early_exit_refill_kernel(
                 nc.vector.tensor_tensor(
                     both[:, 1],
                     old_last[c][:, P * b0 : P * b1].rearrange("p (b t) -> p b t", t=P),
-                    pages[last % PAGES][:, cols].rearrange("p (b t) -> p b t", t=P),
+                    page_of(last)[:, cols].rearrange("p (b t) -> p b t", t=P),
                     ALU.add,
                 )
                 nc.vector.tensor_copy(

@@ -119,9 +119,9 @@ def tile_list_early_exit_refill_kernel(
         pages = [big(index, [P, T2], F32) for index in PAGE_BUFFERS[:2]]
         for page in pages:
             nc.vector.memset(page[:].bitcast(I32), 0)
-        load_tab(0)
         offsets = keep.tile([P, S // 16], U16, name="offsets")
         nc.sync.dma_start(offsets[:], offs)
+        load_tab(0)
         for q in range(4):
             for passes in ([slice(0, 2)] if q % 2 == 0 else [slice(0, 1), slice(1, 2)]):
                 rows_of = slice(32 * q + 4 * passes.start, 32 * q + 4 * passes.stop)
@@ -133,8 +133,9 @@ def tile_list_early_exit_refill_kernel(
         offsets2 = keep.tile([P, S // 16], U16, name="offsets2")
         nc.sync.dma_start(offsets2[:], offs2)
         wgs_rows = keep.tile([P, S], F32, name="wgs_rows")
-        nc.sync.dma_start(out=wgs_rows[:], in_=wgs)
+        nc.sync.dma_start(out=wgs_rows[:, 0:BANK], in_=wgs[:, 0:BANK])
         load_w1_lower(1, 0)
+        nc.sync.dma_start(out=wgs_rows[:, BANK:S], in_=wgs[:, BANK:S])
         load_w1_lower(2, 1)
         load_old(0)
         load_w1_lower(3, 2)

@@ -28,11 +28,14 @@ FIRST_LANE_SLICE = 6
 PAGES = 3
 STREAM_BUFS = 5
 OLD_AHEAD = 3
-EARLY_HALVES = {2: (5, 7), 3: (6,)}
-EARLY_TILES = 2
+EARLY_HALVES = {2: ((5, 0), (7, 0)), 3: ((6, 0),), 4: ((7, 1),)}
+EARLY_TILES = 3
+PIECES = ((384, 512), (256, 384), (0, 256), (512, 768), (768, 1024), (1024, 1536), (1536, 2048))
+DIRECT = 3
+HEIRS = {2: 3, 3: 4, 4: 5, 5: 6}
 PAGE_BUFFERS = (4, 3, 1)
 LAST_PIECE = P
-VECTOR_ABS = (9, 11, 13, 14, 15)
+VECTOR_ABS = (11, 13, 14, 15, 16)
 STAGING_SLOTS = 7
 
 
@@ -110,11 +113,17 @@ def tile_list_early_exit_refill_kernel(
             olds[s] = tile
 
         old_last = []
+        lane_rows = {}
 
         def load_old_last():
-            for c in range(CHUNKS):
-                old_last.append(keep.tile([P, BANK], F32, name="old_last", tag="old_last%d" % c, align_bytes=64))
-                nc.sync.dma_start(out=old_last[c][:], in_=old_lanes[:, 3, BANK * c : BANK * (c + 1)])
+            for i, (t0, t1) in enumerate(PIECES):
+                heir = HEIRS.get(i)
+                extra = 0 if heir is None else (PIECES[heir][1] - PIECES[heir][0]) // 2
+                tile = keep.tile([P, t1 - t0 + extra], F32, name="piece", tag="piece%d" % i, align_bytes=64)
+                old_last.append(tile[:, extra:])
+                nc.sync.dma_start(out=old_last[i], in_=old_lanes[:, 3, t0:t1])
+                if heir is not None:
+                    lane_rows[heir] = tile[:, 0 : 2 * extra].bitcast(BF16).rearrange("p (e t) -> p e t", e=2)
 
         pages = [big(index, [P, T2], F32) for index in PAGE_BUFFERS[:2]]
         for page in pages:
@@ -251,18 +260,17 @@ def tile_list_early_exit_refill_kernel(
 
         z_turned = [keep.tile([P, 4, 2, P, 2], BF16, name="z_turned%d" % c, align_bytes=64) for c in range(CHUNKS)]
 
-        lane_tile = keep.tile([P, 2 * CHUNKS * BANK], BF16, name="rows", align_bytes=64)
-        rows = lane_tile[:].rearrange("p (r b t) -> p r b t", b=4, t=P)
-        lane2_row = [CHUNKS - 1 - c for c in range(CHUNKS)]
-        turned_row = [CHUNKS + c for c in range(CHUNKS)]
-        lane3_row = [turned_row[-1], turned_row[-1], lane2_row[0], lane2_row[1]]
+        lane2_turned = keep.tile([P, CHUNKS - 1, 4, P], BF16, name="lane2_turned", align_bytes=64)
 
         sum_banks = {}
+
+        def chunk_order(s):
+            return range(CHUNKS - 1, -1, -1) if s == FIRST_LANE_SLICE else range(CHUNKS)
 
         def add_turned(s, src, first, closes):
             if first:
                 sum_banks[s] = [next_bank() for c in range(CHUNKS)]
-            for c in range(CHUNKS):
+            for c in chunk_order(s):
                 for b in range(4):
                     t0 = BANK * c + P * b
                     nc.tensor.matmul(
@@ -275,7 +283,7 @@ def tile_list_early_exit_refill_kernel(
                 add_turned(s, pages[1], False, False)
             add_turned(s, page_of(s), False, True)
             sums = [bank.rearrange("t (b r) -> t b r", b=4) for bank in sum_banks[s]]
-            for c in range(CHUNKS):
+            for c in chunk_order(s):
                 if s < AS_THEY_LIE:
                     nc.scalar.copy(
                         out=z_turned[c][:, :, :, 32 * s : 32 * (s + 1), :],
@@ -286,14 +294,16 @@ def tile_list_early_exit_refill_kernel(
                     nc.scalar.copy(
                         out=z_turned[c][:, :, 0, m0 : m0 + 64, :].rearrange("t b m e -> t b (m e)"), in_=sums[c]
                     )
+                elif c > 0:
+                    nc.scalar.copy(out=lane2_turned[:, c - 1], in_=sums[c])
                 else:
-                    nc.scalar.copy(out=rows[:, turned_row[c]], in_=sums[c])
+                    nc.scalar.copy(out=z_turned[c][:, :, 1, :, 0], in_=sums[c])
 
-        def turn_back(c, grouped):
+        def turn_back(c, grouped, halves_and_banks):
             src = z_turned[c][:].rearrange("t b u p e -> t (b u p e)").bitcast(F32)
             dst = grouped.rearrange("p t i -> p (t i)").bitcast(F32)
-            for hb in range(2):
-                pairs = next_bank().rearrange("p (b u t) -> p b u t", b=2, u=2)
+            for hb, bank in halves_and_banks:
+                pairs = bank.rearrange("p (b u t) -> p b u t", b=2, u=2)
                 for b in range(2):
                     for u in range(2):
                         w0 = P * (2 * (2 * hb + b) + u)
@@ -340,10 +350,12 @@ def tile_list_early_exit_refill_kernel(
             nc.scalar.copy(out=dst[:, :, 0], in_=pairs)
 
         def turn_back_lane2(c):
-            back = next_bank().bitcast(BF16)[:, 0:BANK]
+            back = sum_banks[FIRST_LANE_SLICE][c].bitcast(BF16)[:, 0:BANK]
             for b in range(4):
-                nc.tensor.transpose(back[:, P * b : P * (b + 1)], rows[:, turned_row[c], b, :], ident_bf16[:])
-            nc.scalar.copy(out=rows[:, lane2_row[c]], in_=back.rearrange("p (b t) -> p b t", b=4))
+                nc.tensor.transpose(back[:, P * b : P * (b + 1)], lane2_turned[:, c - 1, b, :], ident_bf16[:])
+            for i, (t0, t1) in enumerate(PIECES):
+                if t0 // BANK == c:
+                    nc.scalar.copy(out=lane_rows[i][:, 0, :], in_=back[:, t0 % BANK : t0 % BANK + t1 - t0])
 
         prepare_w1_lower(0)
         for j0, j1 in first_pieces:
@@ -375,8 +387,8 @@ def tile_list_early_exit_refill_kernel(
                 for piece in halves:
                     if (s + 2, piece) not in h_pieces:
                         first_product(s + 2, piece)
-            for early in EARLY_HALVES.get(s, ()):
-                first_product(early, halves[0])
+            for early, half in EARLY_HALVES.get(s, ()):
+                first_product(early, halves[half])
             if s == 0:
                 prepare_w1_upper(0)
             if s < last:
@@ -386,79 +398,71 @@ def tile_list_early_exit_refill_kernel(
                     if c % 2 == 0:
                         two_chunks = big(c, [P, 2, BANK, 4], BF16)
                     z_lower[c] = two_chunks[:, c % 2, :, :]
-                    turn_back(c, z_lower[c])
+                    turn_back(c, z_lower[c], [(hb, next_bank()) for hb in range(2)])
                     if c == 0:
                         z_tiles(0, 0, "codes0_0")
                         quantize_z(0, 0, z_lower[0], slice(BANK // 2, BANK))
             if s == FIRST_LANE_SLICE - 1:
-                for c in range(CHUNKS):
+                for c in range(1, CHUNKS):
                     turn_back_pair(c)
             if s == FIRST_LANE_SLICE:
                 acc_banks = [next_bank() for c in range(CHUNKS)]
-                for c in range(CHUNKS):
+                for c in range(CHUNKS - 1, 0, -1):
                     turn_back_lane2(c)
+                turn_back(0, z_upper[0], [(1, sum_banks[s][3]), (0, sum_banks[s][2])])
             if s + 1 < last:
                 add_turned(s + 1, olds[s + 1], True, False)
 
-        acc_banks = acc_banks + taken[-CHUNKS:]
+        freed = sum_banks[FIRST_LANE_SLICE]
+        acc_banks = acc_banks[0:3] + [freed[3], freed[2], acc_banks[3], freed[1], freed[0]]
         out_rows = out.rearrange("(n p) t -> p n t", p=P)
         groups = []
-        for c in range(CHUNKS):
-            for g in range(N_TILES):
-                if c == 0 and g < 2:
-                    b = 3 - g
-                    groups.append((c, [(n, P * b, P) for n in range(N_TILES)], out_rows[:, :, P * b : P * (b + 1)]))
-                elif c == 0:
-                    pair = (2 * g - 4, 2 * g - 3)
-                    parts = [(n, P * b, P) for n in pair for b in (0, 1)]
-                    groups.append((c, parts, out_rows[:, pair[0] : pair[1] + 1, 0 : 2 * P]))
-                else:
-                    groups.append((c, [(g, 0, BANK)], out_rows[:, g : g + 1, BANK * c : BANK * (c + 1)]))
+        for i, (t0, t1) in enumerate(PIECES):
+            c, width = t0 // BANK, t1 - t0
+            count = 2 if i == 0 else BANK // width
+            for n0 in range(0, N_TILES, count):
+                parts = [(n, t0 % BANK, width) for n in range(n0, n0 + count)]
+                groups.append((c, parts, out_rows[:, n0 : n0 + count, t0:t1]))
         for idx in range(EARLY_TILES):
             second_product(acc_banks[idx], 0, *groups[idx][:2])
         z_codes[0, 0] = big(PAGE_BUFFERS[2 * (last - 1) % PAGES], [P, BANK // 2], U32)
         quantize_z(0, 0, z_lower[0], slice(0, BANK // 2))
-        for c in range(CHUNKS):
-            z_tiles(1, c, "codes1_%d" % c)
-            for b0, b1 in ((3, 4), (2, 3), (0, 2)) if c == 0 else ((0, 4),):
-                cols = slice(BANK * c + P * b0, BANK * c + P * b1)
-                if (c, b0) == (0, 0):
-                    both = rows[:, lane2_row[c]].rearrange("p (e b) t -> p e b t", e=2)
-                else:
-                    both = rows[:, lane2_row[c] : lane3_row[c] + 1 : lane3_row[c] - lane2_row[c], b0:b1, :]
-                nc.vector.tensor_tensor(
-                    both[:, 1],
-                    old_last[c][:, P * b0 : P * b1].rearrange("p (b t) -> p b t", t=P),
-                    page_of(last)[:, cols].rearrange("p (b t) -> p b t", t=P),
-                    ALU.add,
-                )
-                nc.vector.tensor_copy(
-                    out=z_upper[c][:, P * b0 : P * b1, 2:4].rearrange("p (b t) e -> p b t e", t=P),
-                    in_=both.rearrange("p e b t -> p b t e"),
-                )
-                quantize_z(1, c, z_upper[c], slice(P * b0, P * b1))
-            late = c + 1
-            if late < CHUNKS:
-                z_tiles(0, late, "old_last%d" % c)
-                quantize_z(0, late, z_lower[late], slice(0, BANK))
+        for i, (t0, t1) in enumerate(PIECES):
+            c = t0 // BANK
+            cols = slice(t0 % BANK, t0 % BANK + t1 - t0)
+            if (1, c) not in z_codes:
+                z_tiles(1, c, "codes1_%d" % c)
+            target = z_upper[c][:, cols, 3] if i < DIRECT else lane_rows[i][:, 1, :]
+            nc.vector.tensor_tensor(target, old_last[i], page_of(last)[:, t0:t1], ALU.add)
+            if (0, c) not in z_codes:
+                z_tiles(0, c, "piece%d" % c)
+                quantize_z(0, c, z_lower[c], slice(0, BANK))
+            if i >= DIRECT:
+                nc.vector.tensor_copy(out=z_upper[c][:, cols, 2:4], in_=lane_rows[i].rearrange("p e t -> p t e"))
+            quantize_z(1, c, z_upper[c], cols)
+        filled = 0
         for idx, (c, parts, dst) in enumerate(groups):
             acc = acc_banks[idx % len(acc_banks)]
-            if idx % N_TILES == 0:
-                result = stream.tile([P, N_TILES, BANK], F32, name="stream", tag="stream", align_bytes=64)
+            width = len(parts) * parts[0][2]
+            if filled % (N_TILES * BANK) == 0:
+                result = stream.tile([P, N_TILES * BANK], F32, name="stream", tag="stream", align_bytes=64)
             if idx >= EARLY_TILES:
                 second_product(acc, 0, c, parts)
             second_product(acc, 1, c, parts)
+            acc = acc[:, 0:width]
             staged = slot(idx % STAGING_SLOTS, [P, 2, BANK], F32)
-            magnitude = staged[:, 0, :]
+            magnitude = staged[:, 0, 0:width]
             if idx in VECTOR_ABS:
-                signed = staged[:, 1, :]
+                signed = staged[:, 1, 0:width]
                 nc.vector.tensor_copy(out=signed, in_=acc)
                 nc.vector.scalar_tensor_tensor(
                     out=magnitude, in0=signed, scalar=-1.0, in1=signed, op0=ALU.mult, op1=ALU.max
                 )
             else:
                 nc.scalar.activation(out=magnitude, in_=acc, func=ACT.Abs)
-            logs = result[:, idx % N_TILES, :]
+            start = filled % (N_TILES * BANK)
+            logs = result[:, start : start + width]
+            filled = filled + width
             if idx < len(groups) - 1:
                 nc.scalar.activation(out=logs, in_=magnitude, func=ACT.Ln, bias=one[:], scale=0.5)
                 nc.sync.dma_start(out=dst, in_=logs.rearrange("p (n t) -> p n t", n=dst.shape[1]))

@@ -32,10 +32,10 @@ EARLY_HALVES = {2: ((5, 0), (7, 0)), 3: ((6, 0),), 4: ((7, 1),)}
 EARLY_TILES = 3
 PIECES = ((384, 512), (256, 384), (0, 256), (512, 768), (768, 1024), (1024, 1536), (1536, 2048))
 DIRECT = 3
-HEIRS = {2: 3, 3: 4, 4: 5, 5: 6}
+HEIRS = {1: 3, 0: 4, 3: 5, 4: 6}
 PAGE_BUFFERS = (4, 3, 1)
-LAST_PIECE = P
-VECTOR_ABS = (11, 13, 14, 15, 16)
+LAST_PIECE = 2 * P
+VECTOR_ABS = (11, 12, 13, 15, 16)
 STAGING_SLOTS = 7
 
 
@@ -435,7 +435,7 @@ def tile_list_early_exit_refill_kernel(
             target = z_upper[c][:, cols, 3] if i < DIRECT else lane_rows[i][:, 1, :]
             nc.vector.tensor_tensor(target, old_last[i], page_of(last)[:, t0:t1], ALU.add)
             if (0, c) not in z_codes:
-                z_tiles(0, c, "piece%d" % c)
+                z_tiles(0, c, "piece%d" % (DIRECT - c))
                 quantize_z(0, c, z_lower[c], slice(0, BANK))
             if i >= DIRECT:
                 nc.vector.tensor_copy(out=z_upper[c][:, cols, 2:4], in_=lane_rows[i].rearrange("p e t -> p t e"))
@@ -452,22 +452,22 @@ def tile_list_early_exit_refill_kernel(
             acc = acc[:, 0:width]
             staged = slot(idx % STAGING_SLOTS, [P, 2, BANK], F32)
             magnitude = staged[:, 0, 0:width]
-            if idx in VECTOR_ABS:
-                signed = staged[:, 1, 0:width]
-                nc.vector.tensor_copy(out=signed, in_=acc)
-                nc.vector.scalar_tensor_tensor(
-                    out=magnitude, in0=signed, scalar=-1.0, in1=signed, op0=ALU.mult, op1=ALU.max
-                )
-            else:
-                nc.scalar.activation(out=magnitude, in_=acc, func=ACT.Abs)
             start = filled % (N_TILES * BANK)
             logs = result[:, start : start + width]
             filled = filled + width
             if idx < len(groups) - 1:
-                nc.scalar.activation(out=logs, in_=magnitude, func=ACT.Ln, bias=one[:], scale=0.5)
-                nc.sync.dma_start(out=dst, in_=logs.rearrange("p (n t) -> p n t", n=dst.shape[1]))
+                pieces = [(slice(0, width), nc.sync, dst)]
             else:
                 cut = BANK - LAST_PIECE
-                for cols, queue in ((slice(0, cut), nc.sync), (slice(cut, BANK), nc.scalar)):
-                    nc.scalar.activation(out=logs[:, cols], in_=magnitude[:, cols], func=ACT.Ln, bias=one[:], scale=0.5)
-                    queue.dma_start(out=dst[:, 0, cols], in_=logs[:, cols])
+                pieces = [(cols, queue, dst[:, :, cols]) for cols, queue in ((slice(0, cut), nc.sync), (slice(cut, BANK), nc.scalar))]
+            for cols, queue, place in pieces:
+                if idx in VECTOR_ABS:
+                    signed = staged[:, 1, cols]
+                    nc.vector.tensor_copy(out=signed, in_=acc[:, cols])
+                    nc.vector.scalar_tensor_tensor(
+                        out=magnitude[:, cols], in0=signed, scalar=-1.0, in1=signed, op0=ALU.mult, op1=ALU.max
+                    )
+                else:
+                    nc.scalar.activation(out=magnitude[:, cols], in_=acc[:, cols], func=ACT.Abs)
+                nc.scalar.activation(out=logs[:, cols], in_=magnitude[:, cols], func=ACT.Ln, bias=one[:], scale=0.5)
+                queue.dma_start(out=place, in_=logs[:, cols].rearrange("p (n t) -> p n t", n=place.shape[1]))

@@ -32,10 +32,11 @@ EARLY_HALVES = {2: ((5, 0), (7, 0)), 3: ((6, 0),), 4: ((7, 1),)}
 EARLY_TILES = 3
 PIECES = ((384, 512), (256, 384), (0, 256), (512, 768), (768, 1024), (1024, 1536), (1536, 2048))
 DIRECT = 3
-HEIRS = {1: 3, 0: 4, 3: 5, 4: 6}
+HEIRS = {1: 3, 0: 4, 3: 5}
+WORD_CHUNKS = (0, 3)
 PAGE_BUFFERS = (4, 3, 1)
 LAST_PIECE = 2 * P
-VECTOR_ABS = (11, 12, 13, 15, 16)
+VECTOR_ABS = (8, 9, 12, 13, 15, 17)
 STAGING_SLOTS = 7
 
 
@@ -260,12 +261,12 @@ def tile_list_early_exit_refill_kernel(
 
         z_turned = [keep.tile([P, 4, 2, P, 2], BF16, name="z_turned%d" % c, align_bytes=64) for c in range(CHUNKS)]
 
-        lane2_turned = keep.tile([P, CHUNKS - 1, 4, P], BF16, name="lane2_turned", align_bytes=64)
+        lane2_turned = keep.tile([P, 2, 4, P], BF16, name="lane2_turned", align_bytes=64)
 
         sum_banks = {}
 
         def chunk_order(s):
-            return range(CHUNKS - 1, -1, -1) if s == FIRST_LANE_SLICE else range(CHUNKS)
+            return (1, 2, 0, 3) if s == FIRST_LANE_SLICE else range(CHUNKS)
 
         def add_turned(s, src, first, closes):
             if first:
@@ -294,22 +295,22 @@ def tile_list_early_exit_refill_kernel(
                     nc.scalar.copy(
                         out=z_turned[c][:, :, 0, m0 : m0 + 64, :].rearrange("t b m e -> t b (m e)"), in_=sums[c]
                     )
-                elif c > 0:
+                elif c not in WORD_CHUNKS:
                     nc.scalar.copy(out=lane2_turned[:, c - 1], in_=sums[c])
                 else:
                     nc.scalar.copy(out=z_turned[c][:, :, 1, :, 0], in_=sums[c])
 
         def turn_back(c, grouped, halves_and_banks):
             src = z_turned[c][:].rearrange("t b u p e -> t (b u p e)").bitcast(F32)
-            dst = grouped.rearrange("p t i -> p (t i)").bitcast(F32)
             for hb, bank in halves_and_banks:
+                dst = grouped[:, hb].rearrange("p t i -> p (t i)").bitcast(F32)
                 pairs = bank.rearrange("p (b u t) -> p b u t", b=2, u=2)
                 for b in range(2):
                     for u in range(2):
                         w0 = P * (2 * (2 * hb + b) + u)
                         nc.tensor.transpose(pairs[:, b, u, :], src[:, w0 : w0 + P], ident[:])
                 nc.scalar.copy(
-                    out=dst[:, BANK * hb : BANK * (hb + 1)].rearrange("p (b t u) -> p b t u", b=2, u=2),
+                    out=dst.rearrange("p (b t u) -> p b t u", b=2, u=2),
                     in_=pairs[:].rearrange("p b u t -> p b t u"),
                 )
 
@@ -317,11 +318,16 @@ def tile_list_early_exit_refill_kernel(
         z_planes = {}
 
         def quantize_z(a, c, grouped, cols):
-            nc.vector.quantize_mx(
-                out=z_codes[a, c][:, cols].bitcast(FP8X4),
-                scales=z_planes[a, c][:, cols],
-                in_=grouped[:, cols, :].rearrange("p t i -> p (t i)"),
-            )
+            half = BANK // 2
+            if cols.stop - cols.start <= half:
+                h = cols.start // half
+                runs = [(cols, grouped[:, h, cols.start - half * h : cols.stop - half * h, :].rearrange("p t i -> p (t i)"))]
+            elif a == 0:
+                runs = [(cols, grouped.rearrange("p h t i -> p (h t i)"))]
+            else:
+                runs = [(slice(half * h, half * (h + 1)), grouped[:, h].rearrange("p t i -> p (t i)")) for h in range(2)]
+            for part, values in runs:
+                nc.vector.quantize_mx(out=z_codes[a, c][:, part].bitcast(FP8X4), scales=z_planes[a, c][:, part], in_=values)
 
         def z_tiles(a, c, tag):
             z_codes[a, c] = keep.tile([P, BANK], U32, name="z_codes", tag=tag, align_bytes=64)
@@ -339,15 +345,17 @@ def tile_list_early_exit_refill_kernel(
                     stop=(a == PASSES - 1 and i == len(parts) - 1),
                 )
 
-        z_upper = [keep.tile([P, BANK, 4], BF16, name="z_upper%d" % c, align_bytes=64)[:] for c in range(CHUNKS)]
+        z_upper = [keep.tile([P, 2, BANK // 2, 4], BF16, name="z_upper%d" % c, align_bytes=64)[:] for c in range(2)]
+        woven = keep.tile([P, 2, 2, BANK // 2, 4], BF16, name="z_upper_woven", align_bytes=64)
+        z_upper = z_upper + [woven[:, :, 0], woven[:, :, 1]]
 
         def turn_back_pair(c):
             src = z_turned[c][:].rearrange("t b u p e -> t (b u p e)").bitcast(F32)
-            dst = z_upper[c].rearrange("p t i -> p (t i)").bitcast(F32).rearrange("p (t u) -> p t u", u=2)
+            dst = z_upper[c].rearrange("p h t i -> p h (t i)").bitcast(F32).rearrange("p h (t u) -> p h t u", u=2)
             pairs = next_bank()
             for b in range(4):
                 nc.tensor.transpose(pairs[:, P * b : P * (b + 1)], src[:, 2 * P * b : 2 * P * b + P], ident[:])
-            nc.scalar.copy(out=dst[:, :, 0], in_=pairs)
+            nc.scalar.copy(out=dst[:, :, :, 0], in_=pairs.rearrange("p (h t) -> p h t", h=2))
 
         def turn_back_lane2(c):
             back = sum_banks[FIRST_LANE_SLICE][c].bitcast(BF16)[:, 0:BANK]
@@ -396,25 +404,26 @@ def tile_list_early_exit_refill_kernel(
             if s == AS_THEY_LIE - 1:
                 for c in range(CHUNKS):
                     if c % 2 == 0:
-                        two_chunks = big(c, [P, 2, BANK, 4], BF16)
-                    z_lower[c] = two_chunks[:, c % 2, :, :]
+                        two_chunks = big(c, [P, 2, 2, BANK // 2, 4], BF16)
+                    z_lower[c] = two_chunks[:, c % 2]
                     turn_back(c, z_lower[c], [(hb, next_bank()) for hb in range(2)])
                     if c == 0:
                         z_tiles(0, 0, "codes0_0")
                         quantize_z(0, 0, z_lower[0], slice(BANK // 2, BANK))
             if s == FIRST_LANE_SLICE - 1:
-                for c in range(1, CHUNKS):
+                for c in (1, 2):
                     turn_back_pair(c)
             if s == FIRST_LANE_SLICE:
                 acc_banks = [next_bank() for c in range(CHUNKS)]
-                for c in range(CHUNKS - 1, 0, -1):
+                for c in (1, 2):
                     turn_back_lane2(c)
-                turn_back(0, z_upper[0], [(1, sum_banks[s][3]), (0, sum_banks[s][2])])
+                turn_back(0, z_upper[0], [(1, sum_banks[s][0]), (0, acc_banks[3])])
+                turn_back(3, z_upper[3], [(0, sum_banks[s][3]), (1, sum_banks[s][1])])
             if s + 1 < last:
                 add_turned(s + 1, olds[s + 1], True, False)
 
         freed = sum_banks[FIRST_LANE_SLICE]
-        acc_banks = acc_banks[0:3] + [freed[3], freed[2], acc_banks[3], freed[1], freed[0]]
+        acc_banks = acc_banks[0:3] + [freed[3], freed[1], acc_banks[3], freed[0], freed[2]]
         out_rows = out.rearrange("(n p) t -> p n t", p=P)
         groups = []
         for i, (t0, t1) in enumerate(PIECES):
@@ -423,6 +432,9 @@ def tile_list_early_exit_refill_kernel(
             for n0 in range(0, N_TILES, count):
                 parts = [(n, t0 % BANK, width) for n in range(n0, n0 + count)]
                 groups.append((c, parts, out_rows[:, n0 : n0 + count, t0:t1]))
+        c, [(n, t0, width)], dst = groups.pop()
+        for cols in (slice(0, width - LAST_PIECE), slice(width - LAST_PIECE, width)):
+            groups.append((c, [(n, cols.start, cols.stop - cols.start)], dst[:, :, cols]))
         for idx in range(EARLY_TILES):
             second_product(acc_banks[idx], 0, *groups[idx][:2])
         z_codes[0, 0] = big(PAGE_BUFFERS[2 * (last - 1) % PAGES], [P, BANK // 2], U32)
@@ -432,14 +444,32 @@ def tile_list_early_exit_refill_kernel(
             cols = slice(t0 % BANK, t0 % BANK + t1 - t0)
             if (1, c) not in z_codes:
                 z_tiles(1, c, "codes1_%d" % c)
-            target = z_upper[c][:, cols, 3] if i < DIRECT else lane_rows[i][:, 1, :]
-            nc.vector.tensor_tensor(target, old_last[i], page_of(last)[:, t0:t1], ALU.add)
+            count = max(1, (t1 - t0) // (BANK // 2))
+            h0, c0 = divmod(t0 % BANK, BANK // 2)
+            grouped = z_upper[c][:, h0 : h0 + count, c0 : c0 + (t1 - t0) // count, :]
+            old_part = old_last[i].rearrange("p (h t) -> p h t", h=count)
+            page_part = page_of(last)[:, t0:t1].rearrange("p (h t) -> p h t", h=count)
+            if c == CHUNKS - 1:
+                nc.gpsimd.tensor_tensor(grouped[:, :, :, 3], old_part, page_part, ALU.add)
+                continue
+            if c in WORD_CHUNKS:
+                nc.vector.tensor_tensor(grouped[:, :, :, 3], old_part, page_part, ALU.add)
+            else:
+                nc.vector.tensor_tensor(lane_rows[i][:, 1, :], old_last[i], page_of(last)[:, t0:t1], ALU.add)
             if (0, c) not in z_codes:
                 z_tiles(0, c, "piece%d" % (DIRECT - c))
                 quantize_z(0, c, z_lower[c], slice(0, BANK))
-            if i >= DIRECT:
-                nc.vector.tensor_copy(out=z_upper[c][:, cols, 2:4], in_=lane_rows[i].rearrange("p e t -> p t e"))
+            if c not in WORD_CHUNKS:
+                nc.vector.tensor_copy(out=grouped[:, :, :, 2:4], in_=lane_rows[i].rearrange("p e (h t) -> p h t e", h=count))
+            if c == CHUNKS - 2:
+                z_tiles(0, c + 1, "piece0")
+                quantize_z(0, c + 1, z_lower[c + 1], slice(0, BANK))
             quantize_z(1, c, z_upper[c], cols)
+        def finish(logs, magnitude, dst, queue):
+            nc.scalar.activation(out=logs, in_=magnitude, func=ACT.Ln, bias=one[:], scale=0.5)
+            queue.dma_start(out=dst, in_=logs.rearrange("p (n t) -> p n t", n=dst.shape[1]))
+
+        waiting = []
         filled = 0
         for idx, (c, parts, dst) in enumerate(groups):
             acc = acc_banks[idx % len(acc_banks)]
@@ -455,19 +485,18 @@ def tile_list_early_exit_refill_kernel(
             start = filled % (N_TILES * BANK)
             logs = result[:, start : start + width]
             filled = filled + width
-            if idx < len(groups) - 1:
-                pieces = [(slice(0, width), nc.sync, dst)]
+            if idx in VECTOR_ABS:
+                negated = staged[:, 1, 0:width]
+                nc.vector.tensor_scalar(out=negated, in0=acc, scalar1=-1.0, scalar2=None, op0=ALU.mult)
+                nc.vector.tensor_tensor(magnitude, acc, negated, ALU.max)
+                waiting.append((logs, magnitude, dst))
             else:
-                cut = BANK - LAST_PIECE
-                pieces = [(cols, queue, dst[:, :, cols]) for cols, queue in ((slice(0, cut), nc.sync), (slice(cut, BANK), nc.scalar))]
-            for cols, queue, place in pieces:
-                if idx in VECTOR_ABS:
-                    signed = staged[:, 1, cols]
-                    nc.vector.tensor_copy(out=signed, in_=acc[:, cols])
-                    nc.vector.scalar_tensor_tensor(
-                        out=magnitude[:, cols], in0=signed, scalar=-1.0, in1=signed, op0=ALU.mult, op1=ALU.max
-                    )
-                else:
-                    nc.scalar.activation(out=magnitude[:, cols], in_=acc[:, cols], func=ACT.Abs)
-                nc.scalar.activation(out=logs[:, cols], in_=magnitude[:, cols], func=ACT.Ln, bias=one[:], scale=0.5)
-                queue.dma_start(out=place, in_=logs[:, cols].rearrange("p (n t) -> p n t", n=place.shape[1]))
+                nc.scalar.activation(out=magnitude, in_=acc, func=ACT.Abs)
+                waiting.insert(1, (logs, magnitude, dst))
+                count = 2 if c < CHUNKS - 1 else len(waiting)
+                for entry in waiting[:count]:
+                    finish(*entry, nc.sync)
+                waiting = waiting[count:]
+            if idx == VECTOR_ABS[1]:
+                quantize_z(1, CHUNKS - 1, z_upper[CHUNKS - 1], slice(0, BANK))
+        finish(*waiting[0], nc.scalar)

@@ -36,7 +36,7 @@ HEIRS = {1: 3, 0: 4, 3: 5}
 WORD_CHUNKS = (0, 3)
 PAGE_BUFFERS = (4, 3, 1)
 LAST_PIECE = 2 * P
-VECTOR_ABS = (8, 9, 12, 13, 15, 17)
+VECTOR_ABS = (8, 9, 12, 13, 15, 16)
 STAGING_SLOTS = 7
 
 
@@ -439,37 +439,50 @@ def tile_list_early_exit_refill_kernel(
             second_product(acc_banks[idx], 0, *groups[idx][:2])
         z_codes[0, 0] = big(PAGE_BUFFERS[2 * (last - 1) % PAGES], [P, BANK // 2], U32)
         quantize_z(0, 0, z_lower[0], slice(0, BANK // 2))
-        for i, (t0, t1) in enumerate(PIECES):
-            c = t0 // BANK
-            cols = slice(t0 % BANK, t0 % BANK + t1 - t0)
-            if (1, c) not in z_codes:
-                z_tiles(1, c, "codes1_%d" % c)
+
+        def grouped_piece(i):
+            t0, t1 = PIECES[i]
             count = max(1, (t1 - t0) // (BANK // 2))
             h0, c0 = divmod(t0 % BANK, BANK // 2)
-            grouped = z_upper[c][:, h0 : h0 + count, c0 : c0 + (t1 - t0) // count, :]
-            old_part = old_last[i].rearrange("p (h t) -> p h t", h=count)
-            page_part = page_of(last)[:, t0:t1].rearrange("p (h t) -> p h t", h=count)
-            if c == CHUNKS - 1:
-                nc.gpsimd.tensor_tensor(grouped[:, :, :, 3], old_part, page_part, ALU.add)
-                continue
-            if c in WORD_CHUNKS:
-                nc.vector.tensor_tensor(grouped[:, :, :, 3], old_part, page_part, ALU.add)
+            return z_upper[t0 // BANK][:, h0 : h0 + count, c0 : c0 + (t1 - t0) // count, :]
+
+        def add_piece(i, engine):
+            t0, t1 = PIECES[i]
+            if i in lane_rows:
+                engine.tensor_tensor(lane_rows[i][:, 1, :], old_last[i], page_of(last)[:, t0:t1], ALU.add)
             else:
-                nc.vector.tensor_tensor(lane_rows[i][:, 1, :], old_last[i], page_of(last)[:, t0:t1], ALU.add)
+                lane3 = grouped_piece(i)[:, :, :, 3]
+                old_part = old_last[i].rearrange("p (h t) -> p h t", h=lane3.shape[1])
+                page_part = page_of(last)[:, t0:t1].rearrange("p (h t) -> p h t", h=lane3.shape[1])
+                engine.tensor_tensor(lane3, old_part, page_part, ALU.add)
+
+        def quantize_late(c):
+            z_tiles(0, c, "piece%d" % (DIRECT - c))
+            quantize_z(0, c, z_lower[c], slice(0, BANK))
+
+        for c in range(CHUNKS):
+            z_tiles(1, c, "codes1_%d" % c)
+        add_piece(0, nc.vector)
+        for i, (t0, t1) in enumerate(PIECES[:-1]):
+            c = t0 // BANK
             if (0, c) not in z_codes:
-                z_tiles(0, c, "piece%d" % (DIRECT - c))
-                quantize_z(0, c, z_lower[c], slice(0, BANK))
-            if c not in WORD_CHUNKS:
-                nc.vector.tensor_copy(out=grouped[:, :, :, 2:4], in_=lane_rows[i].rearrange("p e (h t) -> p h t e", h=count))
-            if c == CHUNKS - 2:
-                z_tiles(0, c + 1, "piece0")
-                quantize_z(0, c + 1, z_lower[c + 1], slice(0, BANK))
-            quantize_z(1, c, z_upper[c], cols)
+                quantize_late(c)
+            if i in lane_rows:
+                lanes = grouped_piece(i)[:, :, :, 2:4]
+                nc.vector.tensor_copy(out=lanes, in_=lane_rows[i].rearrange("p e (h t) -> p h t e", h=lanes.shape[1]))
+            if i + 2 < len(PIECES):
+                add_piece(i + 1, nc.vector)
+            else:
+                quantize_late(c + 1)
+            quantize_z(1, c, z_upper[c], slice(t0 % BANK, t0 % BANK + t1 - t0))
+        add_piece(len(PIECES) - 1, nc.gpsimd)
+
         def finish(logs, magnitude, dst, queue):
             nc.scalar.activation(out=logs, in_=magnitude, func=ACT.Ln, bias=one[:], scale=0.5)
             queue.dma_start(out=dst, in_=logs.rearrange("p (n t) -> p n t", n=dst.shape[1]))
 
         waiting = []
+        pair = []
         filled = 0
         for idx, (c, parts, dst) in enumerate(groups):
             acc = acc_banks[idx % len(acc_banks)]
@@ -488,15 +501,18 @@ def tile_list_early_exit_refill_kernel(
             if idx in VECTOR_ABS:
                 negated = staged[:, 1, 0:width]
                 nc.vector.tensor_scalar(out=negated, in0=acc, scalar1=-1.0, scalar2=None, op0=ALU.mult)
-                nc.vector.tensor_tensor(magnitude, acc, negated, ALU.max)
+                pair.append((magnitude, acc, negated))
                 waiting.append((logs, magnitude, dst))
+                if len(pair) == 2:
+                    for operands in pair:
+                        nc.vector.tensor_tensor(*operands, ALU.max)
+                    pair = []
             else:
                 nc.scalar.activation(out=magnitude, in_=acc, func=ACT.Abs)
                 waiting.insert(1, (logs, magnitude, dst))
                 count = 2 if c < CHUNKS - 1 else len(waiting)
                 for entry in waiting[:count]:
-                    finish(*entry, nc.sync)
+                    finish(*entry, nc.scalar if idx == len(groups) - 1 and entry is waiting[-1] else nc.sync)
                 waiting = waiting[count:]
             if idx == VECTOR_ABS[1]:
                 quantize_z(1, CHUNKS - 1, z_upper[CHUNKS - 1], slice(0, BANK))
-        finish(*waiting[0], nc.scalar)

@@ -507,12 +507,17 @@ def tile_list_early_exit_refill_kernel(
                     for operands in pair:
                         nc.vector.tensor_tensor(*operands, ALU.max)
                     pair = []
-            else:
+            elif idx < len(groups) - 1:
                 nc.scalar.activation(out=magnitude, in_=acc, func=ACT.Abs)
                 waiting.insert(1, (logs, magnitude, dst))
                 count = 2 if c < CHUNKS - 1 else len(waiting)
                 for entry in waiting[:count]:
-                    finish(*entry, nc.scalar if idx == len(groups) - 1 and entry is waiting[-1] else nc.sync)
+                    finish(*entry, nc.sync)
                 waiting = waiting[count:]
+            else:
+                finish(*waiting[0], nc.sync)
+                nc.scalar.activation(out=magnitude, in_=acc, func=ACT.Abs)
+                finish(*waiting[1], nc.sync)
+                finish(logs, magnitude, dst, nc.scalar)
             if idx == VECTOR_ABS[1]:
                 quantize_z(1, CHUNKS - 1, z_upper[CHUNKS - 1], slice(0, BANK))

@@ -29,7 +29,6 @@ PAGES = 3
 STREAM_BUFS = 5
 OLD_AHEAD = 3
 EARLY_HALVES = {2: ((5, 0), (7, 0)), 3: ((6, 0),), 4: ((7, 1),)}
-EARLY_TILES = 3
 PIECES = ((384, 512), (256, 384), (0, 256), (512, 768), (768, 1024), (1024, 1536), (1536, 2048))
 DIRECT = 3
 HEIRS = {1: 3, 0: 4, 3: 5}
@@ -259,7 +258,7 @@ def tile_list_early_exit_refill_kernel(
             else:
                 nc.vector.tensor_tensor(page[:].indirect(offsets2[:]), h_tiles[s], weights, ALU.mult)
 
-        z_turned = [keep.tile([P, 4, 2, P, 2], BF16, name="z_turned%d" % c, align_bytes=64) for c in range(CHUNKS)]
+        z_turned = [keep.tile([P, 4, 2, P, 2], BF16, name="z_turned", tag="z_turned%d" % c, align_bytes=64) for c in range(CHUNKS)]
 
         lane2_turned = keep.tile([P, 2, 4, P], BF16, name="lane2_turned", align_bytes=64)
 
@@ -407,9 +406,6 @@ def tile_list_early_exit_refill_kernel(
                         two_chunks = big(c, [P, 2, 2, BANK // 2, 4], BF16)
                     z_lower[c] = two_chunks[:, c % 2]
                     turn_back(c, z_lower[c], [(hb, next_bank()) for hb in range(2)])
-                    if c == 0:
-                        z_tiles(0, 0, "codes0_0")
-                        quantize_z(0, 0, z_lower[0], slice(BANK // 2, BANK))
             if s == FIRST_LANE_SLICE - 1:
                 for c in (1, 2):
                     turn_back_pair(c)
@@ -423,7 +419,7 @@ def tile_list_early_exit_refill_kernel(
                 add_turned(s + 1, olds[s + 1], True, False)
 
         freed = sum_banks[FIRST_LANE_SLICE]
-        acc_banks = acc_banks[0:3] + [freed[3], freed[1], acc_banks[3], freed[0], freed[2]]
+        acc_banks = [freed[2], freed[0], acc_banks[3], freed[3], freed[1]] + acc_banks[0:3]
         out_rows = out.rearrange("(n p) t -> p n t", p=P)
         groups = []
         for i, (t0, t1) in enumerate(PIECES):
@@ -435,10 +431,9 @@ def tile_list_early_exit_refill_kernel(
         c, [(n, t0, width)], dst = groups.pop()
         for cols in (slice(0, width - LAST_PIECE), slice(width - LAST_PIECE, width)):
             groups.append((c, [(n, cols.start, cols.stop - cols.start)], dst[:, :, cols]))
-        for idx in range(EARLY_TILES):
-            second_product(acc_banks[idx], 0, *groups[idx][:2])
-        z_codes[0, 0] = big(PAGE_BUFFERS[2 * (last - 1) % PAGES], [P, BANK // 2], U32)
-        quantize_z(0, 0, z_lower[0], slice(0, BANK // 2))
+        z_tiles(0, 0, "big%d" % PAGE_BUFFERS[2 * (last - 1) % PAGES])
+        for cols in (slice(BANK // 2, BANK), slice(0, BANK // 2)):
+            quantize_z(0, 0, z_lower[0], cols)
 
         def grouped_piece(i):
             t0, t1 = PIECES[i]
@@ -489,9 +484,8 @@ def tile_list_early_exit_refill_kernel(
             width = len(parts) * parts[0][2]
             if filled % (N_TILES * BANK) == 0:
                 result = stream.tile([P, N_TILES * BANK], F32, name="stream", tag="stream", align_bytes=64)
-            if idx >= EARLY_TILES:
-                second_product(acc, 0, c, parts)
-            second_product(acc, 1, c, parts)
+            for a in range(PASSES):
+                second_product(acc, a, c, parts)
             acc = acc[:, 0:width]
             staged = slot(idx % STAGING_SLOTS, [P, 2, BANK], F32)
             magnitude = staged[:, 0, 0:width]

@@ -62,10 +62,13 @@ def tile_list_early_exit_refill_kernel(
         def big(index, shape, dtype):
             return keep.tile(shape, dtype, name="big%d" % index, tag="big%d" % index, align_bytes=64)
 
-        tab_planes = keep.tile([P, T], U8, name="tab_planes", align_bytes=64)
-        nc.vector.memset(tab_planes[:].bitcast(I32), 0)
+        tab_rows = keep.tile([P, T], U8, name="tab_rows", align_bytes=64)
         one = keep.tile([P, 1], F32, name="one")
         nc.gpsimd.memset(one[:], 1.0)
+        for rows in (slice(32, 64), slice(64, P)):
+            nc.gpsimd.memset(tab_rows[rows, :].bitcast(I32), 0)
+        v_planes = keep.tile([P, S], U8, name="v_planes", align_bytes=64)
+        nc.gpsimd.memset(v_planes[:].bitcast(I32), 0)
         zero = keep.tile([P, 1], F32, name="zero")
         nc.scalar.activation(out=zero[:], in_=one[:], func=ACT.Ln)
         ident = keep.tile([P, P], F32, name="ident")
@@ -73,7 +76,6 @@ def tile_list_early_exit_refill_kernel(
         ident_bf16 = keep.tile([P, P], BF16, name="ident_bf16")
         nc.scalar.copy(out=ident_bf16[:], in_=ident[:])
         w2_planes = keep.tile([P, PASSES, N], U8, name="w2_planes", align_bytes=64)
-        nc.vector.memset(w2_planes[:].rearrange("p a n -> p (a n)").bitcast(I32), 0)
 
         tabs = [big(a, [P, T], I32) for a in range(PASSES)]
 
@@ -127,16 +129,14 @@ def tile_list_early_exit_refill_kernel(
 
         pages = [big(index, [P, T2], F32) for index in PAGE_BUFFERS[:2]]
         for page in pages:
-            nc.vector.memset(page[:].bitcast(I32), 0)
+            nc.gpsimd.memset(page[:].bitcast(I32), 0)
+        nc.gpsimd.memset(w2_planes[:].rearrange("p a n -> p (a n)").bitcast(I32), 0)
         offsets = keep.tile([P, S // 16], U16, name="offsets")
         nc.sync.dma_start(offsets[:], offs)
+        nc.sync.dma_start(
+            out=tab_rows[0:32, :].bitcast(I32), in_=tab_scales.rearrange("a q t -> (a q) t").bitcast(I32)
+        )
         load_tab(0)
-        for q in range(4):
-            for passes in ([slice(0, 2)] if q % 2 == 0 else [slice(0, 1), slice(1, 2)]):
-                rows_of = slice(32 * q + 4 * passes.start, 32 * q + 4 * passes.stop)
-                nc.sync.dma_start(
-                    out=tab_planes[rows_of, :].bitcast(I32), in_=tab_scales[passes, 4 * q : 4 * q + 4, :].bitcast(I32)
-                )
         load_w1_lower(0, 6)
         load_tab(1)
         offsets2 = keep.tile([P, S // 16], U16, name="offsets2")
@@ -168,12 +168,21 @@ def tile_list_early_exit_refill_kernel(
                 in_=w2_scales[:, 4 * q : 4 * q + 4, :].rearrange("a r n -> r a n").bitcast(I32),
             )
 
-        v_planes = keep.tile([P, S], U8, name="v_planes", align_bytes=64)
-        v_words = [keep.tile([P, S], U32, name="v_words%d" % a, align_bytes=64) for a in range(PASSES)]
+        v_rows = keep.tile([P, S], U8, name="v_rows", align_bytes=64)
+        v_words = [keep.tile([P, S], U32, name="v_words0", align_bytes=64)]
         halves = [(0, BANK), (BANK, S)]
         first_pieces = [(0, BANK // 2), (BANK // 2, BANK), (BANK, S)]
+        nc.vector.tensor_copy(v_rows[:], tab_rows[:].indirect(offsets[:]))
+        for a in range(PASSES):
+            for q in range(4):
+                src = 16 * a + 4 * q
+                dst = 32 * q + 4 * a
+                if src != dst:
+                    nc.scalar.dma_start(
+                        out=v_planes[dst : dst + 4, :].bitcast(I32), in_=v_rows[src : src + 4, :].bitcast(I32)
+                    )
         nc.vector.tensor_copy(v_words[0][:], tabs[0][:].bitcast(U32).indirect(offsets[:]))
-        nc.vector.tensor_copy(v_planes[:], tab_planes[:].indirect(offsets[:]))
+        nc.vector.tensor_copy(v_planes[0:4, :].bitcast(I32), v_rows[0:4, :].bitcast(I32))
 
         w1_codes = {}
         w1_planes = {}
@@ -200,6 +209,21 @@ def tile_list_early_exit_refill_kernel(
                     in_=w1_raw[s][:, a, :, :].rearrange("p j (c i) -> p c j i", i=4),
                 )
             quantize_w1(s, grouped[:])
+
+        def prepare_w1_first():
+            for a, tag in enumerate(("w1_first", "v_words1")):
+                grouped = keep.tile([P, P, 4], BF16, name="w1_first", tag=tag, align_bytes=64)
+                nc.scalar.copy(
+                    out=grouped[:].rearrange("p (c i) j -> p c j i", i=4),
+                    in_=w1_raw[0][:, a, :, :].rearrange("p j (c i) -> p c j i", i=4),
+                )
+                codes = keep.tile([P, P], U32, name="w1_codes_first%d" % a, align_bytes=64)
+                planes = keep.tile([P, P], U8, name="w1_planes_first%d" % a, align_bytes=64)
+                nc.vector.quantize_mx(
+                    out=codes[:].bitcast(FP8X4), scales=planes[:], in_=grouped[:].rearrange("p c j -> p (c j)")
+                )
+                w1_codes[0, a] = codes[:]
+                w1_planes[0, a] = planes[:]
 
         lanes_grouped = keep.tile([P, 2, PASSES, P, 4], BF16, name="lanes_grouped", align_bytes=64)
 
@@ -364,7 +388,8 @@ def tile_list_early_exit_refill_kernel(
                 if t0 // BANK == c:
                     nc.scalar.copy(out=lane_rows[i][:, 0, :], in_=back[:, t0 % BANK : t0 % BANK + t1 - t0])
 
-        prepare_w1_lower(0)
+        prepare_w1_first()
+        v_words.append(keep.tile([P, S], U32, name="v_words1", tag="v_words1", align_bytes=64))
         for j0, j1 in first_pieces:
             nc.vector.tensor_copy(v_words[1][:, j0:j1], tabs[1][:].bitcast(U32).indirect(offsets[:, j0 // 16 : j1 // 16]))
         pages.append(big(PAGE_BUFFERS[2], [P, T2], F32))

@@ -66,16 +66,15 @@ def tile_list_early_exit_refill_kernel(
         one = keep.tile([P, 1], F32, name="one")
         nc.gpsimd.memset(one[:], 1.0)
         for rows in (slice(32, 64), slice(64, P)):
-            nc.gpsimd.memset(tab_rows[rows, :].bitcast(I32), 0)
+            nc.vector.memset(tab_rows[rows, :].bitcast(I32), 0)
         v_planes = keep.tile([P, S], U8, name="v_planes", align_bytes=64)
-        nc.gpsimd.memset(v_planes[:].bitcast(I32), 0)
+        nc.vector.memset(v_planes[:].bitcast(I32), 0)
         zero = keep.tile([P, 1], F32, name="zero")
         nc.scalar.activation(out=zero[:], in_=one[:], func=ACT.Ln)
         ident = keep.tile([P, P], F32, name="ident")
         make_identity(nc, ident[:])
         ident_bf16 = keep.tile([P, P], BF16, name="ident_bf16")
         nc.scalar.copy(out=ident_bf16[:], in_=ident[:])
-        w2_planes = keep.tile([P, PASSES, N], U8, name="w2_planes", align_bytes=64)
 
         tabs = [big(a, [P, T], I32) for a in range(PASSES)]
 
@@ -127,10 +126,8 @@ def tile_list_early_exit_refill_kernel(
                 if heir is not None:
                     lane_rows[heir] = tile[:, 0 : 2 * extra].bitcast(BF16).rearrange("p (e t) -> p e t", e=2)
 
-        pages = [big(index, [P, T2], F32) for index in PAGE_BUFFERS[:2]]
-        for page in pages:
-            nc.gpsimd.memset(page[:].bitcast(I32), 0)
-        nc.gpsimd.memset(w2_planes[:].rearrange("p a n -> p (a n)").bitcast(I32), 0)
+        pages = {0: big(PAGE_BUFFERS[0], [P, T2], F32)}
+        nc.vector.memset(pages[0][:].bitcast(I32), 0)
         offsets = keep.tile([P, S // 16], U16, name="offsets")
         nc.sync.dma_start(offsets[:], offs)
         nc.sync.dma_start(
@@ -162,11 +159,6 @@ def tile_list_early_exit_refill_kernel(
             nc.sync.dma_start(out=wgs_lanes[32 * g : 32 * (g + 1), :, :], in_=wgs_by_lane[:, 2:4, :])
         w2_codes = keep.tile([P, PASSES, 2 * N], U8, name="w2_codes", align_bytes=64)
         nc.sync.dma_start(out=w2_codes[:].bitcast(I32), in_=w2_words.rearrange("a p c -> p a c").bitcast(I32))
-        for q in range(4):
-            nc.sync.dma_start(
-                out=w2_planes[32 * q : 32 * q + 4, :, :].bitcast(I32),
-                in_=w2_scales[:, 4 * q : 4 * q + 4, :].rearrange("a r n -> r a n").bitcast(I32),
-            )
 
         v_rows = keep.tile([P, S], U8, name="v_rows", align_bytes=64)
         v_words = [keep.tile([P, S], U32, name="v_words0", align_bytes=64)]
@@ -202,7 +194,11 @@ def tile_list_early_exit_refill_kernel(
                     w1_planes[first + i, a] = planes[:, i, a, :]
 
         def prepare_w1_lower(s):
-            grouped = ring.tile([P, 1, PASSES, P, 4], BF16, name="w1_grouped", tag="w1_grouped", align_bytes=64)
+            if s < 3:
+                tag = ("w1_second", "big%d" % PAGE_BUFFERS[1])[s - 1]
+                grouped = keep.tile([P, 1, PASSES, P, 4], BF16, name="w1_grouped", tag=tag, align_bytes=64)
+            else:
+                grouped = ring.tile([P, 1, PASSES, P, 4], BF16, name="w1_grouped", tag="w1_grouped", align_bytes=64)
             for a in range(PASSES):
                 nc.scalar.copy(
                     out=grouped[:, 0, a, :, :].rearrange("p (c i) j -> p c j i", i=4),
@@ -276,9 +272,9 @@ def tile_list_early_exit_refill_kernel(
             else:
                 weights = wgs_lanes[:, s - FIRST_LANE_SLICE, :]
             if s == 0:
-                for (j0, j1), target in zip(first_pieces, (page, pages[1], page)):
-                    places = target[:].indirect(offsets2[:, j0 // 16 : j1 // 16])
-                    nc.vector.tensor_tensor(places, h_pieces[s, (j0, j1)], weights[:, j0:j1], ALU.mult)
+                for (j0, j1), h in zip(halves, (h_first[:], h_tiles[0][:, BANK:S])):
+                    places = page[:].indirect(offsets2[:, j0 // 16 : j1 // 16])
+                    nc.vector.tensor_tensor(places, h, weights[:, j0:j1], ALU.mult)
             else:
                 nc.vector.tensor_tensor(page[:].indirect(offsets2[:]), h_tiles[s], weights, ALU.mult)
 
@@ -303,8 +299,6 @@ def tile_list_early_exit_refill_kernel(
                     )
 
         def sum_turned(s):
-            if s == 0:
-                add_turned(s, pages[1], False, False)
             add_turned(s, page_of(s), False, True)
             sums = [bank.rearrange("t (b r) -> t b r", b=4) for bank in sum_banks[s]]
             for c in chunk_order(s):
@@ -392,12 +386,21 @@ def tile_list_early_exit_refill_kernel(
         v_words.append(keep.tile([P, S], U32, name="v_words1", tag="v_words1", align_bytes=64))
         for j0, j1 in first_pieces:
             nc.vector.tensor_copy(v_words[1][:, j0:j1], tabs[1][:].bitcast(U32).indirect(offsets[:, j0 // 16 : j1 // 16]))
-        pages.append(big(PAGE_BUFFERS[2], [P, T2], F32))
-        nc.gpsimd.memset(pages[-1][:].bitcast(I32), 0)
+        pages[2] = big(PAGE_BUFFERS[2], [P, T2], F32)
+        nc.gpsimd.memset(pages[2][:].bitcast(I32), 0)
         prepare_w1_lower(1)
+        w2_planes = keep.tile([P, PASSES, N], U8, name="w2_planes", tag="w1_second", align_bytes=64)
+        nc.gpsimd.memset(w2_planes[:].rearrange("p a n -> p (a n)").bitcast(I32), 0)
+        for q in range(4):
+            nc.sync.dma_start(
+                out=w2_planes[32 * q : 32 * q + 4, :, :].bitcast(I32),
+                in_=w2_scales[:, 4 * q : 4 * q + 4, :].rearrange("a r n -> r a n").bitcast(I32),
+            )
         for piece in first_pieces:
             first_product(0, piece)
         prepare_w1_lower(2)
+        pages[1] = big(PAGE_BUFFERS[1], [P, T2], F32)
+        nc.gpsimd.memset(pages[1][:].bitcast(I32), 0)
         for piece in halves:
             first_product(1, piece)
         add_turned(0, olds[0], True, False)

@@ -36,6 +36,7 @@ WORD_CHUNKS = (0, 3)
 PAGE_BUFFERS = (4, 3, 1)
 LAST_PIECE = 2 * P
 VECTOR_ABS = (8, 9, 12, 13, 15, 16)
+FIRST_PASSES = {0: (0, 1, 2), 2: (3, 4), 5: (5, 6, 7, 8), 9: (9, 10, 11, 12), 13: (13, 14, 15, 16, 17)}
 STAGING_SLOTS = 7
 
 
@@ -447,7 +448,7 @@ def tile_list_early_exit_refill_kernel(
                 add_turned(s + 1, olds[s + 1], True, False)
 
         freed = sum_banks[FIRST_LANE_SLICE]
-        acc_banks = [freed[2], freed[0], acc_banks[3], freed[3], freed[1]] + acc_banks[0:3]
+        acc_banks = [freed[2], freed[0], acc_banks[3]] + acc_banks[0:3] + [freed[3], freed[1]]
         out_rows = out.rearrange("(n p) t -> p n t", p=P)
         groups = []
         for i, (t0, t1) in enumerate(PIECES):
@@ -512,8 +513,9 @@ def tile_list_early_exit_refill_kernel(
             width = len(parts) * parts[0][2]
             if filled % (N_TILES * BANK) == 0:
                 result = stream.tile([P, N_TILES * BANK], F32, name="stream", tag="stream", align_bytes=64)
-            for a in range(PASSES):
-                second_product(acc, a, c, parts)
+            for ahead in FIRST_PASSES.get(idx, ()):
+                second_product(acc_banks[ahead % len(acc_banks)], 0, *groups[ahead][0:2])
+            second_product(acc, 1, c, parts)
             acc = acc[:, 0:width]
             staged = slot(idx % STAGING_SLOTS, [P, 2, BANK], F32)
             magnitude = staged[:, 0, 0:width]

@@ -37,6 +37,7 @@ PAGE_BUFFERS = (4, 3, 1)
 LAST_PIECE = 2 * P
 VECTOR_ABS = (8, 9, 12, 13, 15, 16)
 FIRST_PASSES = {0: (0, 1, 2), 2: (3, 4), 5: (5, 6, 7, 8), 9: (9, 10, 11, 12), 13: (13, 14, 15, 16, 17)}
+NEGATED_IN = {6: 0, 9: 1, 10: 2, 13: 1, 15: 3, 16: 2}
 STAGING_SLOTS = 7
 
 
@@ -340,7 +341,7 @@ def tile_list_early_exit_refill_kernel(
             if cols.stop - cols.start <= half:
                 h = cols.start // half
                 runs = [(cols, grouped[:, h, cols.start - half * h : cols.stop - half * h, :].rearrange("p t i -> p (t i)"))]
-            elif a == 0:
+            elif a == 0 or c < CHUNKS - 1:
                 runs = [(cols, grouped.rearrange("p h t i -> p (h t i)"))]
             else:
                 runs = [(slice(half * h, half * (h + 1)), grouped[:, h].rearrange("p t i -> p (t i)")) for h in range(2)]
@@ -363,9 +364,9 @@ def tile_list_early_exit_refill_kernel(
                     stop=(a == PASSES - 1 and i == len(parts) - 1),
                 )
 
-        z_upper = [keep.tile([P, 2, BANK // 2, 4], BF16, name="z_upper%d" % c, align_bytes=64)[:] for c in range(2)]
-        woven = keep.tile([P, 2, 2, BANK // 2, 4], BF16, name="z_upper_woven", align_bytes=64)
-        z_upper = z_upper + [woven[:, :, 0], woven[:, :, 1]]
+        z_upper = [keep.tile([P, 2, BANK // 2, 4], BF16, name="z_upper%d" % c, align_bytes=64)[:] for c in range(3)]
+        woven = keep.tile([P, 4, BANK // 2, 4], BF16, name="z_woven", align_bytes=64)
+        z_upper.append(woven[:, 0:4:3])
 
         def turn_back_pair(c):
             src = z_turned[c][:].rearrange("t b u p e -> t (b u p e)").bitcast(F32)
@@ -433,7 +434,7 @@ def tile_list_early_exit_refill_kernel(
                 for c in range(CHUNKS):
                     if c % 2 == 0:
                         two_chunks = big(c, [P, 2, 2, BANK // 2, 4], BF16)
-                    z_lower[c] = two_chunks[:, c % 2]
+                    z_lower[c] = two_chunks[:, c % 2] if c < CHUNKS - 1 else woven[:, 1:3]
                     turn_back(c, z_lower[c], [(hb, next_bank()) for hb in range(2)])
             if s == FIRST_LANE_SLICE - 1:
                 for c in (1, 2):
@@ -484,7 +485,7 @@ def tile_list_early_exit_refill_kernel(
             z_tiles(0, c, "piece%d" % (DIRECT - c))
             quantize_z(0, c, z_lower[c], slice(0, BANK))
 
-        for c in range(CHUNKS):
+        for c in range(CHUNKS - 1):
             z_tiles(1, c, "codes1_%d" % c)
         add_piece(0, nc.vector)
         for i, (t0, t1) in enumerate(PIECES[:-1]):
@@ -496,52 +497,79 @@ def tile_list_early_exit_refill_kernel(
                 nc.vector.tensor_copy(out=lanes, in_=lane_rows[i].rearrange("p e (h t) -> p h t e", h=lanes.shape[1]))
             if i + 2 < len(PIECES):
                 add_piece(i + 1, nc.vector)
-            else:
-                quantize_late(c + 1)
-            quantize_z(1, c, z_upper[c], slice(t0 % BANK, t0 % BANK + t1 - t0))
-        add_piece(len(PIECES) - 1, nc.gpsimd)
+                quantize_z(1, c, z_upper[c], slice(t0 % BANK, t0 % BANK + t1 - t0))
 
-        def finish(logs, magnitude, dst, queue):
-            nc.scalar.activation(out=logs, in_=magnitude, func=ACT.Ln, bias=one[:], scale=0.5)
-            queue.dma_start(out=dst, in_=logs.rearrange("p (n t) -> p n t", n=dst.shape[1]))
+        sums = {}
+        results = []
 
-        waiting = []
-        pair = []
-        filled = 0
-        for idx, (c, parts, dst) in enumerate(groups):
-            acc = acc_banks[idx % len(acc_banks)]
+        def multiply(idx):
+            c, parts, dst = groups[idx]
             width = len(parts) * parts[0][2]
-            if filled % (N_TILES * BANK) == 0:
-                result = stream.tile([P, N_TILES * BANK], F32, name="stream", tag="stream", align_bytes=64)
+            acc = acc_banks[idx % len(acc_banks)]
             for ahead in FIRST_PASSES.get(idx, ()):
                 second_product(acc_banks[ahead % len(acc_banks)], 0, *groups[ahead][0:2])
             second_product(acc, 1, c, parts)
-            acc = acc[:, 0:width]
-            staged = slot(idx % STAGING_SLOTS, [P, 2, BANK], F32)
-            magnitude = staged[:, 0, 0:width]
-            start = filled % (N_TILES * BANK)
-            logs = result[:, start : start + width]
-            filled = filled + width
-            if idx in VECTOR_ABS:
-                negated = staged[:, 1, 0:width]
-                nc.vector.tensor_scalar(out=negated, in0=acc, scalar1=-1.0, scalar2=None, op0=ALU.mult)
-                pair.append((magnitude, acc, negated))
-                waiting.append((logs, magnitude, dst))
-                if len(pair) == 2:
-                    for operands in pair:
-                        nc.vector.tensor_tensor(*operands, ALU.max)
-                    pair = []
-            elif idx < len(groups) - 1:
-                nc.scalar.activation(out=magnitude, in_=acc, func=ACT.Abs)
-                waiting.insert(1, (logs, magnitude, dst))
-                count = 2 if c < CHUNKS - 1 else len(waiting)
-                for entry in waiting[:count]:
-                    finish(*entry, nc.sync)
-                waiting = waiting[count:]
+            start = sum(len(g[1]) * g[1][0][2] for g in groups[:idx]) % (N_TILES * BANK)
+            if start == 0:
+                results.append(stream.tile([P, N_TILES * BANK], F32, name="stream", tag="stream", align_bytes=64))
+            magnitude = slot(idx % STAGING_SLOTS, [P, BANK], F32)
+            sums[idx] = (acc[:, 0:width], magnitude[:, 0:width], results[-1][:, start : start + width], dst)
+
+        negated = {}
+
+        def negate(idx):
+            acc = sums[idx][0]
+            tile = keep.tile([P, BANK], F32, name="negated", tag="negated%d" % NEGATED_IN[idx], align_bytes=64)
+            negated[idx] = tile[:, 0 : acc.shape[1]]
+            nc.vector.tensor_scalar(out=negated[idx], in0=acc, scalar1=-1.0, scalar2=None, op0=ALU.mult)
+
+        def larger(idx):
+            nc.vector.tensor_tensor(sums[idx][1], sums[idx][0], negated[idx], ALU.max)
+
+        def absolute(idx):
+            nc.scalar.activation(out=sums[idx][1], in_=sums[idx][0], func=ACT.Abs)
+
+        def finish(idx, queue):
+            acc, magnitude, logs, dst = sums[idx]
+            nc.scalar.activation(out=logs, in_=magnitude, func=ACT.Ln, bias=one[:], scale=0.5)
+            queue.dma_start(out=dst, in_=logs.rearrange("p (n t) -> p n t", n=dst.shape[1]))
+
+        for idx in range(9):
+            multiply(idx)
+            if idx == 6:
+                negate(idx)
             else:
-                finish(*waiting[0], nc.sync)
-                nc.scalar.activation(out=magnitude, in_=acc, func=ACT.Abs)
-                finish(*waiting[1], nc.sync)
-                finish(logs, magnitude, dst, nc.scalar)
-            if idx == VECTOR_ABS[1]:
-                quantize_z(1, CHUNKS - 1, z_upper[CHUNKS - 1], slice(0, BANK))
+                absolute(idx)
+                finish(idx, nc.sync)
+        quantize_z(1, 2, z_upper[2], slice(0, BANK))
+        quantize_late(3)
+        add_piece(len(PIECES) - 1, nc.gpsimd)
+        larger(6)
+        finish(6, nc.sync)
+        for idx in (9, 10, 11, 12):
+            multiply(idx)
+        for idx in (9, 10):
+            negate(idx)
+        larger(9)
+        for idx in (11, 12):
+            absolute(idx)
+        for idx in (9, 11):
+            finish(idx, nc.sync)
+        z_tiles(1, 3, "negated0")
+        quantize_z(1, 3, z_upper[3], slice(0, BANK))
+        larger(10)
+        finish(10, nc.sync)
+        for idx in (13, 14, 15, 16, 17):
+            multiply(idx)
+        for idx in (13, 15):
+            negate(idx)
+        larger(13)
+        negate(16)
+        for idx in (15, 16):
+            larger(idx)
+        absolute(14)
+        for idx in (12, 14, 13, 15):
+            finish(idx, nc.sync)
+        absolute(17)
+        finish(16, nc.sync)
+        finish(17, nc.scalar)

@@ -30,15 +30,15 @@ STREAM_BUFS = 5
 OLD_AHEAD = 3
 EARLY_HALVES = {2: ((5, 0), (7, 0)), 3: ((6, 0),), 4: ((7, 1),)}
 PIECES = ((384, 512), (256, 384), (0, 256), (512, 768), (768, 1024), (1024, 1536), (1536, 2048))
-DIRECT = 3
-HEIRS = {1: 3, 0: 4, 3: 5}
 WORD_CHUNKS = (0, 3)
+HEIRS = {1: 3, 0: 4, 3: 5}
+LATE_CODES_IN = {1: 2, 2: 1, 3: 0}
 PAGE_BUFFERS = (4, 3, 1)
 LAST_PIECE = 2 * P
-VECTOR_ABS = (8, 9, 12, 13, 15, 16)
 FIRST_PASSES = {0: (0, 1, 2), 2: (3, 4), 5: (5, 6, 7, 8), 9: (9, 10, 11, 12), 13: (13, 14, 15, 16, 17)}
 NEGATED_IN = {6: 0, 9: 1, 10: 2, 13: 1, 15: 3, 16: 2}
 STAGING_SLOTS = 7
+SCALE_ROWS = 32
 
 
 def tile_list_early_exit_refill_kernel(
@@ -67,7 +67,7 @@ def tile_list_early_exit_refill_kernel(
         tab_rows = keep.tile([P, T], U8, name="tab_rows", align_bytes=64)
         one = keep.tile([P, 1], F32, name="one")
         nc.gpsimd.memset(one[:], 1.0)
-        for rows in (slice(32, 64), slice(64, P)):
+        for rows in (slice(SCALE_ROWS, P // 2), slice(P // 2, P)):
             nc.vector.memset(tab_rows[rows, :].bitcast(I32), 0)
         v_planes = keep.tile([P, S], U8, name="v_planes", align_bytes=64)
         nc.vector.memset(v_planes[:].bitcast(I32), 0)
@@ -133,7 +133,7 @@ def tile_list_early_exit_refill_kernel(
         offsets = keep.tile([P, S // 16], U16, name="offsets")
         nc.sync.dma_start(offsets[:], offs)
         nc.sync.dma_start(
-            out=tab_rows[0:32, :].bitcast(I32), in_=tab_scales.rearrange("a q t -> (a q) t").bitcast(I32)
+            out=tab_rows[0:SCALE_ROWS, :].bitcast(I32), in_=tab_scales.rearrange("a q t -> (a q) t").bitcast(I32)
         )
         load_tab(0)
         load_w1_lower(0, 6)
@@ -195,9 +195,11 @@ def tile_list_early_exit_refill_kernel(
                     w1_codes[first + i, a] = codes[:, i, a, :]
                     w1_planes[first + i, a] = planes[:, i, a, :]
 
+        cleared_behind = {1: "big%d" % PAGE_BUFFERS[1], 2: "w2_planes"}
+
         def prepare_w1_lower(s):
-            if s < 3:
-                tag = ("w1_second", "big%d" % PAGE_BUFFERS[1])[s - 1]
+            if s in cleared_behind:
+                tag = cleared_behind[s]
                 grouped = keep.tile([P, 1, PASSES, P, 4], BF16, name="w1_grouped", tag=tag, align_bytes=64)
             else:
                 grouped = ring.tile([P, 1, PASSES, P, 4], BF16, name="w1_grouped", tag="w1_grouped", align_bytes=64)
@@ -263,7 +265,7 @@ def tile_list_early_exit_refill_kernel(
             nc.scalar.activation(out=h, in_=acc, func=ACT.Relu, bias=zero[:])
 
         def page_of(s):
-            return pages[2 * s % PAGES]
+            return pages[2 * (s + 1) % PAGES]
 
         def scatter(s):
             page = page_of(s)
@@ -274,13 +276,15 @@ def tile_list_early_exit_refill_kernel(
             else:
                 weights = wgs_lanes[:, s - FIRST_LANE_SLICE, :]
             if s == 0:
-                for (j0, j1), h in zip(halves, (h_first[:], h_tiles[0][:, BANK:S])):
-                    places = page[:].indirect(offsets2[:, j0 // 16 : j1 // 16])
+                for (j0, j1), h, target in zip(halves, (h_first[:], h_tiles[0][:, BANK:S]), (pages[0], page)):
+                    places = target[:].indirect(offsets2[:, j0 // 16 : j1 // 16])
                     nc.vector.tensor_tensor(places, h, weights[:, j0:j1], ALU.mult)
             else:
                 nc.vector.tensor_tensor(page[:].indirect(offsets2[:]), h_tiles[s], weights, ALU.mult)
 
-        z_turned = [keep.tile([P, 4, 2, P, 2], BF16, name="z_turned", tag="z_turned%d" % c, align_bytes=64) for c in range(CHUNKS)]
+        z_turned = [
+            keep.tile([P, 4, 2, P, 2], BF16, name="z_turned", tag="z_turned%d" % c, align_bytes=64) for c in range(CHUNKS)
+        ]
 
         lane2_turned = keep.tile([P, 2, 4, P], BF16, name="lane2_turned", align_bytes=64)
 
@@ -301,6 +305,8 @@ def tile_list_early_exit_refill_kernel(
                     )
 
         def sum_turned(s):
+            if s == 0:
+                add_turned(s, pages[0], False, False)
             add_turned(s, page_of(s), False, True)
             sums = [bank.rearrange("t (b r) -> t b r", b=4) for bank in sum_banks[s]]
             for c in chunk_order(s):
@@ -340,13 +346,14 @@ def tile_list_early_exit_refill_kernel(
             half = BANK // 2
             if cols.stop - cols.start <= half:
                 h = cols.start // half
-                runs = [(cols, grouped[:, h, cols.start - half * h : cols.stop - half * h, :].rearrange("p t i -> p (t i)"))]
+                part = grouped[:, h, cols.start - half * h : cols.stop - half * h, :]
+                runs = [(cols, part.rearrange("p t i -> p (t i)"))]
             elif a == 0 or c < CHUNKS - 1:
                 runs = [(cols, grouped.rearrange("p h t i -> p (h t i)"))]
             else:
                 runs = [(slice(half * h, half * (h + 1)), grouped[:, h].rearrange("p t i -> p (t i)")) for h in range(2)]
-            for part, values in runs:
-                nc.vector.quantize_mx(out=z_codes[a, c][:, part].bitcast(FP8X4), scales=z_planes[a, c][:, part], in_=values)
+            for run, values in runs:
+                nc.vector.quantize_mx(out=z_codes[a, c][:, run].bitcast(FP8X4), scales=z_planes[a, c][:, run], in_=values)
 
         def z_tiles(a, c, tag):
             z_codes[a, c] = keep.tile([P, BANK], U32, name="z_codes", tag=tag, align_bytes=64)
@@ -354,8 +361,9 @@ def tile_list_early_exit_refill_kernel(
 
         def second_product(acc, a, c, parts):
             for i, (n, t0, width) in enumerate(parts):
+                first = sum(part[2] for part in parts[:i])
                 nc.tensor.matmul_mx(
-                    out=acc[:, width * i : width * (i + 1)],
+                    out=acc[:, first : first + width],
                     lhsT=w2_codes[:, a, 2 * P * n : 2 * P * (n + 1)].bitcast(FP4X4),
                     lhsT_scale=w2_planes[:, a, P * n : P * (n + 1)],
                     rhs=z_codes[a, c][:, t0 : t0 + width].bitcast(FP8X4),
@@ -391,18 +399,18 @@ def tile_list_early_exit_refill_kernel(
         pages[2] = big(PAGE_BUFFERS[2], [P, T2], F32)
         nc.gpsimd.memset(pages[2][:].bitcast(I32), 0)
         prepare_w1_lower(1)
-        w2_planes = keep.tile([P, PASSES, N], U8, name="w2_planes", tag="w1_second", align_bytes=64)
+        pages[1] = big(PAGE_BUFFERS[1], [P, T2], F32)
+        nc.gpsimd.memset(pages[1][:].bitcast(I32), 0)
+        for piece in first_pieces:
+            first_product(0, piece)
+        prepare_w1_lower(2)
+        w2_planes = keep.tile([P, PASSES, N], U8, name="w2_planes", tag=cleared_behind[2], align_bytes=64)
         nc.gpsimd.memset(w2_planes[:].rearrange("p a n -> p (a n)").bitcast(I32), 0)
         for q in range(4):
             nc.sync.dma_start(
                 out=w2_planes[32 * q : 32 * q + 4, :, :].bitcast(I32),
                 in_=w2_scales[:, 4 * q : 4 * q + 4, :].rearrange("a r n -> r a n").bitcast(I32),
             )
-        for piece in first_pieces:
-            first_product(0, piece)
-        prepare_w1_lower(2)
-        pages[1] = big(PAGE_BUFFERS[1], [P, T2], F32)
-        nc.gpsimd.memset(pages[1][:].bitcast(I32), 0)
         for piece in halves:
             first_product(1, piece)
         add_turned(0, olds[0], True, False)
@@ -461,7 +469,7 @@ def tile_list_early_exit_refill_kernel(
         c, [(n, t0, width)], dst = groups.pop()
         for cols in (slice(0, width - LAST_PIECE), slice(width - LAST_PIECE, width)):
             groups.append((c, [(n, cols.start, cols.stop - cols.start)], dst[:, :, cols]))
-        z_tiles(0, 0, "big%d" % PAGE_BUFFERS[2 * (last - 1) % PAGES])
+        z_tiles(0, 0, "big%d" % PAGE_BUFFERS[2 * last % PAGES])
         for cols in (slice(BANK // 2, BANK), slice(0, BANK // 2)):
             quantize_z(0, 0, z_lower[0], cols)
 
@@ -482,7 +490,7 @@ def tile_list_early_exit_refill_kernel(
                 engine.tensor_tensor(lane3, old_part, page_part, ALU.add)
 
         def quantize_late(c):
-            z_tiles(0, c, "piece%d" % (DIRECT - c))
+            z_tiles(0, c, "piece%d" % LATE_CODES_IN[c])
             quantize_z(0, c, z_lower[c], slice(0, BANK))
 
         for c in range(CHUNKS - 1):
@@ -504,12 +512,12 @@ def tile_list_early_exit_refill_kernel(
 
         def multiply(idx):
             c, parts, dst = groups[idx]
-            width = len(parts) * parts[0][2]
+            width = sum(part[2] for part in parts)
             acc = acc_banks[idx % len(acc_banks)]
             for ahead in FIRST_PASSES.get(idx, ()):
                 second_product(acc_banks[ahead % len(acc_banks)], 0, *groups[ahead][0:2])
             second_product(acc, 1, c, parts)
-            start = sum(len(g[1]) * g[1][0][2] for g in groups[:idx]) % (N_TILES * BANK)
+            start = sum(part[2] for g in groups[:idx] for part in g[1]) % (N_TILES * BANK)
             if start == 0:
                 results.append(stream.tile([P, N_TILES * BANK], F32, name="stream", tag="stream", align_bytes=64))
             magnitude = slot(idx % STAGING_SLOTS, [P, BANK], F32)
@@ -536,7 +544,7 @@ def tile_list_early_exit_refill_kernel(
 
         for idx in range(9):
             multiply(idx)
-            if idx == 6:
+            if idx in NEGATED_IN:
                 negate(idx)
             else:
                 absolute(idx)
@@ -546,7 +554,7 @@ def tile_list_early_exit_refill_kernel(
         add_piece(len(PIECES) - 1, nc.gpsimd)
         larger(6)
         finish(6, nc.sync)
-        for idx in (9, 10, 11, 12):
+        for idx in FIRST_PASSES[9]:
             multiply(idx)
         for idx in (9, 10):
             negate(idx)
@@ -555,11 +563,11 @@ def tile_list_early_exit_refill_kernel(
             absolute(idx)
         for idx in (9, 11):
             finish(idx, nc.sync)
-        z_tiles(1, 3, "negated0")
+        z_tiles(1, 3, "negated%d" % NEGATED_IN[6])
         quantize_z(1, 3, z_upper[3], slice(0, BANK))
         larger(10)
         finish(10, nc.sync)
-        for idx in (13, 14, 15, 16, 17):
+        for idx in FIRST_PASSES[13]:
             multiply(idx)
         for idx in (13, 15):
             negate(idx)

from contextlib import ExitStack

import concourse.mybir as mybir
from concourse.masks import make_identity

K, H, N, T, S, T2, P = 1024, 1024, 512, 2048, 1024, 2048, 128
FLOPS = 2 * K * H * S + 2 * H * N * T2

F32 = mybir.dt.float32
BF16 = mybir.dt.bfloat16
I32 = mybir.dt.int32
U32 = mybir.dt.uint32
U16 = mybir.dt.uint16
U8 = mybir.dt.uint8
FP8X4 = mybir.dt.float8_e4m3fn_x4
FP4X4 = mybir.dt.float4_e2m1fn_x4
ACT = mybir.ActivationFunctionType
ALU = mybir.AluOpType

BANK = 512
PASS_ROWS = 512
PASSES = 2
SLICES = H // P
CHUNKS = T2 // BANK
N_TILES = N // P
AS_THEY_LIE = 4
FIRST_LANE_SLICE = 6
PAGES = 3
STREAM_BUFS = 5
OLD_AHEAD = 3
EARLY_HALVES = {2: ((5, 0), (7, 0)), 3: ((6, 0),), 4: ((7, 1),)}
PIECES = ((384, 512), (256, 384), (0, 256), (512, 768), (768, 1024), (1024, 1536), (1536, 2048))
WORD_CHUNKS = (0, 3)
HEIRS = {1: 3, 0: 4, 3: 5}
LATE_CODES_IN = {1: 2, 2: 1, 3: 0}
PAGE_BUFFERS = (4, 3, 1)
LAST_PIECE = 2 * P
FIRST_PASSES = {0: (0, 1, 2), 2: (3, 4), 5: (5, 6, 7, 8), 9: (9, 10, 11, 12), 13: (13, 14, 15, 16, 17)}
NEGATED_IN = {6: 0, 9: 1, 10: 2, 13: 1, 15: 3, 16: 2}
STAGING_SLOTS = 7
SCALE_ROWS = 32


def tile_list_early_exit_refill_kernel(
    tc, tab_words, tab_scales, offs, w1, wgs, offs2, old, w2_words, w2_scales, out
):
    nc = tc.nc
    with ExitStack() as ctx:
        keep = ctx.enter_context(tc.tile_pool(name="keep", bufs=1))
        ring = ctx.enter_context(tc.tile_pool(name="ring", bufs=2))
        stream = ctx.enter_context(tc.tile_pool(name="stream", bufs=STREAM_BUFS))
        psum = ctx.enter_context(tc.psum_pool(name="psum", bufs=1))

        banks = [psum.tile([P, BANK], F32, name="bank%d" % b)[:] for b in range(8)]
        taken = []

        def next_bank():
            taken.append(banks[len(taken) % len(banks)])
            return taken[-1]

        def slot(index, shape, dtype):
            return keep.tile(shape, dtype, name="slot%d" % index, tag="slot%d" % index, align_bytes=64)

        def big(index, shape, dtype):
            return keep.tile(shape, dtype, name="big%d" % index, tag="big%d" % index, align_bytes=64)

        tab_rows = keep.tile([P, T], U8, name="tab_rows", align_bytes=64)
        one = keep.tile([P, 1], F32, name="one")
        nc.gpsimd.memset(one[:], 1.0)
        for rows in (slice(SCALE_ROWS, P // 2), slice(P // 2, P)):
            nc.vector.memset(tab_rows[rows, :].bitcast(I32), 0)
        v_planes = keep.tile([P, S], U8, name="v_planes", align_bytes=64)
        nc.vector.memset(v_planes[:].bitcast(I32), 0)
        zero = keep.tile([P, 1], F32, name="zero")
        nc.scalar.activation(out=zero[:], in_=one[:], func=ACT.Ln)
        ident = keep.tile([P, P], F32, name="ident")
        make_identity(nc, ident[:])
        ident_bf16 = keep.tile([P, P], BF16, name="ident_bf16")
        nc.scalar.copy(out=ident_bf16[:], in_=ident[:])

        tabs = [big(a, [P, T], I32) for a in range(PASSES)]

        def load_tab(a):
            nc.sync.dma_start(out=tabs[a][:], in_=tab_words[a].rearrange("p t i -> p (t i)").bitcast(I32))

        w1_raw = {}

        def load_w1_lower(s, index):
            raw = slot(index, [P, PASSES, 4, P], F32)
            for a in range(PASSES):
                part = w1[PASS_ROWS * a : PASS_ROWS * (a + 1), P * s : P * (s + 1)]
                nc.sync.dma_start(out=raw[:, a, :, :], in_=part.rearrange("(p j) c -> p j c", j=4))
            w1_raw[s] = raw

        def load_w1_upper(half, indices):
            c0 = PASS_ROWS + 2 * P * half
            for a in range(PASSES):
                raw = slot(indices[a], [P, 4, 2 * P], F32)
                part = w1[PASS_ROWS * a : PASS_ROWS * (a + 1), c0 : c0 + 2 * P]
                nc.sync.dma_start(out=raw[:], in_=part.rearrange("(p j) c -> p j c", j=4))
                w1_raw[AS_THEY_LIE + half, a] = raw

        olds = {}
        old_lanes = old[PASS_ROWS:H, :].rearrange("(p i) t -> p i t", i=4)

        def load_old(s):
            tile = stream.tile([P, T2], F32, name="stream", tag="stream", align_bytes=64)
            if s < AS_THEY_LIE:
                nc.sync.dma_start(out=tile[:], in_=old[P * s : P * (s + 1), :])
            elif s < FIRST_LANE_SLICE:
                m0 = 64 * (s - AS_THEY_LIE)
                for e in range(2):
                    nc.sync.dma_start(out=tile[e:P:2, :], in_=old_lanes[m0 : m0 + 64, e, :])
            else:
                nc.sync.dma_start(out=tile[:], in_=old_lanes[:, s - AS_THEY_LIE, :])
            olds[s] = tile

        old_last = []
        lane_rows = {}

        def load_old_last():
            for i, (t0, t1) in enumerate(PIECES):
                heir = HEIRS.get(i)
                extra = 0 if heir is None else (PIECES[heir][1] - PIECES[heir][0]) // 2
                tile = keep.tile([P, t1 - t0 + extra], F32, name="piece", tag="piece%d" % i, align_bytes=64)
                old_last.append(tile[:, extra:])
                nc.sync.dma_start(out=old_last[i], in_=old_lanes[:, 3, t0:t1])
                if heir is not None:
                    lane_rows[heir] = tile[:, 0 : 2 * extra].bitcast(BF16).rearrange("p (e t) -> p e t", e=2)

        pages = {0: big(PAGE_BUFFERS[0], [P, T2], F32)}
        nc.vector.memset(pages[0][:].bitcast(I32), 0)
        offsets = keep.tile([P, S // 16], U16, name="offsets")
        nc.sync.dma_start(offsets[:], offs)
        nc.sync.dma_start(
            out=tab_rows[0:SCALE_ROWS, :].bitcast(I32), in_=tab_scales.rearrange("a q t -> (a q) t").bitcast(I32)
        )
        load_tab(0)
        load_w1_lower(0, 6)
        load_tab(1)
        offsets2 = keep.tile([P, S // 16], U16, name="offsets2")
        nc.sync.dma_start(offsets2[:], offs2)
        wgs_rows = keep.tile([P, S], F32, name="wgs_rows")
        nc.sync.dma_start(out=wgs_rows[:, 0:BANK], in_=wgs[:, 0:BANK])
        load_w1_lower(1, 0)
        nc.sync.dma_start(out=wgs_rows[:, BANK:S], in_=wgs[:, BANK:S])
        load_w1_lower(2, 1)
        load_old(0)
        load_w1_lower(3, 2)
        load_w1_upper(0, (7, 6))
        load_old(1)
        load_w1_upper(1, (5, 3))
        load_old(2)
        wgs_by_lane = wgs.rearrange("(q i) j -> q i j", i=4)
        wgs_pair = keep.tile([P, S], F32, name="wgs_pair")
        for e in range(2):
            for g in range(2):
                nc.sync.dma_start(out=wgs_pair[64 * g + e : 64 * (g + 1) : 2, :], in_=wgs_by_lane[:, e, :])
        wgs_lanes = keep.tile([P, 2, S], F32, name="wgs_lanes")
        for g in (0, 2, 1, 3):
            nc.sync.dma_start(out=wgs_lanes[32 * g : 32 * (g + 1), :, :], in_=wgs_by_lane[:, 2:4, :])
        w2_codes = keep.tile([P, PASSES, 2 * N], U8, name="w2_codes", align_bytes=64)
        nc.sync.dma_start(out=w2_codes[:].bitcast(I32), in_=w2_words.rearrange("a p c -> p a c").bitcast(I32))

        v_rows = keep.tile([P, S], U8, name="v_rows", align_bytes=64)
        v_words = [keep.tile([P, S], U32, name="v_words0", align_bytes=64)]
        halves = [(0, BANK), (BANK, S)]
        first_pieces = [(0, BANK // 2), (BANK // 2, BANK), (BANK, S)]
        nc.vector.tensor_copy(v_rows[:], tab_rows[:].indirect(offsets[:]))
        for a in range(PASSES):
            for q in range(4):
                src = 16 * a + 4 * q
                dst = 32 * q + 4 * a
                if src != dst:
                    nc.scalar.dma_start(
                        out=v_planes[dst : dst + 4, :].bitcast(I32), in_=v_rows[src : src + 4, :].bitcast(I32)
                    )
        nc.vector.tensor_copy(v_words[0][:], tabs[0][:].bitcast(U32).indirect(offsets[:]))
        nc.vector.tensor_copy(v_planes[0:4, :].bitcast(I32), v_rows[0:4, :].bitcast(I32))

        w1_codes = {}
        w1_planes = {}

        def quantize_w1(first, grouped):
            count = grouped.shape[1]
            codes = keep.tile([P, count, PASSES, P], U32, name="w1_codes%d" % first, align_bytes=64)
            planes = keep.tile([P, count, PASSES, P], U8, name="w1_planes%d" % first, align_bytes=64)
            nc.vector.quantize_mx(
                out=codes[:].rearrange("p i a c -> p (i a c)").bitcast(FP8X4),
                scales=planes[:].rearrange("p i a c -> p (i a c)"),
                in_=grouped.rearrange("p i a c j -> p (i a c j)"),
            )
            for i in range(count):
                for a in range(PASSES):
                    w1_codes[first + i, a] = codes[:, i, a, :]
                    w1_planes[first + i, a] = planes[:, i, a, :]

        cleared_behind = {1: "big%d" % PAGE_BUFFERS[1], 2: "w2_planes"}

        def prepare_w1_lower(s):
            if s in cleared_behind:
                tag = cleared_behind[s]
                grouped = keep.tile([P, 1, PASSES, P, 4], BF16, name="w1_grouped", tag=tag, align_bytes=64)
            else:
                grouped = ring.tile([P, 1, PASSES, P, 4], BF16, name="w1_grouped", tag="w1_grouped", align_bytes=64)
            for a in range(PASSES):
                nc.scalar.copy(
                    out=grouped[:, 0, a, :, :].rearrange("p (c i) j -> p c j i", i=4),
                    in_=w1_raw[s][:, a, :, :].rearrange("p j (c i) -> p c j i", i=4),
                )
            quantize_w1(s, grouped[:])

        def prepare_w1_first():
            for a, tag in enumerate(("w1_first", "v_words1")):
                grouped = keep.tile([P, P, 4], BF16, name="w1_first", tag=tag, align_bytes=64)
                nc.scalar.copy(
                    out=grouped[:].rearrange("p (c i) j -> p c j i", i=4),
                    in_=w1_raw[0][:, a, :, :].rearrange("p j (c i) -> p c j i", i=4),
                )
                codes = keep.tile([P, P], U32, name="w1_codes_first%d" % a, align_bytes=64)
                planes = keep.tile([P, P], U8, name="w1_planes_first%d" % a, align_bytes=64)
                nc.vector.quantize_mx(
                    out=codes[:].bitcast(FP8X4), scales=planes[:], in_=grouped[:].rearrange("p c j -> p (c j)")
                )
                w1_codes[0, a] = codes[:]
                w1_planes[0, a] = planes[:]

        lanes_grouped = keep.tile([P, 2, PASSES, P, 4], BF16, name="lanes_grouped", align_bytes=64)

        def prepare_w1_upper(half):
            grouped = ring.tile([P, 1, PASSES, P, 4], BF16, name="w1_grouped", tag="w1_grouped", align_bytes=64)
            for a in range(PASSES):
                raw = w1_raw[AS_THEY_LIE + half, a][:].rearrange("p j (m i) -> p m j i", i=4)
                nc.scalar.copy(out=grouped[:, 0, a, :, :].rearrange("p (m e) j -> p m j e", e=2), in_=raw[:, :, :, 0:2])
                nc.scalar.copy(
                    out=lanes_grouped[:, :, a, 64 * half : 64 * (half + 1), :].rearrange("p i m j -> p m j i"),
                    in_=raw[:, :, :, 2:4],
                )
            quantize_w1(AS_THEY_LIE + half, grouped[:])

        h_tiles = {}
        h_pieces = {}
        h_first = keep.tile([P, BANK], F32, name="h_first")

        def first_product(s, piece):
            cols = slice(*piece)
            if s == 0 and piece[0] < BANK:
                h = h_first[:, cols]
            else:
                if s not in h_tiles:
                    h_tiles[s] = slot(s, [P, S], F32)[:]
                h = h_tiles[s][:, cols]
            h_pieces[s, piece] = h
            acc = next_bank()[:, 0 : piece[1] - piece[0]]
            for a in range(PASSES):
                nc.tensor.matmul_mx(
                    out=acc,
                    lhsT=w1_codes[s, a].bitcast(FP8X4),
                    lhsT_scale=w1_planes[s, a],
                    rhs=v_words[a][:, cols].bitcast(FP8X4),
                    rhs_scale=v_planes[4 * a : P, cols],
                    start=(a == 0),
                    stop=(a == PASSES - 1),
                )
            nc.scalar.activation(out=h, in_=acc, func=ACT.Relu, bias=zero[:])

        def page_of(s):
            return pages[2 * (s + 1) % PAGES]

        def scatter(s):
            page = page_of(s)
            if s < AS_THEY_LIE:
                weights = wgs_rows[:]
            elif s < FIRST_LANE_SLICE:
                weights = wgs_pair[:]
            else:
                weights = wgs_lanes[:, s - FIRST_LANE_SLICE, :]
            if s == 0:
                for (j0, j1), h, target in zip(halves, (h_first[:], h_tiles[0][:, BANK:S]), (pages[0], page)):
                    places = target[:].indirect(offsets2[:, j0 // 16 : j1 // 16])
                    nc.vector.tensor_tensor(places, h, weights[:, j0:j1], ALU.mult)
            else:
                nc.vector.tensor_tensor(page[:].indirect(offsets2[:]), h_tiles[s], weights, ALU.mult)

        z_turned = [
            keep.tile([P, 4, 2, P, 2], BF16, name="z_turned", tag="z_turned%d" % c, align_bytes=64) for c in range(CHUNKS)
        ]

        lane2_turned = keep.tile([P, 2, 4, P], BF16, name="lane2_turned", align_bytes=64)

        sum_banks = {}

        def chunk_order(s):
            return (1, 2, 0, 3) if s == FIRST_LANE_SLICE else range(CHUNKS)

        def add_turned(s, src, first, closes):
            if first:
                sum_banks[s] = [next_bank() for c in range(CHUNKS)]
            for c in chunk_order(s):
                for b in range(4):
                    t0 = BANK * c + P * b
                    nc.tensor.matmul(
                        out=sum_banks[s][c][:, P * b : P * (b + 1)], lhsT=src[:, t0 : t0 + P], rhs=ident[:],
                        is_transpose=True, start=(first and b == 0), stop=(closes and b == 3),
                    )

        def sum_turned(s):
            if s == 0:
                add_turned(s, pages[0], False, False)
            add_turned(s, page_of(s), False, True)
            sums = [bank.rearrange("t (b r) -> t b r", b=4) for bank in sum_banks[s]]
            for c in chunk_order(s):
                if s < AS_THEY_LIE:
                    nc.scalar.copy(
                        out=z_turned[c][:, :, :, 32 * s : 32 * (s + 1), :],
                        in_=sums[c].rearrange("t b (q u e) -> t b u q e", u=2, e=2),
                    )
                elif s < FIRST_LANE_SLICE:
                    m0 = 64 * (s - AS_THEY_LIE)
                    nc.scalar.copy(
                        out=z_turned[c][:, :, 0, m0 : m0 + 64, :].rearrange("t b m e -> t b (m e)"), in_=sums[c]
                    )
                elif c not in WORD_CHUNKS:
                    nc.scalar.copy(out=lane2_turned[:, c - 1], in_=sums[c])
                else:
                    nc.scalar.copy(out=z_turned[c][:, :, 1, :, 0], in_=sums[c])

        def turn_back(c, grouped, halves_and_banks):
            src = z_turned[c][:].rearrange("t b u p e -> t (b u p e)").bitcast(F32)
            for hb, bank in halves_and_banks:
                dst = grouped[:, hb].rearrange("p t i -> p (t i)").bitcast(F32)
                pairs = bank.rearrange("p (b u t) -> p b u t", b=2, u=2)
                for b in range(2):
                    for u in range(2):
                        w0 = P * (2 * (2 * hb + b) + u)
                        nc.tensor.transpose(pairs[:, b, u, :], src[:, w0 : w0 + P], ident[:])
                nc.scalar.copy(
                    out=dst.rearrange("p (b t u) -> p b t u", b=2, u=2),
                    in_=pairs[:].rearrange("p b u t -> p b t u"),
                )

        z_codes = {}
        z_planes = {}

        def quantize_z(a, c, grouped, cols):
            half = BANK // 2
            if cols.stop - cols.start <= half:
                h = cols.start // half
                part = grouped[:, h, cols.start - half * h : cols.stop - half * h, :]
                runs = [(cols, part.rearrange("p t i -> p (t i)"))]
            elif a == 0 or c < CHUNKS - 1:
                runs = [(cols, grouped.rearrange("p h t i -> p (h t i)"))]
            else:
                runs = [(slice(half * h, half * (h + 1)), grouped[:, h].rearrange("p t i -> p (t i)")) for h in range(2)]
            for run, values in runs:
                nc.vector.quantize_mx(out=z_codes[a, c][:, run].bitcast(FP8X4), scales=z_planes[a, c][:, run], in_=values)

        def z_tiles(a, c, tag):
            z_codes[a, c] = keep.tile([P, BANK], U32, name="z_codes", tag=tag, align_bytes=64)
            z_planes[a, c] = keep.tile([P, BANK], U8, name="z_planes%d_%d" % (a, c), align_bytes=64)

        def second_product(acc, a, c, parts):
            for i, (n, t0, width) in enumerate(parts):
                first = sum(part[2] for part in parts[:i])
                nc.tensor.matmul_mx(
                    out=acc[:, first : first + width],
                    lhsT=w2_codes[:, a, 2 * P * n : 2 * P * (n + 1)].bitcast(FP4X4),
                    lhsT_scale=w2_planes[:, a, P * n : P * (n + 1)],
                    rhs=z_codes[a, c][:, t0 : t0 + width].bitcast(FP8X4),
                    rhs_scale=z_planes[a, c][:, t0 : t0 + width],
                    start=(a == 0 and i == 0),
                    stop=(a == PASSES - 1 and i == len(parts) - 1),
                )

        z_upper = [keep.tile([P, 2, BANK // 2, 4], BF16, name="z_upper%d" % c, align_bytes=64)[:] for c in range(3)]
        woven = keep.tile([P, 4, BANK // 2, 4], BF16, name="z_woven", align_bytes=64)
        z_upper.append(woven[:, 0:4:3])

        def turn_back_pair(c):
            src = z_turned[c][:].rearrange("t b u p e -> t (b u p e)").bitcast(F32)
            dst = z_upper[c].rearrange("p h t i -> p h (t i)").bitcast(F32).rearrange("p h (t u) -> p h t u", u=2)
            pairs = next_bank()
            for b in range(4):
                nc.tensor.transpose(pairs[:, P * b : P * (b + 1)], src[:, 2 * P * b : 2 * P * b + P], ident[:])
            nc.scalar.copy(out=dst[:, :, :, 0], in_=pairs.rearrange("p (h t) -> p h t", h=2))

        def turn_back_lane2(c):
            back = sum_banks[FIRST_LANE_SLICE][c].bitcast(BF16)[:, 0:BANK]
            for b in range(4):
                nc.tensor.transpose(back[:, P * b : P * (b + 1)], lane2_turned[:, c - 1, b, :], ident_bf16[:])
            for i, (t0, t1) in enumerate(PIECES):
                if t0 // BANK == c:
                    nc.scalar.copy(out=lane_rows[i][:, 0, :], in_=back[:, t0 % BANK : t0 % BANK + t1 - t0])

        prepare_w1_first()
        v_words.append(keep.tile([P, S], U32, name="v_words1", tag="v_words1", align_bytes=64))
        for j0, j1 in first_pieces:
            nc.vector.tensor_copy(v_words[1][:, j0:j1], tabs[1][:].bitcast(U32).indirect(offsets[:, j0 // 16 : j1 // 16]))
        pages[2] = big(PAGE_BUFFERS[2], [P, T2], F32)
        nc.gpsimd.memset(pages[2][:].bitcast(I32), 0)
        prepare_w1_lower(1)
        pages[1] = big(PAGE_BUFFERS[1], [P, T2], F32)
        nc.gpsimd.memset(pages[1][:].bitcast(I32), 0)
        for piece in first_pieces:
            first_product(0, piece)
        prepare_w1_lower(2)
        w2_planes = keep.tile([P, PASSES, N], U8, name="w2_planes", tag=cleared_behind[2], align_bytes=64)
        nc.gpsimd.memset(w2_planes[:].rearrange("p a n -> p (a n)").bitcast(I32), 0)
        for q in range(4):
            nc.sync.dma_start(
                out=w2_planes[32 * q : 32 * q + 4, :, :].bitcast(I32),
                in_=w2_scales[:, 4 * q : 4 * q + 4, :].rearrange("a r n -> r a n").bitcast(I32),
            )
        for piece in halves:
            first_product(1, piece)
        add_turned(0, olds[0], True, False)

        z_lower = {}
        last = SLICES - 1
        for s in range(SLICES):
            scatter(s)
            if s + OLD_AHEAD < last:
                load_old(s + OLD_AHEAD)
            if s + OLD_AHEAD == last:
                load_old_last()
            if s == 0:
                prepare_w1_lower(AS_THEY_LIE - 1)
            if s == 1:
                prepare_w1_upper(1)
                quantize_w1(FIRST_LANE_SLICE, lanes_grouped[:])
            if s + 2 < SLICES:
                for piece in halves:
                    if (s + 2, piece) not in h_pieces:
                        first_product(s + 2, piece)
            for early, half in EARLY_HALVES.get(s, ()):
                first_product(early, halves[half])
            if s == 0:
                prepare_w1_upper(0)
            if s < last:
                sum_turned(s)
            if s == AS_THEY_LIE - 1:
                for c in range(CHUNKS):
                    if c % 2 == 0:
                        two_chunks = big(c, [P, 2, 2, BANK // 2, 4], BF16)
                    z_lower[c] = two_chunks[:, c % 2] if c < CHUNKS - 1 else woven[:, 1:3]
                    turn_back(c, z_lower[c], [(hb, next_bank()) for hb in range(2)])
            if s == FIRST_LANE_SLICE - 1:
                for c in (1, 2):
                    turn_back_pair(c)
            if s == FIRST_LANE_SLICE:
                acc_banks = [next_bank() for c in range(CHUNKS)]
                for c in (1, 2):
                    turn_back_lane2(c)
                turn_back(0, z_upper[0], [(1, sum_banks[s][0]), (0, acc_banks[3])])
                turn_back(3, z_upper[3], [(0, sum_banks[s][3]), (1, sum_banks[s][1])])
            if s + 1 < last:
                add_turned(s + 1, olds[s + 1], True, False)

        freed = sum_banks[FIRST_LANE_SLICE]
        acc_banks = [freed[2], freed[0], acc_banks[3]] + acc_banks[0:3] + [freed[3], freed[1]]
        out_rows = out.rearrange("(n p) t -> p n t", p=P)
        groups = []
        for i, (t0, t1) in enumerate(PIECES):
            c, width = t0 // BANK, t1 - t0
            count = 2 if i == 0 else BANK // width
            for n0 in range(0, N_TILES, count):
                parts = [(n, t0 % BANK, width) for n in range(n0, n0 + count)]
                groups.append((c, parts, out_rows[:, n0 : n0 + count, t0:t1]))
        c, [(n, t0, width)], dst = groups.pop()
        for cols in (slice(0, width - LAST_PIECE), slice(width - LAST_PIECE, width)):
            groups.append((c, [(n, cols.start, cols.stop - cols.start)], dst[:, :, cols]))
        z_tiles(0, 0, "big%d" % PAGE_BUFFERS[2 * last % PAGES])
        for cols in (slice(BANK // 2, BANK), slice(0, BANK // 2)):
            quantize_z(0, 0, z_lower[0], cols)

        def grouped_piece(i):
            t0, t1 = PIECES[i]
            count = max(1, (t1 - t0) // (BANK // 2))
            h0, c0 = divmod(t0 % BANK, BANK // 2)
            return z_upper[t0 // BANK][:, h0 : h0 + count, c0 : c0 + (t1 - t0) // count, :]

        def add_piece(i, engine):
            t0, t1 = PIECES[i]
            if i in lane_rows:
                engine.tensor_tensor(lane_rows[i][:, 1, :], old_last[i], page_of(last)[:, t0:t1], ALU.add)
            else:
                lane3 = grouped_piece(i)[:, :, :, 3]
                old_part = old_last[i].rearrange("p (h t) -> p h t", h=lane3.shape[1])
                page_part = page_of(last)[:, t0:t1].rearrange("p (h t) -> p h t", h=lane3.shape[1])
                engine.tensor_tensor(lane3, old_part, page_part, ALU.add)

        def quantize_late(c):
            z_tiles(0, c, "piece%d" % LATE_CODES_IN[c])
            quantize_z(0, c, z_lower[c], slice(0, BANK))

        for c in range(CHUNKS - 1):
            z_tiles(1, c, "codes1_%d" % c)
        add_piece(0, nc.vector)
        for i, (t0, t1) in enumerate(PIECES[:-1]):
            c = t0 // BANK
            if (0, c) not in z_codes:
                quantize_late(c)
            if i in lane_rows:
                lanes = grouped_piece(i)[:, :, :, 2:4]
                nc.vector.tensor_copy(out=lanes, in_=lane_rows[i].rearrange("p e (h t) -> p h t e", h=lanes.shape[1]))
            if i + 2 < len(PIECES):
                add_piece(i + 1, nc.vector)
                quantize_z(1, c, z_upper[c], slice(t0 % BANK, t0 % BANK + t1 - t0))

        sums = {}
        results = []

        def multiply(idx):
            c, parts, dst = groups[idx]
            width = sum(part[2] for part in parts)
            acc = acc_banks[idx % len(acc_banks)]
            for ahead in FIRST_PASSES.get(idx, ()):
                second_product(acc_banks[ahead % len(acc_banks)], 0, *groups[ahead][0:2])
            second_product(acc, 1, c, parts)
            start = sum(part[2] for g in groups[:idx] for part in g[1]) % (N_TILES * BANK)
            if start == 0:
                results.append(stream.tile([P, N_TILES * BANK], F32, name="stream", tag="stream", align_bytes=64))
            magnitude = slot(idx % STAGING_SLOTS, [P, BANK], F32)
            sums[idx] = (acc[:, 0:width], magnitude[:, 0:width], results[-1][:, start : start + width], dst)

        negated = {}

        def negate(idx):
            acc = sums[idx][0]
            tile = keep.tile([P, BANK], F32, name="negated", tag="negated%d" % NEGATED_IN[idx], align_bytes=64)
            negated[idx] = tile[:, 0 : acc.shape[1]]
            nc.vector.tensor_scalar(out=negated[idx], in0=acc, scalar1=-1.0, scalar2=None, op0=ALU.mult)

        def larger(idx):
            nc.vector.tensor_tensor(sums[idx][1], sums[idx][0], negated[idx], ALU.max)

        def absolute(idx):
            nc.scalar.activation(out=sums[idx][1], in_=sums[idx][0], func=ACT.Abs)

        def finish(idx, queue):
            acc, magnitude, logs, dst = sums[idx]
            nc.scalar.activation(out=logs, in_=magnitude, func=ACT.Ln, bias=one[:], scale=0.5)
            queue.dma_start(out=dst, in_=logs.rearrange("p (n t) -> p n t", n=dst.shape[1]))

        for idx in range(9):
            multiply(idx)
            if idx in NEGATED_IN:
                negate(idx)
            else:
                absolute(idx)
                finish(idx, nc.sync)
        quantize_z(1, 2, z_upper[2], slice(0, BANK))
        quantize_late(3)
        add_piece(len(PIECES) - 1, nc.gpsimd)
        larger(6)
        finish(6, nc.sync)
        for idx in FIRST_PASSES[9]:
            multiply(idx)
        for idx in (9, 10):
            negate(idx)
        larger(9)
        for idx in (11, 12):
            absolute(idx)
        for idx in (9, 11):
            finish(idx, nc.sync)
        z_tiles(1, 3, "negated%d" % NEGATED_IN[6])
        quantize_z(1, 3, z_upper[3], slice(0, BANK))
        larger(10)
        finish(10, nc.sync)
        for idx in FIRST_PASSES[13]:
            multiply(idx)
        for idx in (13, 15):
            negate(idx)
        larger(13)
        negate(16)
        for idx in (15, 16):
            larger(idx)
        absolute(14)
        for idx in (12, 14, 13, 15):
            finish(idx, nc.sync)
        absolute(17)
        finish(16, nc.sync)
        finish(17, nc.scalar)
